import numpy as np, ml_dtypes
CORES = [1,5,17,21,33,37,49,53]
N = 8
BF = ml_dtypes.bfloat16
def gentries(a):
    return np.ascontiguousarray(a.reshape(8, 16, -1).transpose(0, 2, 1)).reshape(8, -1)
def gtable(e):
    e = np.asarray(e); return np.ascontiguousarray(e.reshape(8, -1, 16).transpose(0, 2, 1)).reshape(128, -1).astype(np.int32)
def f(rng, *shape):
    return (rng.standard_normal(shape, dtype=np.float32) * np.exp2(rng.integers(-2, 3, shape[:-1] + (1,)))).astype(BF)
def wide(rng, *shape):
    v = f(rng, *shape).astype(np.float32); k = shape[:-2] + (1, shape[-1])
    return (v * np.exp2(rng.integers(-6, 7, k)) * (rng.random(k) > 0.0625)).astype(BF)
V, W, G, P, Q, RO = 3072, 2048, 128, 256, 96, 3
M = V + (N - 1) * G + 1
def nodes(an, of):
    A = np.full((N, 8, M), M - 1, np.int64); A[..., :V] = an
    O = np.zeros((N, 8, M), np.int64); O[..., :M - 1] = of
    return A, O
def dates(A, O):
    s, p = O, A
    for i in range(3):
        s = s + np.take_along_axis(s, p, 2); p = np.take_along_axis(p, p, 2)
    return s & (W - 1)
def parts(rng):
    u = rng.random((N, 8, V))
    an = np.where(u < 0.25, M - 1, np.where(u < 0.4, rng.integers(V, M - 1, (N, 8, V)), rng.integers(0, V, (N, 8, V))))
    return an, rng.integers(0, W, (N, 8, M - 1)), rng.integers(0, 256, (N, 8, 16, W)), rng.integers(0, V, (N, 8, (N - 1) * G))
def statures(rng):
    sc = np.exp2(rng.integers(-2, 3, (1, 8, 16, 1)).astype(np.float64)); sh = rng.choice(np.array([-0.8, -0.5, -0.2, 0.1]), (N, 8, 1, 1))
    x = rng.standard_normal((N, 8, 16, V)) + 0.7 * rng.standard_normal((N, 8, 1, V)) + sh
    s = rng.standard_normal((N, 8, 16, W)) + 0.7 * rng.standard_normal((N, 8, 1, W))
    return np.floor(8 * x) * 0.125 * sc, np.floor(8 * s) * 0.125 * sc
def pack(x, an, of, s, wk, snd):
    b = lambda v: np.ascontiguousarray(v).reshape(N, 128, -1).astype(np.float32).astype(BF)
    return {"x": b(x), "an0": np.stack([gtable(e) for e in an]), "of0": np.stack([gtable(e) for e in of]), "s0": b(s), "wk": b(wk), "snd": np.stack([gtable(e) for e in snd])}
def setup_inputs(rng):
    an, of, wk, snd = parts(rng); x, s = statures(rng)
    return pack(x, an, of, s, wk, snd)
def setup_inputs_room(rng):
    an, of, wk, snd = parts(rng); day = np.arange(W)
    an[..., 0] = M - 1; an[..., V - 1] = M - 1; of[..., 0] = 0; of[..., V - 1] = W - 2
    D = dates(*nodes(an, of))[..., :V]
    s = rng.integers(36, 61, (N, 8, 16, W)) * 0.25
    s[..., day % 4 == 3] = rng.integers(4, 29, (N, 8, 16, W // 4)) * 0.25
    o = s[1::2]; o[..., day % 4 == 1] = rng.integers(-32, -3, (o.shape[0], 8, 16, W // 4)) * 0.25
    k = rng.permutation(16)
    wk[:, :, k[0]] = 4 * rng.integers(0, 64, (N, 8, W)) + (day + 1) % 4
    wk[1::2, :, k[1]] = 4 * rng.integers(0, 64, (o.shape[0], 8, W)) + (day + 3) % 4
    x = 16 + rng.integers(0, 33, (N, 8, 16, V)) * 0.25
    for q in range(N):
        for g in range(8):
            n = int(rng.choice(np.array([0, 1, 2, P - 1, P, P + 1, P + Q]))); nf = int(rng.choice(np.array([0, 1, Q - 1, Q, Q + 1, P])))
            if q == 0: n = (P, P + 1, P - 1, 1, 0, P, P, P)[g]; nf = (Q, Q + 1, Q - 1, 1, 0, 0, P, Q + 1)[g]
            e = np.flatnonzero(D[q, g] % 2 == 0); e = e[(e > 0) & (e < V - 1)]
            w = np.concatenate([np.array([0, V - 1]), rng.permutation(e)])[:n]
            x[q, g][:, w] = rng.integers(29, 36, (16, len(w))) * 0.25
            i = w[len(w) - min(nf, len(w)):]
            x[q, g][:, i] = rng.integers(0, 4, (16, len(i))) * 0.25
    return pack(x, an, of, s, wk, snd)
def setup_inputs_ties(rng):
    an, of, wk, snd = parts(rng)
    of = rng.choice(np.array([0, 1, W - 1, W // 2, 14]), (N, 8, M - 1)); wk[:, ::2] = rng.choice(np.array([0, 1, 2, 255]), (N, 4, 16, W))
    x = np.floor(4 * rng.random((N, 8, 16, V)) * (0.3 + 0.7 * rng.random((N, 8, 1, V))))
    s = np.floor(4 * rng.random((N, 8, 16, W)) * (0.3 + 0.7 * rng.random((N, 8, 1, W)))) + 2 * (rng.random((N, 8, 1, W)) < 0.4)
    x[..., 0] = -1; x[..., V - 1] = -1
    x = np.where((x == 0) & (rng.random(x.shape) < 0.5), -0.0, x); s = np.where((s == 0) & (rng.random(s.shape) < 0.5), -0.0, s)
    return pack(x, an, of, s, wk, snd)
def setup_inputs_chains(rng):
    an, of, wk, snd = parts(rng); x, s = statures(rng); v = np.arange(V); d = int(rng.integers(0, W))
    for q in range(N):
        for g in range(8):
            k = (g + q) % 8
            if k == 0: an[q, g] = (v + 1) % V
            if k == 1: an[q, g] = v
            if k == 2: an[q, g] = rng.integers(V, M - 1, V)
            if k == 3: an[q, g] = M - 1
            if k == 4: an[q, g] = rng.choice(np.array([0, 5, V - 1]), V)
            if k == 5: an[q, g] = np.where(v == 0, M - 1, v - 1)
            if k > 5:
                an[q, g] = M - 1; of[q, g, :V] = d
                w = 1 + rng.permutation(255)[:16]; wk[q, g, :, d] = w; c = (d + 7 * w) & (W - 1)
                i = np.sort(rng.permutation(16)[:2])
                s[q, g] = 16 + 0.25 * rng.integers(0, 32, (16, W))
                s[q, g][:, c[i[0]]] = 0.25 * rng.integers(0, 16, 16)
                m = np.arange(P) if k == 6 else np.arange(int(rng.integers(0, 16)), V, 16)
                y = 28 + 0.25 * rng.integers(0, 16, (16, V))
                y[:, m] = 8 + 0.25 * rng.integers(0, 16, (16, len(m)))
                if k == 6: y[:, rng.permutation(P)[:56]] = -8 + 0.25 * rng.integers(0, 16, (16, 56))
                if k == 7: s[q, g][:, c[i[1]]] = -16 + 0.25 * rng.integers(0, 16, 16)
                x[q, g] = y
    snd[:, ::2] = rng.choice(np.array([0, 3, V // 2, V - 1]), (N, 4, (N - 1) * G))
    return pack(x, an, of, s, wk, snd)
def setup_inputs_calm(rng):
    an, of, wk, snd = parts(rng); x, s = statures(rng); q = int(rng.integers(0, N)); g = int(rng.integers(0, 8))
    x[:, g] += 64
    x[(q + 2) % N] += 64; x[q] = np.minimum(x[q], 20) - 64
    o = s[(q + 1) % N]; o[..., 1::2] -= 128
    w = rng.permutation(256)[:16]; wk[:, g, :, 0] = w; day = (7 * w) & (W - 1)
    for r in range(N):
        if r != q: s[r, g][:, day] = -2.0 ** 20
    x[q, :, :, 0] = -2.0 ** 20
    return pack(x, an, of, s, wk, snd)
def setup_inputs_spread(rng):
    an, of, wk, snd = parts(rng)
    of = np.minimum(np.exp2(13 * rng.random((N, 8, M - 1))).astype(np.int64) - 1, W - 1)
    x = np.abs(wide(rng, N, 8, 16, V).astype(np.float32)); s = np.abs(wide(rng, N, 8, 16, W).astype(np.float32))
    k = rng.permutation(8); sc = np.ones((1, 8, 1, 1), np.float32); sc[:, k[0]] = 2.0 ** -40; sc[:, k[1]] = 512
    x = np.minimum(x * sc, np.float32(2.0 ** 20)); s = np.minimum(s * sc, np.float32(2.0 ** 20))
    x[:, k[1], :, V - 1] = 2.0 ** 20; s[:, k[1], :, W - 1] = 2.0 ** 20
    return pack(x, an, of, s, wk, snd)
def check_inputs(d):
    bad = []
    for k, lo, hi in (("x", -2 ** 20, 2 ** 20), ("s0", -2 ** 20, 2 ** 20), ("wk", 0, 255), ("an0", 0, M - 1), ("of0", 0, W - 1), ("snd", 0, V - 1)):
        v = np.asarray(d[k]).astype(np.float64)
        if not (np.min(v) >= lo and np.max(v) <= hi): bad.append("range of " + k)
        elif k == "wk" and np.any(v != np.floor(v)): bad.append("whole numbers of wk")
        elif k in ("x", "s0") and np.any((v != 0) & (np.abs(v) < 2.0 ** -100)): bad.append("tiny numbers of " + k)
    return bad
def best(S, K, x, D):
    c = (D + 7 * K[:, D]) & (W - 1)
    e = np.sum((x[:, None, :] > S[:, c]).astype(np.int64), axis=0)
    k = np.argmax(e, axis=0); i = np.arange(len(D))
    return c[k, i], e[k, i]
def put(S, c, x):
    u, i = np.unique(c, return_index=True)
    S[:, u] = x[:, i]
def reference(x, an0, of0, s0, wk, snd):
    X = x.astype(np.float32).reshape(N, 8, 16, V); S = s0.astype(np.float32).reshape(N, 8, 16, W).copy(); K = wk.astype(np.float32).astype(np.int64).reshape(N, 8, 16, W)
    A, O = nodes(np.stack([gentries(e) for e in an0]).astype(np.int64), np.stack([gentries(e) for e in of0]).astype(np.int64))
    sl = np.stack([gentries(e) for e in snd]).astype(np.int64).reshape(N, 8, N - 1, G)
    odd = np.zeros(N, np.int64)
    for t in range(RO):
        D = dates(A, O)[..., :V]
        a = np.sum((X >= np.take_along_axis(S, D[:, :, None, :], 3)).astype(np.int64), axis=2)
        moves = np.zeros(N, np.int64); go = {}
        for q in range(N):
            for g in range(8):
                v = np.flatnonzero(a[q, g] < 5)[:P]
                c, e = best(S[q, g], K[q, g], X[q, g][:, v], D[q, g, v])
                ok = e >= 9 + odd[q]; w = v[ok]
                A[q, g, w] = M - 1; O[q, g, w] = c[ok]
                put(S[q, g], c[ok], X[q, g][:, w])
                moves[q] += len(w)
                r = v[~ok][:Q]; go[q, g] = (X[q, g][:, r], D[q, g, r])
        for q in range(N):
            for g in range(8):
                y, b = go[(q - 1 - t % (N - 1)) % N, g]
                c, e = best(S[q, g], K[q, g], y, b)
                ok = e >= 9 + odd[q]
                put(S[q, g], c[ok], y[:, ok])
        odd = moves & 1
        for q in range(N):
            for d in range(1, N):
                p = (q - d) % N
                O[q, :, V + (d - 1) * G:V + d * G] = np.take_along_axis(D[p], sl[p, :, d - 1], 1)
    return {"ys": S.reshape(N, 128, W).astype(BF), "yan": A[..., :V].astype(np.float32), "yof": O[..., :V].astype(np.float32)}

@@ -1,0 +1,676 @@
+from concourse.mybir import AluOpType as A, AxisListType, ActivationFunctionType as F
+
+V, W, NG, Q, RO = 3072, 2048, 896, 96, 3
+ROOT, BWW = 3968, 3984
+NEG = -4194304.0
+SC = 32768.0
+TINY = 2.0 ** -120
+bf, f3, i3, u1, fh = "bfloat16", "float32", "int32", "uint16", "float16"
+SCRATCH = {}
+
+
+def _sb(dt_, **kw):
+    for n, w in kw.items():
+        SCRATCH[n] = ("sbuf", [128] + (w if isinstance(w, list) else [w]), dt_)
+
+
+_sb(i3, anL=192, ofL=248, snL=56, tA=192, tB=248, tE=248, DI=192, DL=192, dg1=192, dg2=192, posI=192, loI=192, hiI=192,
+    ci=256, cm=256, key=496, smi=96, cpi=4, crow=128, crq=128, crg=128, c8=8, kri=256, kr2=256, j16=16)
+_sb(bf, pl0=248, pl1=248, pl2=248, pl3=248, XR=3968, XW=3088, SWIN=2304, WK=2048, BW=4240, SW1=BWW, SW2=BWW, G2=3088, GW=V,
+    Zb=V, Zs=V,
+    dh=192, dlo=192, bits=V, SG=512, bT=192, binc=192, lob=192, hib=192, sq=192, OHL=V, OHH=V, indA=256, indB=256, ov=240,
+    xB=256, G2g=256, Dg=256, XX=4096, XXg=1536, B2=[16, 256], wkg=256, smb=80, RD=256, DE=[16, 256], DMb=[16, 16], dupR=256,
+    XP=2048, XS=2048, XE=2048, XLh=2048, XLl=2048, SA=2048, BD=128, BDt=128, M1=128, M1g=128, ID=128, NI=128, I7=128, CB=128, ONE=256,
+    ZER=256, OC=40, krow=256, KC=256, MK=[16, 16], GL0=NG, GL1=NG, GO0=NG, GO1=NG, GS0=544, GS1=544, GS2=544, GX0=192, GX1=192, GX2=192)
+_sb(f3, vf=16, sml=256, thr=3, ccol=64, BG=8, BA=8, tr=64)
+_sb(u1, SL=56, PL=192, PL1=192, PL2=192, DU=192, cu=256, smu=80)
+_sb(fh, ctc=[16, 32], ctt=[16, 32], cmh=16, cR=256, XA=2048, Ie=128, Io=128)
+SCRATCH["OUT"] = ("sbuf", [40, V], f3)
+for _b in range(8):
+    SCRATCH["ps%d" % _b] = ("psum", [128, 512], f3)
+SEMAPHORES = ["sv", "ss", "sp", "sg", "loc", "gh0", "gh1", "gu0", "gu1", "gu2"] + ["d%d" % k for k in range(60)]
+
+
+def rank_program(g, core, T, topo):
+    r = T.rank_of(core)
+    if r is None:
+        return
+    cores = T.cores
+    N = len(cores)
+    ENG = {"v": g.vector, "s": g.scalar, "p": g.tensor, "g": g, "y": g.sync}
+    SEM = {"v": "sv", "s": "ss", "p": "sp", "g": "sg"}
+    cnt = {"v": 0, "s": 0, "p": 0, "g": 0}
+    seen = {e: {} for e in ENG}
+    know = {}
+    tags = {}
+    total = {}
+
+    def tag(t):
+        if t not in tags:
+            tags[t] = {"w": [], "a": [], "r": []}
+        return tags[t]
+
+    def waits(e, deps):
+        m = {}
+        for sem, val in deps:
+            if seen[e].get(sem, 0) < val:
+                m[sem] = max(m.get(sem, 0), val)
+        for sem, val in list(m.items()):
+            for s2, v2 in m.items():
+                if s2 != sem and know.get((s2, v2), {}).get(sem, 0) >= val:
+                    m[sem] = 0
+        for sem, val in m.items():
+            if val:
+                ENG[e].wait_ge(T.sem[sem], val)
+            for s2, v2 in know.get((sem, val), {}).items():
+                seen[e][s2] = max(seen[e].get(s2, 0), v2)
+            seen[e][sem] = max(seen[e].get(sem, 0), val)
+
+    def deps_of(e, rd, wr, ap):
+        def some(x):
+            return [(s, n) for s, n, q in x if not (q == "p" and e == "p")]
+        d = []
+        for t in rd:
+            x = tag(t)
+            d += some(x["w"] + x["a"])
+            if t[:2] == "ps":
+                d += [(s, n) for s, n, q in x["r"] if q != e]
+        for t in wr:
+            x = tag(t)
+            d += some(x["w"] + x["a"] + x["r"])
+        for t in ap:
+            x = tag(t)
+            if x["r"]:
+                x["w"] = x["r"]; x["a"] = []; x["r"] = []
+            d += some(x["w"])
+        return d
+
+    def note(me, rd, wr, ap):
+        for t in rd:
+            tag(t)["r"].append(me)
+        for t in wr:
+            x = tag(t); x["w"] = [me]; x["a"] = []; x["r"] = []
+        for t in ap:
+            tag(t)["a"].append(me)
+
+    def op(e, fn, rd=(), wr=(), ap=()):
+        waits(e, deps_of(e, rd, wr, ap))
+        cnt[e] += 1
+        fn(ENG[e]).then_inc(T.sem[SEM[e]], 1)
+        know[(SEM[e], cnt[e])] = dict(seen[e])
+        total[SEM[e]] = cnt[e]
+        note((SEM[e], cnt[e], e), rd, wr, ap)
+
+    nd = [0]
+
+    def dma(out, in_, rd=(), wr=(), ap=()):
+        waits("y", deps_of("dma", rd, wr, ap))
+        s = "d%d" % nd[0]; nd[0] += 1
+        g.sync.dma_start(out, in_).then_inc(T.sem[s], 16)
+        know[(s, 16)] = dict(seen["y"])
+        total[s] = 16
+        note((s, 16, "dma"), rd, wr, ap)
+
+    def engs(src, dst):
+        return topo.engines(src, dst)[:8]
+
+    def arrive(sem, n, t):
+        total[sem] = n
+        tag(t)["w"].append((sem, n, "rem"))
+
+    def send(out, in_, dst, sem, rd):
+        waits("g", deps_of("rem", rd, (), ()))
+        rid, pid, _ = topo.addr(dst)
+        e = engs(core, dst)
+        m = 0
+        for k in e:
+            m |= 1 << k
+        g.remote_dma(out, in_, T.sem[sem], T.sem.loc, pid, rid, m)
+        total["loc"] = total.get("loc", 0) + len(e)
+
+    def ts(out, in0, s1, op0, rd, wr=(), ap=(), s2=None, op1=None):
+        if op1 is None:
+            op("v", lambda q: q.tensor_scalar(out, in0, s1, None, op0), rd, wr, ap)
+        else:
+            op("v", lambda q: q.tensor_scalar(out, in0, s1, s2, op0, op1), rd, wr, ap)
+
+    def tt(out, a, b, o, rd, wr=(), ap=()):
+        op("v", lambda q: q.tensor_tensor(out, a, b, o), rd, wr, ap)
+
+    def cp(out, in_, rd, wr=(), ap=()):
+        op("v", lambda q: q.tensor_copy(out, in_), rd, wr, ap)
+
+    def ms(out, c, wr=(), ap=()):
+        op("v", lambda q: q.memset(out, c), (), wr, ap)
+
+    def act(out, in_, rd, wr=(), ap=(), f=F.Copy, **kw):
+        op("s", lambda q: q.activation(out, in_, f, **kw), rd, wr, ap)
+
+    def mm(out, l, rh, st, sp, rd, wr=(), ap=()):
+        op("p", lambda q: q.matmul(out, l, rh, st, sp), rd, wr, ap)
+
+    def iota(out, pat, base, cm, wr):
+        op("g", lambda q: q.iota(out, pat, base, cm), (), wr)
+
+    def sl(i):
+        return slice(i * 128, (i + 1) * 128)
+
+    f_ = lambda k, nj: T.sml[:, 16 * k:16 * k + nj]
+    n_ = lambda k, nj: T.smi[:, 16 * k:16 * k + nj]
+    b_ = lambda k, nj: T.smb[:, 16 * k:16 * k + nj]
+    u_ = lambda k, nj: T.smu[:, 16 * k:16 * k + nj]
+    tr = lambda k, nj: T.tr[:, 16 * k:16 * k + nj]
+
+    dma(T.anL[:], T.an0[:], (), ["anL"])
+    dma(T.ofL[:], T.of0[:], (), ["ofL"])
+    dma(T.snL[:], T.snd[:], (), ["snL"])
+    dma(T.SWIN[:, 0:W], T.s0[:], (), ["S"])
+    dma(T.XW[:, 0:V], T.x[:], (), ["XWx"])
+    dma(T.WK[:], T.wk[:], (), ["WK"])
+    iota(T.cpi[:, 0:1], [[1, 1]], 0, 1, ["cpi"])
+    iota(T.c8[:], [[1, 8]], 0, 0, ["c8"])
+    iota(T.crow[:], [[1, 128]], 0, 0, ["crow"])
+    iota(T.j16[:], [[16, 16]], 0, 0, ["j16"])
+    iota(T.kri[:], [[1, 256]], 0, 0, ["kri"])
+    for n, w in (("Zb", V), ("Zs", V), ("SA", 2048), ("XE", 2048), ("XLh", 2048), ("XLl", 2048)):
+        op("g", lambda q, n=n, w=w: q.iota(T[n][:], [[0, w]], 0, 0, allow_small_or_imprecise_dtypes=True), (), [n])
+    ms(T.XR[:], 0.0, ["XR"])
+
+    def col(k):
+        return T.ccol[:, k:k + 1]
+
+    ts(T.cpi[:, 1:2], T.cpi[:, 0:1], 15, A.bitwise_and, ["cpi"], ["cpi1"])
+    ts(T.cpi[:, 2:3], T.cpi[:, 0:1], 4, A.arith_shift_right, ["cpi"], ["cpi2"])
+    ts(T.cpi[:, 3:4], T.cpi[:, 0:1], 7, A.bitwise_and, ["cpi"], ["cpi3"])
+    cp(col(0), T.cpi[:, 0:1], ["cpi"], ["c0"])
+    cp(col(1), T.cpi[:, 1:2], ["cpi1"], ["c1"])
+    cp(col(2), T.cpi[:, 2:3], ["cpi2"], ["c2"])
+    cp(col(8), T.cpi[:, 3:4], ["cpi3"], ["c8c"])
+    ts(col(9), col(1), 0.0, A.is_equal, ["c1"], ["c9"], s2=256.0, op1=A.mult)
+    ts(col(10), col(1), 1.0, A.is_equal, ["c1"], ["c10"])
+    ts(T.BG[:], T.c8[:], col(2), A.is_equal, ["c8", "c2"], ["BG"])
+    tt(col(3), col(9), col(10), A.add, ["c9", "c10"], ["c3"])
+    ts(col(11), col(1), 2.0, A.is_equal, ["c1"], ["c11"], s2=32.0, op1=A.mult)
+    ts(col(12), col(1), 10.0, A.is_equal, ["c1"], ["c12"])
+    ts(col(15), col(1), 2.0, A.is_equal, ["c1"], ["c15"], s2=-252.0, op1=A.mult)
+    ts(col(13), col(9), 15.0 / 256.0, A.mult, ["c9"], ["c13"])
+    ts(col(14), col(10), 128.0, A.mult, ["c10"], ["c14"])
+    tt(col(4), col(11), col(12), A.add, ["c11", "c12"], ["c4"])
+    tt(col(5), col(13), col(14), A.add, ["c13", "c14"], ["c5"])
+    ms(T.pl0[:, 192:248], 15.0, ["pl0g"]); ms(T.pl1[:, 192:248], 128.0, ["pl1g"])
+    ts(T.tA[:], T.anL[:], 8, A.arith_shift_right, ["anL"], ["tA"])
+    ts(T.tB[:, 0:192], T.anL[:], 255, A.bitwise_and, ["anL"], ["tB"])
+    cp(T.pl0[:, 0:192], T.tA[:], ["tA"], ["pl0"])
+    cp(T.pl1[:, 0:192], T.tB[:, 0:192], ["tB"], ["pl1"])
+    dma(T.XR[0::16, :], T.pl0[:], ["pl0", "pl0g"], (), ["XR"])
+    dma(T.XR[1::16, :], T.pl1[:], ["pl1", "pl1g"], (), ["XR"])
+    ts(T.tB[:], T.ofL[:], 5, A.arith_shift_right, ["ofL"], ["tB"])
+    ts(T.tE[:], T.ofL[:], 31, A.bitwise_and, ["ofL"], ["tE"])
+    cp(T.pl2[:], T.tB[:], ["tB"], ["pl2"])
+    cp(T.pl3[:], T.tE[:], ["tE"], ["pl3"])
+    dma(T.XR[2::16, :], T.pl2[:], ["pl2"], (), ["XR"])
+    dma(T.XR[10::16, :], T.pl3[:], ["pl3"], (), ["XR"])
+    cp(T.PL[:], T.anL[:], ["anL"], ["PL"])
+    ms(T.ZER[:], 0.0, ["ZER"])
+    ms(T.XP[:], 0.0, ["XP"]); ms(T.XS[:], 0.0, ["XS"])
+    for b in ("BW", "SW1", "SW2"):
+        ts(T[b][:, ROOT:BWW], T.ZER[:, 0:16], col(5), A.add, ["ZER", "c5"], [b + "r"])
+
+    def fill(n, src, rd, scale, o=None):
+        for i in range(16):
+            act(T[n][:, i * 128 + (i if o is None else o):(i + 1) * 128:16], T[src][:], [src] + rd, (), [n], scale=col(16 + i) if scale is None else scale)
+
+    fill("XP", "BG", ["c3"], col(3))
+    fill("XS", "BG", ["c4"], col(4))
+
+    def consts2():
+        ts(T.crq[:], T.crow[:], 15, A.bitwise_and, ["crow"], ["crq"])
+        ts(T.crg[:], T.crow[:], 4, A.arith_shift_right, ["crow"], ["crg"])
+        ts(T.ID[:], T.crow[:], col(0), A.is_equal, ["crow", "c0"], ["ID"])
+        ts(T.BD[:], T.crg[:], col(2), A.is_equal, ["crg", "c2"], ["BD"])
+        ms(T.ONE[:], 1.0, ["ONE"])
+        ts(T.BDt[:], T.crow[:], col(0), A.is_gt, ["crow", "c0"], ["BDt"], s2=-1.0, op1=A.add)
+        ts(T.M1[:], T.ID[:], -4096.0, A.mult, ["ID"], ["M1"])
+        ts(T.NI[:], T.ID[:], -1.0, A.mult, ["ID"], ["NI"])
+        tt(T.M1[:], T.M1[:], T.BDt[:], A.add, ["M1", "BDt"], ["M1"])
+        ms(T.thr[:, 0:1], 9 * SC, ["thr0"])
+        ts(T.XW[:, V:V + 16], T.ZER[:, 0:16], NEG, A.add, ["ZER"], ["XWp"])
+        cp(T.G2[:, V:V + 16], T.ZER[:, 0:16], ["ZER"], ["G2p"])
+        cp(T.krow[:], T.kri[:], ["kri"], ["krow"])
+        ts(T.BA[:], T.c8[:], col(8), A.is_equal, ["c8", "c8c"], ["BA"], s2=128.0, op1=A.mult)
+
+    def consts3():
+        for t in range(RO):
+            ms(T["GS%d" % t][:, 0:96], NEG, ["GSa%d" % t]); ms(T["GS%d" % t][:, 96:192], 0.0, ["GSb%d" % t])
+        ts(T.GW[:], T.XR[:, 0:V], 0.0, A.mult, ["XR", "c5"], ["GW"], s2=col(5), op1=A.add)
+        a, b = T.dg1[:, 0:56], T.dg2[:, 0:56]
+        ts(a, T.snL[:], 15, A.bitwise_and, ["snL"], ["dg1"])
+        ts(b, T.snL[:], 4, A.arith_shift_right, ["snL"], ["dg2"])
+        ts(a, a, 192.0, A.mult, ["dg1"], ["dg1"])
+        tt(a, a, b, A.add, ["dg1", "dg2"], ["dg1"])
+        cp(T.SL[:], a, ["dg1"], ["SL"])
+
+    def consts4():
+        ts(T.I7[:], T.ID[:], 7.0, A.mult, ["ID"], ["I7"])
+        ts(T.CB[:], T.BD[:], col(4), A.mult, ["BD", "c4"], ["CB"])
+        ts(T.cpi[:, 3:4], T.cpi[:, 2:3], 1, A.bitwise_and, ["cpi2", "c8c"], ["cpi3"])
+        ts(tr(0, 16), T.j16[:], col(1), A.add, ["j16", "c1"], ["kL"])
+        ts(T.kr2[:], T.kri[:], 15, A.bitwise_and, ["kri"], ["kr2"])
+        cp(col(7), T.cpi[:, 3:4], ["cpi3"], ["c7"])
+        ts(T.BDt[:], T.crq[:], col(1), A.is_gt, ["crq", "c1"], ["BDt"], s2=-1.0, op1=A.add)
+        ts(col(6), col(7), -1.0, A.mult, ["c7"], ["c6"], s2=1.0, op1=A.add)
+        ts(T.Io[:], T.ID[:], col(7), A.mult, ["ID", "c7"], ["Io"])
+        ts(T.Ie[:], T.ID[:], col(6), A.mult, ["ID", "c6"], ["Ie"])
+        ts(tr(1, 16), tr(0, 16), float(BWW), A.add, ["kL"], ["trP"])
+        ts(tr(2, 16), tr(0, 16), float(W), A.add, ["kL"], ["trS"])
+        ts(tr(3, 16), tr(0, 16), 192.0, A.add, ["kL"], ["trR"])
+        ts(T.KC[:], T.kr2[:], -2048.0, A.mult, ["kr2"], ["KC"], s2=15 * 2048.0, op1=A.add)
+        ts(T.M1g[:], T.ID[:], -4096.0, A.mult, ["ID"], ["M1g"])
+        tt(T.BDt[:], T.BDt[:], T.BD[:], A.mult, ["BDt", "BD"], ["BDt"])
+        ts(T.ccol[:, 16:32], T.crow[:, 0:16], col(1), A.is_equal, ["crow", "c1"], ["c16"])
+        ts(T.MK[:], T.kr2[:], col(1), A.is_gt, ["kr2", "c1"], ["MK"])
+        tt(T.M1g[:], T.M1g[:], T.BDt[:], A.add, ["M1g", "BDt"], ["M1g"])
+
+    def consts5():
+        for i in range(16):
+            ts(T.XA[:, sl(i)], T.BD[:], col(16 + i), A.mult, ["BD", "c16"], (), ["XA"])
+        fill("XLh", "BG", ["c16"], None, 2)
+        fill("XLl", "BG", ["c16"], None, 10)
+        ms(T.OC[:], 0.0, ["OC"])
+        ts(T.OC[:, 0:8], T.BG[:], col(3), A.mult, ["BG", "c3", "OC"], (), ["OC"])
+        ts(T.OC[:, 32:40], T.BG[:], col(4), A.mult, ["BG", "c4", "OC"], (), ["OC"])
+
+    consts2()
+    for i in range(16):
+        o, x = T.BW[:, i:ROOT:16], T.XR[:, i * 248:(i + 1) * 248]
+        if i % 4 < 3:
+            cp(o, x, ["XR"], (), ["BW"])
+        else:
+            act(o, x, ["XR"], (), ["BW"])
+
+    def th(a):
+        return slice(1024 * a, 1024 * (a + 1)), slice(64 * a, 64 * a + 64)
+
+    def keep():
+        for a in range(3):
+            f = th(a)[0]
+            dma(T.Zb[2::8, f], T.BW[2::8, f], ["BW", "Zb"], (), ["Zb%d" % a])
+
+    keep()
+    for b in ("SW1", "SW2"):
+        dma(T[b][:, V:ROOT], T.BW[:, V:ROOT], ["BW"], [b + "g"])
+    consts4()
+
+    def ext(X, src, bank, c0, c1, st, sp, rd):
+        for i in range(16):
+            mm(T[bank][:, c0:c1], T[X][:, sl(i)], T[src][:, 16 * c0 + i:16 * c1:16], st and i == 0, sp and i == 15, [X] + rd, (), [bank])
+
+    BWT = ["BW", "BWg", "BWr"]
+    S1T = ["SW10", "SW11", "SW12", "SW1g", "SW1r"]
+    S2T = ["SW20", "SW21", "SW22", "SW2g", "SW2r"]
+    DB = ["ps1", "ps3", "ps4"]
+    LV = {1: ("BW", BWT, "PL", "Zb", "SW1"), 2: ("SW1", S1T, "PL1", "Zs", "SW2")}
+
+    def dbl(l, a):
+        w, wt, p, z, n = LV[l]
+        f, c = th(a)
+        tt(T[n][:, f], T[w][:, 0:BWW].indirect(T[p][:, c]), T[z][:, f], A.add, wt + [p, z, z + str(a)], [n + str(a)])
+        ext("XP", n, "ps0", 64 * a, 64 * a + 64, True, True, [n + str(a)])
+        if l == 1:
+            dma(T.Zs[2::8, f], T.SW1[2::8, f], ["SW1%d" % a, "Zs"], (), ["Zs%d" % a])
+
+    def anchors(n):
+        cp(T[n][:], T.ps0[:, 0:192], ["ps0"], [n])
+
+    def L3a():
+        for a in range(3):
+            ext("XS", "SW2", DB[a], 64 * a, 64 * a + 64, True, False, S2T[:3])
+        for a in range(2):
+            f, c = th(a)
+            act(T.G2[:, f], T.SW2[:, 0:BWW].indirect(T.PL2[:, c]), S2T + ["PL2"], ["G2%d" % a])
+
+    def L3v():
+        f, c = th(2)
+        cp(T.G2[:, f], T.SW2[:, 0:BWW].indirect(T.PL2[:, c]), S2T + ["PL2"], ["G22"])
+
+    def L3e():
+        for a in range(3):
+            ext("XS", "G2", DB[a], 64 * a, 64 * a + 64, False, True, ["G2%d" % a])
+
+    def L3b():
+        for a in range(3):
+            cp(T.DI[:, th(a)[1]], T[DB[a]][:, th(a)[1]], [DB[a]], (), ["DI"])
+
+    def L3c():
+        ts(T.DL[:], T.DI[:], 2047, A.bitwise_and, ["DI"], ["DL"])
+        cp(T.DU[:], T.DL[:], ["DL"], ["DU"])
+
+    def beaten():
+        def counts(c0, c1, bt):
+            for c in range(c0, c1):
+                mm(T.ps2[:, 8 * c:8 * c + 8], T.bits[:, sl(c)], T.BD[:, 0::16], True, True, [bt, "BD"], (), ["ps2"])
+
+        def vec(l, h, t):
+            tt(T.bits[:, l:h], T.SWIN[:, 0:W].indirect(T.DU[:, l // 16:h // 16]), T.XW[:, l:h], A.is_le, ["S", "DU", "XWx"], [t])
+            counts(l // 128, h // 128, t)
+
+        act(T.SG[:], T.SWIN[:, 0:W].indirect(T.DU[:, 160:192]), ["S", "DU"], ["SG"])
+        vec(0, 1024, "bits0")
+        mm(T.ps7[:, :], T.ID[:], T.XW[:, 2560:3072], True, False, ["ID", "XWx"], ["ps7"])
+        mm(T.ps7[:, :], T.NI[:], T.SG[:], False, True, ["NI", "SG"], (), ["ps7"])
+        act(T.bits[:, 2560:3072], T.ps7[:, :], ["ps7"], ["bits3"], f=F.Sign, bias=TINY)
+        vec(1024, 2048, "bits1")
+        counts(20, 24, "bits3")
+        vec(2048, 2560, "bits2")
+        ts(T.bT[:, 0:160], T.ps2[:, 0:160], 4.5, A.is_lt, ["ps2"], ["bT"])
+        ts(T.bT[:, 160:192], T.ps2[:, 160:192], -7.0, A.is_lt, ["ps2"], (), ["bT"])
+
+    def ghosts_a():
+        ts(T.dg2[:], T.DL[:], 31, A.bitwise_and, ["DL"], ["dg2"])
+        ts(T.dg1[:], T.DL[:], 5, A.arith_shift_right, ["DL"], ["dg1"])
+        cp(T.dlo[:], T.dg2[:], ["dg2"], ["dlo"])
+        cp(T.dh[:], T.dg1[:], ["dg1"], ["dh"])
+        dma(T.GW[10::16, :], T.dlo[:], ["dlo"], (), ["GW"])
+        dma(T.GW[2::16, :], T.dh[:], ["dh"], (), ["GW"])
+
+    def ghosts_b(t):
+        act(T["GO%d" % t][:], T.GW[:].indirect(T.SL[:]), ["GW", "SL"], ["GO%d" % t])
+        for d in range(1, N):
+            send(T["GL%d" % t][:, sl(d - 1)], T["GO%d" % t][:, sl(d - 1)], cores[(r + d) % N], "gh%d" % t, ["GO%d" % t])
+        arrive("gh%d" % t, sum(len(engs(cores[(r - d) % N], core)) for d in range(1, N)), "GL%d" % t)
+
+    def ghosts_in(t):
+        for b in ("BW", "SW1", "SW2"):
+            dma(T[b][:, V:ROOT], T["GL%d" % t][:], ["GL%d" % t], [b + "g"])
+
+    NS = 7
+    vU = u_(4, 16)
+    DUm = lambda nj: u_(3, nj)
+
+    def compact(t):
+        mm(T.ps3[:, 0:192], T.M1[:], T.bT[:], True, False, ["M1", "bT"], ["ps3"])
+        for c in range(8):
+            op("v", lambda q, c=c: q.tensor_tensor_scan(T.binc[:, c::8], T.ONE[:, c:192:8], T.bT[:, c::8], 0.0, A.mult, A.add),
+               ["ONE", "bT"], (), ["binc"])
+        mm(T.ps3[:, 0:192], T.ONE[:, 0:128], T.binc[:], False, True, ["ONE", "binc"], (), ["ps3"])
+        mm(T.ps4[:, 0:1], T.binc[:, 0:128], T.ONE[:, 0:1], True, True, ["binc", "ONE"], ["ps4"])
+        mm(T.ps4[0:64, 1:2], T.binc[:, 128:192], T.ONE[:, 0:1], True, True, ["binc", "ONE"], (), ["ps4"])
+        ts(T.posI[:], T.ps3[:, 0:192], 4095.0, A.add, ["ps3"], ["posI"])
+        ts(T.indA[:], T.krow[:], T.ps4[:, 0:1], A.is_ge, ["krow", "ps4"], ["indA"])
+        ts(T.loI[:], T.posI[:], 15, A.bitwise_and, ["posI"], ["loI"])
+        ts(T.hiI[:], T.posI[:], 4, A.arith_shift_right, ["posI"], ["hiI"])
+        ts(T.indB[0:64, :], T.krow[0:64, :], T.ps4[0:64, 1:2], A.is_ge, ["krow", "ps4"], ["indB"])
+        cp(T.lob[:], T.loI[:], ["loI"], ["lob"])
+        cp(T.hib[:], T.hiI[:], ["hiI"], ["hib"])
+        for i in range(16):
+            mm(T.ps6[:, 0:16], T.SA[:, sl(i)], T.indA[:, i::16], i == 0, False, ["SA", "indA"], (), ["ps6"])
+        for i in range(16):
+            mm(T.ps6[:, 0:16], T.SA[0:64, sl(i)], T.indB[0:64, i::16], False, i == 15, ["SA", "indB"], (), ["ps6"])
+        for i in range(NS):
+            act(T.sq[:], T.lob[:], ["lob"], ["sq"], f=F.Square, bias=-float(i))
+            act(T.OHL[:, i::16], T.sq[:], ["sq"], (), ["OHL"], f=F.Relu, scale=-1.0, bias=1.0)
+        for i in range(NS, 16):
+            ts(T.OHL[:, i::16], T.lob[:], float(i), A.is_equal, ["lob"], (), ["OHL"])
+        for i in range(16):
+            ts(T.OHH[:, i::16], T.hib[:], float(i), A.is_equal, ["hib", "c0"], (), ["OHH"], s2=col(0), op1=A.mult)
+        for c in range(24):
+            mm(T.ps5[:, 0:128], T.OHL[:, sl(c)], T.OHH[:, sl(c)], c == 0, c == 23, ["OHL", "OHH"], (), ["ps5"])
+        if t < RO - 1:
+            ghosts_a()
+        if t == 0:
+            consts5()
+        o = lambda a, b: T.ov[:, a:b]
+        tt(o(0, 128), T.ps5[:, 0:128], T.BD[:], A.mult, ["ps5", "BD"], ["ovm"])
+        tt(o(128, 192), o(0, 64), o(64, 128), A.add, ["ovm"], ["ov1"])
+        tt(o(192, 224), o(128, 160), o(160, 192), A.add, ["ov1"], ["ov2"])
+        tt(o(224, 240), o(192, 208), o(208, 224), A.add, ["ov2"], ["ov3"])
+        tt(T.vf[:], T.ps6[:, 0:16], o(224, 240), A.add, ["ps6", "ov3"], ["vf"])
+        cp(vU, T.vf[:], ["vf"], ["vU"])
+
+    def own_data():
+        act(T.G2g[:], T.G2[:].indirect(vU), ["G20", "G21", "G22", "G2p", "vU", "c15"], ["G2g"], f=F.Identity, bias=col(15))
+        cp(T.xB[:], T.XW[:].indirect(vU), ["XWx", "XWp", "vU"], ["xB"])
+        tt(T.Dg[:], T.SW2[:, 0:BWW].indirect(vU), T.G2g[:], A.add, S2T + ["G2g", "vU"], ["Dg"])
+
+    def spread(x, xt, XX, n, ks, e):
+        for k in ks:
+            if e == "v":
+                cp(T[XX][:, k:16 * n:16], x, [xt], (), [XX])
+            else:
+                act(T[XX][:, k:16 * n:16], x, [xt], (), [XX])
+
+    LB = {16: "ps6", 6: "ps4"}
+
+    def choose_a(Dg, dt_, nj):
+        for i in range(16):
+            mm(T[LB[nj]][:, 0:nj], T.XS[:, sl(i)], Dg[:, i::16], i == 0, i == 15, ["XS", dt_], (), [LB[nj]])
+        mm(T.ps7[:, 0:16 * nj], T.CB[:], Dg, True, False, ["CB", dt_], ["ps7"])
+
+    def choose_b(nj):
+        n = 16 * nj
+        ts(n_(4, nj), T[LB[nj]][:, 0:nj], 8064.0, A.add, [LB[nj]], ["di"])
+        ts(n_(5, nj), n_(4, nj), 2047, A.bitwise_and, ["di"], ["dm"])
+        cp(DUm(nj), n_(5, nj), ["dm"], ["DUm"])
+        cp(T.wkg[:, 0:n], T.WK[:].indirect(DUm(nj)), ["WK", "DUm"], ["wkg"])
+        mm(T.ps7[:, 0:n], T.I7[:], T.wkg[:, 0:n], False, True, ["I7", "wkg"], (), ["ps7"])
+
+    def choose_c(nj):
+        n = 16 * nj
+        ts(T.ci[:, 0:n], T.ps7[:, 0:n], 8064.0, A.add, ["ps7"], ["ci"])
+        ts(T.cm[:, 0:n], T.ci[:, 0:n], 2047, A.bitwise_and, ["ci"], ["cm"])
+        cp(T.cu[:, 0:n], T.cm[:, 0:n], ["cm"], ["cu"])
+
+    def choose_d(XX, nj, parts):
+        n = 16 * nj
+        mm(T.ps2[:, 0:n], T.ID[:], T.KC[:, 0:n], True, False, ["ID", "KC"], ["ps2"])
+        for j0, j1 in parts:
+            for j in range(j0, j1):
+                tt(T.B2[:, j, :], T.SWIN[:, 0:W].indirect(T.cu[:, 16 * j:16 * j + 16]), T[XX][:, 256 * j:256 * j + 256], A.is_lt,
+                   ["S", "cu", XX], ["B2%d" % j])
+            for i in range(16):
+                mm(T.ps2[:, 16 * j0:16 * j1], T.XE[:, sl(i)], T.B2[:, j0:j1, 16 * i:16 * i + 16], False, False,
+                   ["XE"] + ["B2%d" % j for j in range(j0, j1)], (), ["ps2"])
+        cp(T.ctc[:, 0:nj, 0:16], T.cm[:, 0:n], ["cm"], (), ["ctc"])
+        cp(T.ctc[:, 0:nj, 16:32], T.cm[:, 0:n], ["cm"], (), ["ctc"])
+        op("v", lambda q: q.transpose(T.ctt[:, 0:nj, :], T.ctc[:, 0:nj, :]), ["ctc"], ["ctt"])
+        mm(T.ps2[:, 0:n], T.Ie[:], T.ctt[:, 0:nj, 0:16], False, False, ["Ie", "ctt"], (), ["ps2"])
+        mm(T.ps2[:, 0:n], T.Io[:], T.ctt[:, 0:nj, 16:32], False, True, ["Io", "ctt"], (), ["ps2"])
+
+    def choose_e(nj):
+        n = 16 * nj
+        K = T.key
+        cp(K[:, 0:n], T.ps2[:, 0:n], ["ps2"], ["key0"])
+        tt(K[:, 256:256 + n // 2], K[:, 0:n:2], K[:, 1:n:2], A.max, ["key0"], ["key1"])
+        tt(K[:, 384:384 + n // 4], K[:, 256:256 + n // 2:2], K[:, 257:256 + n // 2:2], A.max, ["key1"], ["key2"])
+        tt(K[:, 448:448 + n // 8], K[:, 384:384 + n // 4:2], K[:, 385:384 + n // 4:2], A.max, ["key2"], ["key3"])
+        tt(K[:, 480:480 + nj], K[:, 448:448 + n // 8:2], K[:, 449:448 + n // 8:2], A.max, ["key3"], ["kmax"])
+
+    def moved(t, nj):
+        km = T.key[:, 480:480 + nj]
+        ts(f_(0, nj), km, T.thr[:, t:t + 1], A.is_ge, ["kmax", "thr%d" % t], ["mv"])
+        ts(n_(0, nj), km, 2047, A.bitwise_and, ["kmax"], ["c1i"])
+
+    def early():
+        tt(f_(14, 16), T.vf[:], tr(1, 16), A.subtract, ["vf", "trP"], ["vt"])
+        ts(f_(15, 16), T.vf[:], 3071.5, A.is_lt, ["vf"], ["val"])
+
+    def move_list():
+        km = T.key[:, 480:496]
+        ts(n_(3, 16), km, 31, A.bitwise_and, ["kmax"], ["c4i"])
+        ts(n_(2, 16), km, 5, A.arith_shift_right, ["kmax"], ["c3i"], s2=63, op1=A.bitwise_and)
+        cp(b_(1, 16), n_(3, 16), ["c4i"], ["lb"])
+        cp(b_(0, 16), n_(2, 16), ["c3i"], ["hb"])
+        for i in range(16):
+            mm(T.ps3[:, i:256:16], T.XLh[:, sl(i)], b_(0, 16), True, False, ["XLh", "hb"], (), ["ps3"])
+            mm(T.ps3[:, i:256:16], T.XLl[:, sl(i)], b_(1, 16), False, True, ["XLl", "lb"], (), ["ps3"])
+        act(T.RD[:], T.ps3[:, 0:256], ["ps3", "c5"], ["RD"], f=F.Identity, bias=col(5))
+        tt(f_(2, 16), f_(0, 16), f_(14, 16), A.mult, ["mv", "vt"], ["m1"])
+        tt(u_(0, 16), f_(2, 16), tr(1, 16), A.add, ["m1", "trP"], ["voff"])
+
+    def move_put(last):
+        cp(T.BW[:, 0:4240].indirect(u_(0, 16)), T.RD[:], ["RD", "voff"], BWT)
+        if not last:
+            keep()
+
+    def refuse_a():
+        tt(b_(2, 16), f_(15, 16), f_(0, 16), A.subtract, ["val", "mv"], ["rf"])
+        op("v", lambda q: q.tensor_tensor_scan(b_(3, 16), T.ONE[:, 0:16], b_(2, 16), 0.0, A.mult, A.add), ["ONE", "rf"], ["finc"])
+        mm(T.ps4[:, 0:16], T.M1g[:], b_(2, 16), True, False, ["M1g", "rf"], ["ps4"])
+        mm(T.ps4[:, 0:16], T.BD[:], b_(3, 16), False, True, ["BD", "finc"], (), ["ps4"])
+
+    def refuse_b():
+        ts(f_(3, 16), T.ps4[:, 0:16], 4095.0, A.add, ["ps4"], ["rq"])
+        ts(f_(4, 16), f_(3, 16), 95.5, A.is_lt, ["rq"], ["rs"])
+        tt(f_(5, 16), f_(3, 16), tr(3, 16), A.subtract, ["rq", "trR"], ["rt"])
+        tt(f_(6, 16), f_(4, 16), f_(5, 16), A.mult, ["rs", "rt"], ["rr"])
+        tt(u_(1, 16), f_(6, 16), tr(3, 16), A.add, ["rr", "trR"], ["roff"])
+
+    def refuse_c(t):
+        G = T["GS%d" % t]
+        ga, gb = "GSa%d" % t, "GSb%d" % t
+        cp(G[:, 0:448].indirect(u_(1, 16)), T.xB[:], ["xB", "roff"], [ga, gb])
+        cp(G[:, 96:544].indirect(u_(1, 16)), T.Dg[:], ["Dg", "roff", ga], [gb])
+        dst, src = cores[(r + 1 + t % (N - 1)) % N], cores[(r - 1 - t % (N - 1)) % N]
+        send(T["GX%d" % t][:], G[:, 0:192], dst, "gu%d" % t, [ga, gb])
+        arrive("gu%d" % t, len(engs(src, core)), "GX%d" % t)
+
+    def parity_a():
+        op("v", lambda q: q.tensor_reduce(f_(7, 1), f_(0, 16), AxisListType.X, A.add), ["mv"], ["mr"])
+        cp(b_(4, 1), f_(7, 1), ["mr"], ["mrb"])
+        mm(T.ps4[:, 16:17], T.ONE[:, 0:128], b_(4, 1), True, True, ["ONE", "mrb"], (), ["ps4"])
+
+    def parity_b(t):
+        cp(n_(1, 1), T.ps4[:, 16:17], ["ps4"], ["pi"])
+        ts(n_(1, 1), n_(1, 1), 1, A.bitwise_and, ["pi"], ["pi"])
+        ts(T.thr[:, t + 1:t + 2], n_(1, 1), SC, A.mult, ["pi"], ["thr%d" % (t + 1)], s2=9 * SC, op1=A.add)
+
+    def dedup_a(nj):
+        ts(f_(8, nj), n_(0, nj), 1.0, A.add, ["c1i"], ["cp1"])
+        tt(f_(10, nj), n_(0, nj), tr(2, nj), A.subtract, ["c1i", "trS"], ["ct2"])
+        tt(f_(9, nj), f_(8, nj), f_(0, nj), A.mult, ["cp1", "mv"], ["cmf"])
+        cp(T.cmh[:, 0:nj], f_(9, nj), ["cmf"], ["cmh"])
+        for i in range(16):
+            mm(T.ps5[:, i:16 * nj:16], T.XA[:, sl(i)], T.cmh[:, 0:nj], True, True, ["XA", "cmh"], (), ["ps5"])
+
+    def dedup_b(nj):
+        n = 16 * nj
+        cp(T.cR[:, 0:n], T.ps5[:, 0:n], ["ps5"], ["cR"])
+        mm(T.ps5[:, 0:n], T.BD[:], T.ZER[:, 0:n], True, False, ["BD", "ZER"], ["ps5"])
+        for j in range(nj):
+            ts(T.DE[:, j, 0:n - 16 * j], T.cR[:, 16 * j:n], T.sml[:, 144 + j:145 + j], A.is_equal, ["cR", "cmf"], ["DE%d" % j])
+            if j < nj - 1:
+                mm(T.ps5[:, 16 * (j + 1):n], T.BD[:], T.DE[:, j, 16:n - 16 * j], False, False, ["BD", "DE%d" % j], (), ["ps5"])
+        tt(T.DMb[:, 0:nj, :], T.DE[:, 0:nj, 0:16], T.MK[:, 0:nj, :], A.mult, ["DE%d" % j for j in range(nj)] + ["MK"], ["DMb"])
+        mm(T.ps5[:, 0:n], T.BD[:], T.DMb[:, 0:nj, :], False, True, ["BD", "DMb"], (), ["ps5"])
+
+    def dedup_c(nj):
+        n = 16 * nj
+        cp(T.dupR[:, 0:n], T.ps5[:, 0:n], ["ps5"], ["dupR"])
+        for i in range(16):
+            mm(T.ps6[:, 16:16 + nj], T.XE[:, sl(i)], T.dupR[:, i:n:16], i == 0, i == 15, ["XE", "dupR"], (), ["ps6"])
+
+    def dedup_d(nj, x, xt):
+        ts(f_(11, nj), T.ps6[:, 16:16 + nj], 0.5, A.is_lt, ["ps6"], ["nd"])
+        tt(f_(12, nj), f_(11, nj), f_(0, nj), A.mult, ["nd", "mv"], ["fm"])
+        tt(f_(13, nj), f_(12, nj), f_(10, nj), A.mult, ["fm", "ct2"], ["fq"])
+        tt(u_(2, nj), f_(13, nj), tr(2, nj), A.add, ["fq", "trS"], ["soff"])
+        cp(T.SWIN[:, 0:2304].indirect(u_(2, nj)), x, [xt, "soff"], ["S"])
+
+    for t in range(RO):
+        last = t == RO - 1
+        if t:
+            gx, gt = T["GX%d" % (t - 1)], "GX%d" % (t - 1)
+            ghosts_in(t - 1)
+            ext("XP", "BW", "ps0", 0, 192, True, True, ["BW"])
+            dedup_b(16)
+            anchors("PL")
+        dbl(1, 0)
+        if t:
+            dedup_c(16)
+        dbl(1, 1); dbl(1, 2)
+        if t:
+            dedup_d(16, T.xB[:], "xB")
+        anchors("PL1")
+        if t:
+            spread(gx[:, 0:96], gt, "XXg", Q, range(16), "s")
+            choose_a(gx[:, 96:192], gt, 6)
+        dbl(2, 0)
+        if t == 0:
+            fill("SA", "BA", [], 1.0)
+        else:
+            choose_b(6)
+        dbl(2, 1); dbl(2, 2)
+        if t:
+            choose_c(6)
+        anchors("PL2")
+        L3a()
+        if t == 0:
+            consts3()
+            fill("XE", "BG", [], SC)
+            L3v()
+        else:
+            choose_d("XXg", 6, [(0, 6)])
+            L3v()
+            choose_e(6); moved(t - 1, 6); dedup_a(6)
+        L3e()
+        if t:
+            dedup_b(6)
+        L3b()
+        if t:
+            dedup_c(6)
+        L3c()
+        if t:
+            dedup_d(6, gx[:, 0:96], gt)
+        beaten()
+        compact(t)
+        own_data()
+        spread(T.xB[:], "xB", "XX", 256, range(0, 9), "s")
+        choose_a(T.Dg[:], "Dg", 16)
+        spread(T.xB[:], "xB", "XX", 256, range(9, 16), "v")
+        early()
+        choose_b(16)
+        if not last:
+            ghosts_b(t)
+        choose_c(16)
+        choose_d("XX", 16, [(0, 4), (4, 8), (8, 12), (12, 16)])
+        choose_e(16)
+        moved(t, 16)
+        refuse_a()
+        if last:
+            dedup_a(16)
+            refuse_b(); refuse_c(t)
+        else:
+            move_list()
+            refuse_b()
+            dedup_a(16)
+            parity_a()
+            refuse_c(t)
+            move_put(False)
+            parity_b(t)
+    gx, gt = T.GX2, "GX2"
+    dedup_b(16); dedup_c(16)
+    choose_a(gx[:, 96:192], gt, 6)
+    spread(gx[:, 0:96], gt, "XXg", Q, range(16), "s")
+    dedup_d(16, T.xB[:], "xB")
+    choose_b(6); choose_c(6)
+    move_list()
+    choose_d("XXg", 6, [(0, 6)])
+    move_put(True)
+    choose_e(6); moved(2, 6); dedup_a(6)
+
+    def outs(b):
+        p = ["ps0", "ps1", "ps3"][b % 3]
+        mm(T[p][0:40, :], T.OC[:], T.BW[:, 512 * b:512 * b + 512], True, True, ["OC", "BW"], [p])
+        act(T.OUT[:, 512 * b:512 * b + 512], T[p][0:40, :], [p], (), ["OUT"])
+
+    dedup_b(6)
+    for b in range(2):
+        outs(b)
+    dedup_c(6); dedup_d(6, gx[:, 0:96], gt)
+    for b in range(2, 6):
+        outs(b)
+    dma(T.yan[:], T.OUT[0:8, :], ["OUT"])
+    dma(T.yof[:], T.OUT[32:40, :], ["OUT"])
+    dma(T.ys[:], T.SWIN[:, 0:W], ["S"])
+    for s in total:
+        g.wait_ge(T.sem[s], total[s])

@@ -1,8 +1,9 @@
-from concourse.mybir import AluOpType as A, AxisListType, ActivationFunctionType as F
+from concourse.mybir import AluOpType as A, ActivationFunctionType as F
 
 V, W, NG, Q, RO = 3072, 2048, 896, 96, 3
 ROOT, BWW = 3968, 3984
 NEG = -4194304.0
+BIG = 1048576.0
 SC = 32768.0
 TINY = 2.0 ** -120
 bf, f3, i3, u1, fh = "bfloat16", "float32", "int32", "uint16", "float16"
@@ -14,21 +15,24 @@ def _sb(dt_, **kw):
         SCRATCH[n] = ("sbuf", [128] + (w if isinstance(w, list) else [w]), dt_)
 
 
-_sb(i3, anL=192, ofL=248, snL=56, tA=192, tB=248, tE=248, DI=192, DL=192, dg1=192, dg2=192, posI=192, loI=192, hiI=192,
-    ci=256, cm=256, key=496, smi=96, cpi=4, crow=128, crq=128, crg=128, c8=8, kri=256, kr2=256, j16=16)
-_sb(bf, pl0=248, pl1=248, pl2=248, pl3=248, XR=3968, XW=3088, SWIN=2304, WK=2048, BW=4240, SW1=BWW, SW2=BWW, G2=3088, GW=V,
-    Zb=V, Zs=V,
-    dh=192, dlo=192, bits=V, SG=512, bT=192, binc=192, lob=192, hib=192, sq=192, OHL=V, OHH=V, indA=256, indB=256, ov=240,
-    xB=256, G2g=256, Dg=256, XX=4096, XXg=1536, B2=[16, 256], wkg=256, smb=80, RD=256, DE=[16, 256], DMb=[16, 16], dupR=256,
-    XP=2048, XS=2048, XE=2048, XLh=2048, XLl=2048, SA=2048, BD=128, BDt=128, M1=128, M1g=128, ID=128, NI=128, I7=128, CB=128, ONE=256,
-    ZER=256, OC=40, krow=256, KC=256, MK=[16, 16], GL0=NG, GL1=NG, GO0=NG, GO1=NG, GS0=544, GS1=544, GS2=544, GX0=192, GX1=192, GX2=192)
-_sb(f3, vf=16, sml=256, thr=3, ccol=64, BG=8, BA=8, tr=64)
-_sb(u1, SL=56, PL=192, PL1=192, PL2=192, DU=192, cu=256, smu=80)
-_sb(fh, ctc=[16, 32], ctt=[16, 32], cmh=16, cR=256, XA=2048, Ie=128, Io=128)
+_sb(i3, anL=192, ofL=248, snL=56, tI=496, DI=192, DL=208, dg=384, smi=96, cpi=8, crow=160, crq=128, crg=128, kri=256, j16=16,
+    Dw=24)
+_sb(bf, pl=992, XR=3968, XW=3088, SWIN=2304, WK=2048, BW=4240, W2=BWW, W3=BWW, G3=V, GW=V, Z1=V, Z2=V, dgb=384, bits=4096,
+    SG=1536, fl=192, binc=192, o1=256, o2=256, o3=256, OH=256, xB=528, smb=128, RD=256, EE=1008, XA=2048, XLh=2048, XLl=2048,
+    ZR=2048, BD=128, BDt=128, M1g=128, ID=128, NI=128, I7=128, I12=128, I16=128, IK=128, IeP=160, IoP=160, ONE=192, OC=40,
+    krow=512, kst=512, KQ=256, KL2=256, RST=256, RS32=512, KC=256, KCg=96, MK=512, MKg=192, sg=1024, dd=512, de=512,
+    GL0=NG, GL1=NG, GO0=NG, GO1=NG, GS0=192, GS1=192, GS2=192, GX0=192, GX1=192, GX2=192)
+_sb(f3, vf=16, sml=256, thr=4, ccol=32, BG=8, tr=48, CT=2048, PF=200, LW=40, GN=40, C32=32, key=256, cmw=16, rowS=512)
+_sb(u1, SL=56, PL=192, PL1=192, PL2=192, DU=192, cu=256, smu=128, REP=16, RJ=32, RJg=12, GD0=8, GD1=8, GD2=8, GE0=8, GE1=8, GE2=8)
+_sb(fh, CG=256, TB=[32, 8], TBg=[32, 3], Ds=256, cmh=16)
 SCRATCH["OUT"] = ("sbuf", [40, V], f3)
 for _b in range(8):
     SCRATCH["ps%d" % _b] = ("psum", [128, 512], f3)
-SEMAPHORES = ["sv", "ss", "sp", "sg", "loc", "gh0", "gh1", "gu0", "gu1", "gu2"] + ["d%d" % k for k in range(60)]
+SEMAPHORES = ["sv", "ss", "sp", "sg", "loc", "gh0", "gh1", "gu0", "gu1", "gu2", "gd0", "gd1", "gd2"] + ["d%d" % k for k in range(90)]
+ALL = (1 << 128) - 1
+
+CUT = {0: (1152, 1152), 1: (1792, 1792)}
+CUT3 = {0: (768, 2304), 1: (1152, 2688)}
 
 
 def rank_program(g, core, T, topo):
@@ -42,13 +46,32 @@ def rank_program(g, core, T, topo):
     cnt = {"v": 0, "s": 0, "p": 0, "g": 0}
     seen = {e: {} for e in ENG}
     know = {}
-    tags = {}
+    hist = {}
     total = {}
 
-    def tag(t):
-        if t not in tags:
-            tags[t] = {"w": [], "a": [], "r": []}
-        return tags[t]
+    def R(n, a=0, b=None, s=1, rows=None):
+        w = T[n].shape[1]
+        b = w if b is None else b
+        rs = slice(None) if rows is None else slice(*rows)
+        m = ALL
+        if rows is not None:
+            m = 0
+            for p in range(T[n].shape[0])[rs]:
+                m |= 1 << p
+        return (T[n][rs, a:b:s] if s > 1 else T[n][rs, a:b], [(n, a, a + (b - a - 1) // s * s, s, m)])
+
+    def R3(n, ap):
+        return (ap, [(n, 0, 1 << 20, 1, ALL)])
+
+    def IND(w, o):
+        return (w[0].indirect(o[0]), w[1], o[1])
+
+    def meet(x, y):
+        if x[0][:2] == "ps":
+            return True
+        if x[2] < y[1] or y[2] < x[1] or not x[4] & y[4]:
+            return False
+        return not (x[3] == y[3] > 1 and (x[1] - y[1]) % x[3])
 
     def waits(e, deps):
         m = {}
@@ -66,611 +89,704 @@ def rank_program(g, core, T, topo):
                 seen[e][s2] = max(seen[e].get(s2, 0), v2)
             seen[e][sem] = max(seen[e].get(sem, 0), val)
 
-    def deps_of(e, rd, wr, ap):
-        def some(x):
-            return [(s, n) for s, n, q in x if not (q == "p" and e == "p")]
+    def deps_of(e, rd, wr):
         d = []
-        for t in rd:
-            x = tag(t)
-            d += some(x["w"] + x["a"])
-            if t[:2] == "ps":
-                d += [(s, n) for s, n, q in x["r"] if q != e]
-        for t in wr:
-            x = tag(t)
-            d += some(x["w"] + x["a"] + x["r"])
-        for t in ap:
-            x = tag(t)
-            if x["r"]:
-                x["w"] = x["r"]; x["a"] = []; x["r"] = []
-            d += some(x["w"])
+        for x in rd:
+            for y, w, s, n, q in hist.get(x[0], ()):
+                if not (q == e == "p") and (w or (x[0][:2] == "ps" and q != e)) and meet(x, y):
+                    d.append((s, n))
+        for x in wr:
+            for y, w, s, n, q in hist.get(x[0], ()):
+                if not (q == e == "p") and meet(x, y):
+                    d.append((s, n))
         return d
 
-    def note(me, rd, wr, ap):
-        for t in rd:
-            tag(t)["r"].append(me)
-        for t in wr:
-            x = tag(t); x["w"] = [me]; x["a"] = []; x["r"] = []
-        for t in ap:
-            tag(t)["a"].append(me)
+    def note(s, n, q, rd, wr):
+        for x in wr:
+            h = hist.setdefault(x[0], [])
+            if x[0][:2] == "ps":
+                h[:] = []
+            elif x[3] == 1:
+                h[:] = [y for y in h if not (x[1] <= y[0][1] and y[0][2] <= x[2] and y[0][4] & ~x[4] == 0)]
+            h.append((x, True, s, n, q))
+        for x in rd:
+            h = hist.setdefault(x[0], [])
+            h[:] = [y for y in h if not (not y[1] and y[4] == q and y[2] == s and y[0] == x)]
+            h.append((x, False, s, n, q))
 
-    def op(e, fn, rd=(), wr=(), ap=()):
-        waits(e, deps_of(e, rd, wr, ap))
+    def split(out, ins):
+        rd = list(out[2]) if len(out) > 2 else []
+        for a in ins:
+            if isinstance(a, tuple):
+                rd += a[1] + (a[2] if len(a) > 2 else [])
+        return rd, out[1]
+
+    def ap(a):
+        return a[0] if isinstance(a, tuple) else a
+
+    def op(e, fn, out, ins, more=()):
+        rd, wr = split(out, ins)
+        wr = wr + list(more)
+        waits(e, deps_of(e, rd, wr))
         cnt[e] += 1
         fn(ENG[e]).then_inc(T.sem[SEM[e]], 1)
         know[(SEM[e], cnt[e])] = dict(seen[e])
         total[SEM[e]] = cnt[e]
-        note((SEM[e], cnt[e], e), rd, wr, ap)
+        note(SEM[e], cnt[e], e, rd, wr)
 
     nd = [0]
 
-    def dma(out, in_, rd=(), wr=(), ap=()):
-        waits("y", deps_of("dma", rd, wr, ap))
+    def dma(out, in_):
+        rd, wr = split(out, [in_])
+        waits("y", deps_of("dma", rd, wr))
         s = "d%d" % nd[0]; nd[0] += 1
-        g.sync.dma_start(out, in_).then_inc(T.sem[s], 16)
+        g.sync.dma_start(out[0], in_[0]).then_inc(T.sem[s], 16)
         know[(s, 16)] = dict(seen["y"])
         total[s] = 16
-        note((s, 16, "dma"), rd, wr, ap)
+        note(s, 16, s, rd, wr)
+
+    def hbm(n):
+        return (T[n][:], [])
 
     def engs(src, dst):
         return topo.engines(src, dst)[:8]
 
     def arrive(sem, n, t):
         total[sem] = n
-        tag(t)["w"].append((sem, n, "rem"))
+        note(sem, n, sem, [], R(t)[1])
 
-    def send(out, in_, dst, sem, rd):
-        waits("g", deps_of("rem", rd, (), ()))
+    def send(out, in_, dst, sem):
+        waits("g", deps_of("rem", in_[1], []))
         rid, pid, _ = topo.addr(dst)
         e = engs(core, dst)
         m = 0
         for k in e:
             m |= 1 << k
-        g.remote_dma(out, in_, T.sem[sem], T.sem.loc, pid, rid, m)
+        g.remote_dma(out[0], in_[0], T.sem[sem], T.sem.loc, pid, rid, m)
         total["loc"] = total.get("loc", 0) + len(e)
 
-    def ts(out, in0, s1, op0, rd, wr=(), ap=(), s2=None, op1=None):
+    def ts(out, in0, s1, op0, s2=None, op1=None):
         if op1 is None:
-            op("v", lambda q: q.tensor_scalar(out, in0, s1, None, op0), rd, wr, ap)
+            op("v", lambda q: q.tensor_scalar(out[0], in0[0], ap(s1), None, op0), out, [in0, s1])
         else:
-            op("v", lambda q: q.tensor_scalar(out, in0, s1, s2, op0, op1), rd, wr, ap)
+            op("v", lambda q: q.tensor_scalar(out[0], in0[0], ap(s1), ap(s2), op0, op1), out, [in0, s1, s2])
 
-    def tt(out, a, b, o, rd, wr=(), ap=()):
-        op("v", lambda q: q.tensor_tensor(out, a, b, o), rd, wr, ap)
+    def tt(out, a, b, o):
+        op("v", lambda q: q.tensor_tensor(out[0], a[0], b[0], o), out, [a, b])
 
-    def cp(out, in_, rd, wr=(), ap=()):
-        op("v", lambda q: q.tensor_copy(out, in_), rd, wr, ap)
+    def cp(out, in_):
+        op("v", lambda q: q.tensor_copy(out[0], in_[0]), out, [in_])
 
-    def ms(out, c, wr=(), ap=()):
-        op("v", lambda q: q.memset(out, c), (), wr, ap)
+    def ms(out, c):
+        op("v", lambda q: q.memset(out[0], c), out, [])
 
-    def act(out, in_, rd, wr=(), ap=(), f=F.Copy, **kw):
-        op("s", lambda q: q.activation(out, in_, f, **kw), rd, wr, ap)
+    def scan(out, d0, d1):
+        op("v", lambda q: q.tensor_tensor_scan(out[0], d0[0], d1[0], 0.0, A.mult, A.add), out, [d0, d1])
 
-    def mm(out, l, rh, st, sp, rd, wr=(), ap=()):
-        op("p", lambda q: q.matmul(out, l, rh, st, sp), rd, wr, ap)
+    def act(out, in_, f=F.Copy, **kw):
+        more = kw["accum_out"][1] if "accum_out" in kw else []
+        op("s", lambda q: q.activation(out[0], in_[0], f, **{k: ap(x) for k, x in kw.items()}), out,
+           [in_] + [x for k, x in kw.items() if k != "accum_out"], more)
 
-    def iota(out, pat, base, cm, wr):
-        op("g", lambda q: q.iota(out, pat, base, cm), (), wr)
+    def mm(out, l, rh, st, sp):
+        op("p", lambda q: q.matmul(out[0], l[0], rh[0], st, sp), out, [l, rh])
 
-    def sl(i):
-        return slice(i * 128, (i + 1) * 128)
+    def iota(out, pat, base=0, cm=0):
+        if T[out[1][0][0]].dtype == T.cpi.dtype:
+            op("g", lambda q: q.iota(out[0], pat, base, cm), out, [])
+        else:
+            op("g", lambda q: q.iota(out[0], pat, base, cm, allow_small_or_imprecise_dtypes=True), out, [])
 
-    f_ = lambda k, nj: T.sml[:, 16 * k:16 * k + nj]
-    n_ = lambda k, nj: T.smi[:, 16 * k:16 * k + nj]
-    b_ = lambda k, nj: T.smb[:, 16 * k:16 * k + nj]
-    u_ = lambda k, nj: T.smu[:, 16 * k:16 * k + nj]
-    tr = lambda k, nj: T.tr[:, 16 * k:16 * k + nj]
+    f_ = lambda k, nj=16: R("sml", 16 * k, 16 * k + nj)
+    n_ = lambda k, nj=16: R("smi", 16 * k, 16 * k + nj)
+    b_ = lambda k, nj=16: R("smb", 16 * k, 16 * k + nj)
+    u_ = lambda k, nj=16: R("smu", 16 * k, 16 * k + nj)
+    tr = lambda k, nj=16: R("tr", 16 * k, 16 * k + nj)
+    col = lambda k: R("ccol", k, k + 1)
+    cpi = lambda k: R("cpi", k, k + 1)
+    EP, ES, E1, EI, EC, EH = range(6)
 
-    dma(T.anL[:], T.an0[:], (), ["anL"])
-    dma(T.ofL[:], T.of0[:], (), ["ofL"])
-    dma(T.snL[:], T.snd[:], (), ["snL"])
-    dma(T.SWIN[:, 0:W], T.s0[:], (), ["S"])
-    dma(T.XW[:, 0:V], T.x[:], (), ["XWx"])
-    dma(T.WK[:], T.wk[:], (), ["WK"])
-    iota(T.cpi[:, 0:1], [[1, 1]], 0, 1, ["cpi"])
-    iota(T.c8[:], [[1, 8]], 0, 0, ["c8"])
-    iota(T.crow[:], [[1, 128]], 0, 0, ["crow"])
-    iota(T.j16[:], [[16, 16]], 0, 0, ["j16"])
-    iota(T.kri[:], [[1, 256]], 0, 0, ["kri"])
-    for n, w in (("Zb", V), ("Zs", V), ("SA", 2048), ("XE", 2048), ("XLh", 2048), ("XLl", 2048)):
-        op("g", lambda q, n=n, w=w: q.iota(T[n][:], [[0, w]], 0, 0, allow_small_or_imprecise_dtypes=True), (), [n])
-    ms(T.XR[:], 0.0, ["XR"])
+    def sel(n, i):
+        return R("EE", 144 * n + 15 - i, 144 * n + 143 - i)
 
-    def col(k):
-        return T.ccol[:, k:k + 1]
+    def ext(n, src, c0, c1, bank, o0, st, sp, i0=0, i1=16, step=16):
+        for i in range(i0, i1):
+            mm(R(bank, o0, o0 + (c1 - c0) // step), sel(n, i), R(src, c0 + i, c1, step), st and i == i0, sp and i == i1 - 1)
 
-    ts(T.cpi[:, 1:2], T.cpi[:, 0:1], 15, A.bitwise_and, ["cpi"], ["cpi1"])
-    ts(T.cpi[:, 2:3], T.cpi[:, 0:1], 4, A.arith_shift_right, ["cpi"], ["cpi2"])
-    ts(T.cpi[:, 3:4], T.cpi[:, 0:1], 7, A.bitwise_and, ["cpi"], ["cpi3"])
-    cp(col(0), T.cpi[:, 0:1], ["cpi"], ["c0"])
-    cp(col(1), T.cpi[:, 1:2], ["cpi1"], ["c1"])
-    cp(col(2), T.cpi[:, 2:3], ["cpi2"], ["c2"])
-    cp(col(8), T.cpi[:, 3:4], ["cpi3"], ["c8c"])
-    ts(col(9), col(1), 0.0, A.is_equal, ["c1"], ["c9"], s2=256.0, op1=A.mult)
-    ts(col(10), col(1), 1.0, A.is_equal, ["c1"], ["c10"])
-    ts(T.BG[:], T.c8[:], col(2), A.is_equal, ["c8", "c2"], ["BG"])
-    tt(col(3), col(9), col(10), A.add, ["c9", "c10"], ["c3"])
-    ts(col(11), col(1), 2.0, A.is_equal, ["c1"], ["c11"], s2=32.0, op1=A.mult)
-    ts(col(12), col(1), 10.0, A.is_equal, ["c1"], ["c12"])
-    ts(col(15), col(1), 2.0, A.is_equal, ["c1"], ["c15"], s2=-252.0, op1=A.mult)
-    ts(col(13), col(9), 15.0 / 256.0, A.mult, ["c9"], ["c13"])
-    ts(col(14), col(10), 128.0, A.mult, ["c10"], ["c14"])
-    tt(col(4), col(11), col(12), A.add, ["c11", "c12"], ["c4"])
-    tt(col(5), col(13), col(14), A.add, ["c13", "c14"], ["c5"])
-    ms(T.pl0[:, 192:248], 15.0, ["pl0g"]); ms(T.pl1[:, 192:248], 128.0, ["pl1g"])
-    ts(T.tA[:], T.anL[:], 8, A.arith_shift_right, ["anL"], ["tA"])
-    ts(T.tB[:, 0:192], T.anL[:], 255, A.bitwise_and, ["anL"], ["tB"])
-    cp(T.pl0[:, 0:192], T.tA[:], ["tA"], ["pl0"])
-    cp(T.pl1[:, 0:192], T.tB[:, 0:192], ["tB"], ["pl1"])
-    dma(T.XR[0::16, :], T.pl0[:], ["pl0", "pl0g"], (), ["XR"])
-    dma(T.XR[1::16, :], T.pl1[:], ["pl1", "pl1g"], (), ["XR"])
-    ts(T.tB[:], T.ofL[:], 5, A.arith_shift_right, ["ofL"], ["tB"])
-    ts(T.tE[:], T.ofL[:], 31, A.bitwise_and, ["ofL"], ["tE"])
-    cp(T.pl2[:], T.tB[:], ["tB"], ["pl2"])
-    cp(T.pl3[:], T.tE[:], ["tE"], ["pl3"])
-    dma(T.XR[2::16, :], T.pl2[:], ["pl2"], (), ["XR"])
-    dma(T.XR[10::16, :], T.pl3[:], ["pl3"], (), ["XR"])
-    cp(T.PL[:], T.anL[:], ["anL"], ["PL"])
-    ms(T.ZER[:], 0.0, ["ZER"])
-    ms(T.XP[:], 0.0, ["XP"]); ms(T.XS[:], 0.0, ["XS"])
-    for b in ("BW", "SW1", "SW2"):
-        ts(T[b][:, ROOT:BWW], T.ZER[:, 0:16], col(5), A.add, ["ZER", "c5"], [b + "r"])
+    dma(R("anL"), hbm("an0"))
+    dma(R("ofL"), hbm("of0"))
+    iota(cpi(0), [[1, 1]], 0, 1)
+    iota(R("crow"), [[1, 160]], -16)
+    iota(R("j16"), [[16, 16]])
+    iota(R("krow"), [[0, 2], [1, 256]])
+    iota(R("kst"), [[256, 2], [0, 256]])
+    iota(R("kri"), [[1, 256]])
+    ms(R("XR"), 0.0)
+    ms(R("pl", 192, 248), 15.0); ms(R("pl", 440, 496), 128.0)
+    ts(cpi(1), cpi(0), 15, A.bitwise_and)
+    ts(cpi(2), cpi(0), 4, A.arith_shift_right)
+    ts(R("tI", 0, 192), R("anL"), 8, A.arith_shift_right)
+    ts(R("tI", 192, 384), R("anL"), 255, A.bitwise_and)
+    cp(R("pl", 0, 192), R("tI", 0, 192))
+    cp(R("pl", 248, 440), R("tI", 192, 384))
+    dma(R("XR", rows=(0, 128, 16)), R("pl", 0, 248))
+    dma(R("XR", rows=(1, 128, 16)), R("pl", 248, 496))
+    ts(R("tI", 0, 248), R("ofL"), 5, A.arith_shift_right)
+    ts(R("tI", 248, 496), R("ofL"), 31, A.bitwise_and)
+    cp(R("pl", 496, 992), R("tI"))
+    dma(R("XR", rows=(2, 128, 16)), R("pl", 496, 744))
+    dma(R("XR", rows=(10, 128, 16)), R("pl", 744, 992))
+    dma(R("WK"), hbm("wk"))
+    dma(R("snL"), hbm("snd"))
+    dma(R("SWIN", 0, W), hbm("s0"))
+    dma(R("XW", 0, V), hbm("x"))
+    cp(R("PL"), R("anL"))
+    cp(R("ccol", 0, 3), R("cpi", 0, 3))
+    ts(cpi(3), cpi(2), 1, A.bitwise_and)
+    ts(cpi(4), cpi(0), 2, A.bitwise_and)
+    ms(R("EE"), 0.0)
+    ts(col(9), col(1), 0.0, A.is_equal)
+    ts(col(10), col(1), 1.0, A.is_equal)
+    ts(col(11), col(1), 7.5, A.is_lt, 31.0, A.mult)
+    cp(col(12), cpi(4))
+    cp(col(7), cpi(3))
+    ts(R("BG"), R("crow", 16, 24), col(2), A.is_equal)
+    ts(col(3), col(9), 256.0, A.mult, col(10), A.add)
+    ts(col(13), col(10), 128.0, A.mult)
+    ts(col(11), col(11), 1.0, A.add)
+    ts(col(5), col(9), 15.0, A.mult, col(13), A.add)
+    ts(col(4), col(12), 0.5, A.mult, col(11), A.mult)
+    ts(col(6), col(7), -1.0, A.mult, 1.0, A.add)
+    ts(col(8), col(1), 11.5, A.is_lt)
+    for n, w in ((EP, col(3)), (ES, col(4)), (E1, 1.0), (EI, col(1)), (EC, SC), (EH, SC / 2)):
+        ts(R("EE", 144 * n + 15, 144 * n + 143, 16), R("BG"), w, A.mult)
+    ts(R("ID"), R("crow", 16, 144), col(0), A.is_equal)
+    ms(R("ZR"), 0.0)
+    for b in ("BW", "W2", "W3"):
+        ts(R(b, ROOT, BWW), R("ZR", 0, 16), col(5), A.add)
+    ts(R("I7"), R("ID"), 7.0, A.mult)
+    ts(R("IK"), R("ID"), -1024.0, A.mult)
+    ms(R("Z1", CUT[0][0], V), 0.0)
+    ms(R("Z2", CUT[0][1], V), 0.0)
+    for n, base, st in (("XLh", -2048, 1024), ("XLl", -10240, 1024), ("XA", 0, 0)):
+        op("g", lambda q, n=n, base=base, st=st: q.affine_select(T[n][:], T.ZR[:], [[-1, 16], [-16, 8], [st, 16]], A.not_equal, 1.0, base, 1),
+           R(n), [R("ZR")])
 
-    def fill(n, src, rd, scale, o=None):
-        for i in range(16):
-            act(T[n][:, i * 128 + (i if o is None else o):(i + 1) * 128:16], T[src][:], [src] + rd, (), [n], scale=col(16 + i) if scale is None else scale)
+    def candidates(b):
+        c = (512 * b, 512 * b + 512)
+        s = R("sg", 512 * (b % 2), 512 * (b % 2) + 512)
+        for p in ("ps%d" % (4 + b % 2), "ps%d" % (6 + b % 2)):
+            two = p[2] in "67"
+            mm(R(p), R("I7"), R("WK", *c), True, False)
+            mm(R(p), R("ID"), R("krow"), False, False)
+            mm(R(p), R("ID"), R("kst"), False, not two)
+            if two:
+                mm(R(p), R("IK"), s, False, True)
+                act(R("CT", *c), R(p), F.Identity, bias=512.0 * b - 1024.0)
+            else:
+                act(s, R(p), F.Sign, bias=512.0 * b - 2047.5)
 
-    fill("XP", "BG", ["c3"], col(3))
-    fill("XS", "BG", ["c4"], col(4))
+    candidates(0)
+    for i in range(16):
+        (cp if i % 8 < 6 else act)(R("BW", i, ROOT, 16), R("XR", i * 248, (i + 1) * 248))
 
     def consts2():
-        ts(T.crq[:], T.crow[:], 15, A.bitwise_and, ["crow"], ["crq"])
-        ts(T.crg[:], T.crow[:], 4, A.arith_shift_right, ["crow"], ["crg"])
-        ts(T.ID[:], T.crow[:], col(0), A.is_equal, ["crow", "c0"], ["ID"])
-        ts(T.BD[:], T.crg[:], col(2), A.is_equal, ["crg", "c2"], ["BD"])
-        ms(T.ONE[:], 1.0, ["ONE"])
-        ts(T.BDt[:], T.crow[:], col(0), A.is_gt, ["crow", "c0"], ["BDt"], s2=-1.0, op1=A.add)
-        ts(T.M1[:], T.ID[:], -4096.0, A.mult, ["ID"], ["M1"])
-        ts(T.NI[:], T.ID[:], -1.0, A.mult, ["ID"], ["NI"])
-        tt(T.M1[:], T.M1[:], T.BDt[:], A.add, ["M1", "BDt"], ["M1"])
-        ms(T.thr[:, 0:1], 9 * SC, ["thr0"])
-        ts(T.XW[:, V:V + 16], T.ZER[:, 0:16], NEG, A.add, ["ZER"], ["XWp"])
-        cp(T.G2[:, V:V + 16], T.ZER[:, 0:16], ["ZER"], ["G2p"])
-        cp(T.krow[:], T.kri[:], ["kri"], ["krow"])
-        ts(T.BA[:], T.c8[:], col(8), A.is_equal, ["c8", "c8c"], ["BA"], s2=128.0, op1=A.mult)
+        ts(R("crq"), R("crow", 16, 144), 15, A.bitwise_and)
+        ts(R("crg"), R("crow", 16, 144), 4, A.arith_shift_right)
+        ts(R("NI"), R("ID"), -1.0, A.mult)
+        ts(R("BD"), R("crg"), col(2), A.is_equal)
+        ts(R("BDt"), R("crq"), col(1), A.is_gt, -1.0, A.add)
+        ts(R("M1g"), R("ID"), -4096.0, A.mult)
+        tt(R("BDt"), R("BDt"), R("BD"), A.mult)
+        ms(R("ONE"), 1.0)
+        tt(R("M1g"), R("M1g"), R("BDt"), A.add)
+        ms(R("thr", 0, 1), 9 * SC)
+        ms(R("XW", V, V + 16), NEG)
+        ms(R("DL", 192, 208), 0)
+        ms(R("PF", 192, 200), BIG)
+        ms(R("LW", 32, 40), BIG)
+        ts(R("I12"), R("ID"), 12.0, A.mult)
+        ts(R("I16"), R("ID"), 16.0, A.mult)
 
     def consts3():
-        for t in range(RO):
-            ms(T["GS%d" % t][:, 0:96], NEG, ["GSa%d" % t]); ms(T["GS%d" % t][:, 96:192], 0.0, ["GSb%d" % t])
-        ts(T.GW[:], T.XR[:, 0:V], 0.0, A.mult, ["XR", "c5"], ["GW"], s2=col(5), op1=A.add)
-        a, b = T.dg1[:, 0:56], T.dg2[:, 0:56]
-        ts(a, T.snL[:], 15, A.bitwise_and, ["snL"], ["dg1"])
-        ts(b, T.snL[:], 4, A.arith_shift_right, ["snL"], ["dg2"])
-        ts(a, a, 192.0, A.mult, ["dg1"], ["dg1"])
-        tt(a, a, b, A.add, ["dg1", "dg2"], ["dg1"])
-        cp(T.SL[:], a, ["dg1"], ["SL"])
+        ts(R("dg", 0, 256), R("kri"), 15, A.bitwise_and)
+        ts(R("KL2"), R("krow", 0, 256), 1.0, A.add, col(8), A.mult)
+        ts(R("REP"), R("ZR", 0, 16), col(1), A.add)
+        ts(R("RST"), R("dg", 0, 256), 0.5, A.is_gt)
+        tt(R("KQ"), R("kri"), R("dg", 0, 256), A.subtract)
+        ts(R("KL2"), R("KL2"), -1.0, A.add)
+        ts(R("KQ"), R("KQ"), col(1), A.add)
+        ts(tr(0), R("j16"), col(1), A.add)
+        ts(R("IeP"), R("crow"), col(0), A.is_equal, col(6), A.mult)
+        ts(R("IoP"), R("crow"), col(0), A.is_equal, col(7), A.mult)
+        ts(tr(1), tr(0), float(BWW), A.add)
+        ts(tr(2), tr(0), float(W), A.add)
+        ms(R("xB", 512, 528), NEG)
 
     def consts4():
-        ts(T.I7[:], T.ID[:], 7.0, A.mult, ["ID"], ["I7"])
-        ts(T.CB[:], T.BD[:], col(4), A.mult, ["BD", "c4"], ["CB"])
-        ts(T.cpi[:, 3:4], T.cpi[:, 2:3], 1, A.bitwise_and, ["cpi2", "c8c"], ["cpi3"])
-        ts(tr(0, 16), T.j16[:], col(1), A.add, ["j16", "c1"], ["kL"])
-        ts(T.kr2[:], T.kri[:], 15, A.bitwise_and, ["kri"], ["kr2"])
-        cp(col(7), T.cpi[:, 3:4], ["cpi3"], ["c7"])
-        ts(T.BDt[:], T.crq[:], col(1), A.is_gt, ["crq", "c1"], ["BDt"], s2=-1.0, op1=A.add)
-        ts(col(6), col(7), -1.0, A.mult, ["c7"], ["c6"], s2=1.0, op1=A.add)
-        ts(T.Io[:], T.ID[:], col(7), A.mult, ["ID", "c7"], ["Io"])
-        ts(T.Ie[:], T.ID[:], col(6), A.mult, ["ID", "c6"], ["Ie"])
-        ts(tr(1, 16), tr(0, 16), float(BWW), A.add, ["kL"], ["trP"])
-        ts(tr(2, 16), tr(0, 16), float(W), A.add, ["kL"], ["trS"])
-        ts(tr(3, 16), tr(0, 16), 192.0, A.add, ["kL"], ["trR"])
-        ts(T.KC[:], T.kr2[:], -2048.0, A.mult, ["kr2"], ["KC"], s2=15 * 2048.0, op1=A.add)
-        ts(T.M1g[:], T.ID[:], -4096.0, A.mult, ["ID"], ["M1g"])
-        tt(T.BDt[:], T.BDt[:], T.BD[:], A.mult, ["BDt", "BD"], ["BDt"])
-        ts(T.ccol[:, 16:32], T.crow[:, 0:16], col(1), A.is_equal, ["crow", "c1"], ["c16"])
-        ts(T.MK[:], T.kr2[:], col(1), A.is_gt, ["kr2", "c1"], ["MK"])
-        tt(T.M1g[:], T.M1g[:], T.BDt[:], A.add, ["M1g", "BDt"], ["M1g"])
+        a, b = R("tI", 0, 56), R("tI", 64, 120)
+        ts(a, R("snL"), 15, A.bitwise_and)
+        ts(b, R("snL"), 4, A.arith_shift_right)
+        ts(R("GW"), R("XR", 0, V), 0.0, A.mult, col(5), A.add)
+        ts(a, a, 192.0, A.mult)
+        tt(R("SL"), a, b, A.add)
 
     def consts5():
-        for i in range(16):
-            ts(T.XA[:, sl(i)], T.BD[:], col(16 + i), A.mult, ["BD", "c16"], (), ["XA"])
-        fill("XLh", "BG", ["c16"], None, 2)
-        fill("XLl", "BG", ["c16"], None, 10)
-        ms(T.OC[:], 0.0, ["OC"])
-        ts(T.OC[:, 0:8], T.BG[:], col(3), A.mult, ["BG", "c3", "OC"], (), ["OC"])
-        ts(T.OC[:, 32:40], T.BG[:], col(4), A.mult, ["BG", "c4", "OC"], (), ["OC"])
+        iota(R("KC", 0, 160), [[-2048, 10], [0, 16]], 15 * 2048)
+        iota(R("KC", 160, 256), [[-2048, 6], [0, 16]], 5 * 2048 + 8 * 32768)
+        iota(R("KCg"), [[-2048, 16], [0, 6]], 15 * 2048)
+        iota(R("RS32"), [[0, 16], [1, 32]])
+        iota(R("tI", 0, 32), [[1, 2], [2, 8], [0, 2]])
+        iota(R("tI", 32, 44), [[1, 2], [2, 3], [0, 2]])
+        for n, nb in (("MK", 8), ("MKg", 3)):
+            iota(R(n), [[-16, 2], [0, nb], [1, 32]])
 
-    consts2()
-    for i in range(16):
-        o, x = T.BW[:, i:ROOT:16], T.XR[:, i * 248:(i + 1) * 248]
-        if i % 4 < 3:
-            cp(o, x, ["XR"], (), ["BW"])
+    def consts6():
+        ts(R("RS32"), R("RS32"), 0.5, A.is_gt)
+        cp(R("RJ"), R("tI", 0, 32))
+        cp(R("RJg"), R("tI", 32, 44))
+        for n in ("MK", "MKg"):
+            ts(R(n), R(n), col(1), A.is_ge, 8192.0, A.mult)
+        ms(R("C32", 0, 16), 0.0); ms(R("C32", 16, 32), 4095.0)
+        ms(R("GN", 32, 40), BIG)
+        ms(R("Dw", 16, 24), 0)
+        for t in range(RO):
+            ms(R("GE%d" % t), 0)
+        ms(R("OC"), 0.0)
+        ts(R("OC", 0, 8), R("BG"), col(3), A.mult)
+        ts(R("OC", 32, 40), R("BG"), col(4), A.mult)
+
+    LV = {1: ("BW", "PL", "Z1", "W2", "PL1", (2, 128, 8), (6, 128, 8)), 2: ("W2", "PL1", "Z2", "W3", "PL2", (2, 128, 4), (3, 128, 4))}
+
+    def addends(l, c0, c1=V):
+        w, p, z, n, pn, src, dst = LV[l]
+        dma(R(z, c0, c1, rows=src), R(w, c0, c1, rows=src))
+
+    def dbl_s(l, c0, c1, bank):
+        w, p, z, n, pn, src, dst = LV[l]
+        act(R(n, c0, c1), IND(R(w, 0, BWW), R(p, c0 // 16, c1 // 16)))
+        dma(R(n, c0, c1, rows=dst), R(w, c0, c1, rows=src))
+
+    def dbl_v(l, c0, c1, add=True):
+        w, p, z, n, pn, src, dst = LV[l]
+        if add:
+            tt(R(n, c0, c1), IND(R(w, 0, BWW), R(p, c0 // 16, c1 // 16)), R(z, c0, c1), A.add)
         else:
-            act(o, x, ["XR"], (), ["BW"])
+            cp(R(n, c0, c1), IND(R(w, 0, BWW), R(p, c0 // 16, c1 // 16)))
+            dma(R(n, c0, c1, rows=dst), R(w, c0, c1, rows=src))
 
-    def th(a):
-        return slice(1024 * a, 1024 * (a + 1)), slice(64 * a, 64 * a + 64)
+    def anch(w, c0, c1, bank):
+        ext(EP, w, c0, c1, bank, c0 // 16, True, True)
 
-    def keep():
-        for a in range(3):
-            f = th(a)[0]
-            dma(T.Zb[2::8, f], T.BW[2::8, f], ["BW", "Zb"], (), ["Zb%d" % a])
+    def lst(p, c0, c1, bank):
+        cp(R(p, c0 // 16, c1 // 16), R(bank, c0 // 16, c1 // 16))
 
-    keep()
-    for b in ("SW1", "SW2"):
-        dma(T[b][:, V:ROOT], T.BW[:, V:ROOT], ["BW"], [b + "g"])
-    consts4()
+    def own3(h):
+        ext(ES, "W3", 1536 * h, 1536 * h + 1536, "ps%d" % (2 + h), 0, True, False)
 
-    def ext(X, src, bank, c0, c1, st, sp, rd):
-        for i in range(16):
-            mm(T[bank][:, c0:c1], T[X][:, sl(i)], T[src][:, 16 * c0 + i:16 * c1:16], st and i == 0, sp and i == 15, [X] + rd, (), [bank])
+    def g3(e, c0, c1):
+        (cp if e == "v" else act)(R("G3", c0, c1), IND(R("W3", 0, BWW), R("PL2", c0 // 16, c1 // 16)))
 
-    BWT = ["BW", "BWg", "BWr"]
-    S1T = ["SW10", "SW11", "SW12", "SW1g", "SW1r"]
-    S2T = ["SW20", "SW21", "SW22", "SW2g", "SW2r"]
-    DB = ["ps1", "ps3", "ps4"]
-    LV = {1: ("BW", BWT, "PL", "Zb", "SW1"), 2: ("SW1", S1T, "PL1", "Zs", "SW2")}
+    def e3(c0, c1, sp):
+        h = c0 // 1536
+        ext(ES, "G3", c0, c1, "ps%d" % (2 + h), c0 // 16 - 96 * h, False, sp)
 
-    def dbl(l, a):
-        w, wt, p, z, n = LV[l]
-        f, c = th(a)
-        tt(T[n][:, f], T[w][:, 0:BWW].indirect(T[p][:, c]), T[z][:, f], A.add, wt + [p, z, z + str(a)], [n + str(a)])
-        ext("XP", n, "ps0", 64 * a, 64 * a + 64, True, True, [n + str(a)])
-        if l == 1:
-            dma(T.Zs[2::8, f], T.SW1[2::8, f], ["SW1%d" % a, "Zs"], (), ["Zs%d" % a])
+    def date(h):
+        c = (96 * h, 96 * h + 96)
+        cp(R("DI", *c), R("ps%d" % (2 + h), 0, 96))
+        ts(R("DL", *c), R("DI", *c), 2047, A.bitwise_and)
+        cp(R("DU", *c), R("DL", *c))
 
-    def anchors(n):
-        cp(T[n][:], T.ps0[:, 0:192], ["ps0"], [n])
+    def beat_v(c0, c1):
+        tt(R("bits", c0, c1), IND(R("SWIN", 0, W), R("DU", c0 // 16, c1 // 16)), R("XW", c0, c1), A.is_le)
 
-    def L3a():
-        for a in range(3):
-            ext("XS", "SW2", DB[a], 64 * a, 64 * a + 64, True, False, S2T[:3])
-        for a in range(2):
-            f, c = th(a)
-            act(T.G2[:, f], T.SW2[:, 0:BWW].indirect(T.PL2[:, c]), S2T + ["PL2"], ["G2%d" % a])
+    def beat_g(c0, c1):
+        act(R("SG", c0, c1), IND(R("SWIN", 0, W), R("DU", c0 // 16, c1 // 16)))
 
-    def L3v():
-        f, c = th(2)
-        cp(T.G2[:, f], T.SW2[:, 0:BWW].indirect(T.PL2[:, c]), S2T + ["PL2"], ["G22"])
+    def beat_d(c0, c1, bank):
+        mm(R(bank, 0, c1 - c0), R("ID"), R("XW", c0, c1), True, False)
+        mm(R(bank, 0, c1 - c0), R("NI"), R("SG", c0, c1), False, True)
+        act(R("bits", c0, c1), R(bank, 0, c1 - c0), F.Sign, bias=TINY)
 
-    def L3e():
-        for a in range(3):
-            ext("XS", "G2", DB[a], 64 * a, 64 * a + 64, False, True, ["G2%d" % a])
-
-    def L3b():
-        for a in range(3):
-            cp(T.DI[:, th(a)[1]], T[DB[a]][:, th(a)[1]], [DB[a]], (), ["DI"])
-
-    def L3c():
-        ts(T.DL[:], T.DI[:], 2047, A.bitwise_and, ["DI"], ["DL"])
-        cp(T.DU[:], T.DL[:], ["DL"], ["DU"])
+    def beat_e(c0, c1, bank):
+        ext(E1, "bits", c0, c1, bank, c0 // 16, True, True)
 
     def beaten():
-        def counts(c0, c1, bt):
-            for c in range(c0, c1):
-                mm(T.ps2[:, 8 * c:8 * c + 8], T.bits[:, sl(c)], T.BD[:, 0::16], True, True, [bt, "BD"], (), ["ps2"])
+        beat_g(0, 384); beat_v(1152, 1536); beat_g(384, 768)
+        beat_d(0, 384, "ps4")
 
-        def vec(l, h, t):
-            tt(T.bits[:, l:h], T.SWIN[:, 0:W].indirect(T.DU[:, l // 16:h // 16]), T.XW[:, l:h], A.is_le, ["S", "DU", "XWx"], [t])
-            counts(l // 128, h // 128, t)
-
-        act(T.SG[:], T.SWIN[:, 0:W].indirect(T.DU[:, 160:192]), ["S", "DU"], ["SG"])
-        vec(0, 1024, "bits0")
-        mm(T.ps7[:, :], T.ID[:], T.XW[:, 2560:3072], True, False, ["ID", "XWx"], ["ps7"])
-        mm(T.ps7[:, :], T.NI[:], T.SG[:], False, True, ["NI", "SG"], (), ["ps7"])
-        act(T.bits[:, 2560:3072], T.ps7[:, :], ["ps7"], ["bits3"], f=F.Sign, bias=TINY)
-        vec(1024, 2048, "bits1")
-        counts(20, 24, "bits3")
-        vec(2048, 2560, "bits2")
-        ts(T.bT[:, 0:160], T.ps2[:, 0:160], 4.5, A.is_lt, ["ps2"], ["bT"])
-        ts(T.bT[:, 160:192], T.ps2[:, 160:192], -7.0, A.is_lt, ["ps2"], (), ["bT"])
+    def beaten2():
+        beat_v(1536, 2432)
+        beat_g(768, 1152)
+        beat_d(384, 768, "ps5")
+        beat_e(1152, 1536, "ps0")
+        beat_d(768, 1152, "ps4")
+        beat_v(2432, V)
+        beat_e(1536, 2432, "ps0")
+        beat_e(0, 1152, "ps1")
+        beat_e(2432, V, "ps0")
+        ts(R("fl", 0, 72), R("ps1", 0, 72), -7.0, A.is_lt)
+        ts(R("fl", 72, 192), R("ps0", 72, 192), 4.5, A.is_lt)
 
     def ghosts_a():
-        ts(T.dg2[:], T.DL[:], 31, A.bitwise_and, ["DL"], ["dg2"])
-        ts(T.dg1[:], T.DL[:], 5, A.arith_shift_right, ["DL"], ["dg1"])
-        cp(T.dlo[:], T.dg2[:], ["dg2"], ["dlo"])
-        cp(T.dh[:], T.dg1[:], ["dg1"], ["dh"])
-        dma(T.GW[10::16, :], T.dlo[:], ["dlo"], (), ["GW"])
-        dma(T.GW[2::16, :], T.dh[:], ["dh"], (), ["GW"])
+        ts(R("dg", 0, 192), R("DL", 0, 192), 5, A.arith_shift_right)
+        ts(R("dg", 192, 384), R("DL", 0, 192), 31, A.bitwise_and)
+
+    def ghosts_a2():
+        cp(R("dgb"), R("dg"))
+        dma(R("GW", rows=(2, 128, 16)), R("dgb", 0, 192))
+        dma(R("GW", rows=(10, 128, 16)), R("dgb", 192, 384))
 
     def ghosts_b(t):
-        act(T["GO%d" % t][:], T.GW[:].indirect(T.SL[:]), ["GW", "SL"], ["GO%d" % t])
+        act(R("GO%d" % t), IND(R("GW"), R("SL")))
         for d in range(1, N):
-            send(T["GL%d" % t][:, sl(d - 1)], T["GO%d" % t][:, sl(d - 1)], cores[(r + d) % N], "gh%d" % t, ["GO%d" % t])
+            c = (128 * (d - 1), 128 * d)
+            send(R("GL%d" % t, *c), R("GO%d" % t, *c), cores[(r + d) % N], "gh%d" % t)
         arrive("gh%d" % t, sum(len(engs(cores[(r - d) % N], core)) for d in range(1, N)), "GL%d" % t)
 
-    def ghosts_in(t):
-        for b in ("BW", "SW1", "SW2"):
-            dma(T[b][:, V:ROOT], T["GL%d" % t][:], ["GL%d" % t], [b + "g"])
+    def ghosts_in(t, bs):
+        for b in bs:
+            dma(R(b, V, ROOT, rows=(2, 128, 8)), R("GL%d" % t, rows=(2, 128, 8)))
 
-    NS = 7
-    vU = u_(4, 16)
-    DUm = lambda nj: u_(3, nj)
+    vU, DlU = u_(0), u_(1)
+
+    def count16(win, n, out):
+        tt(R("o1", 0, n), IND(win, R("REP", 0, n // 16)), R("KQ", 0, n), A.is_le)
+        scan(R("o2", 0, n), R("RST", 0, n), R("o1", 0, n))
+        cp(out, R("o2", 15, n, 16))
 
     def compact(t):
-        mm(T.ps3[:, 0:192], T.M1[:], T.bT[:], True, False, ["M1", "bT"], ["ps3"])
-        for c in range(8):
-            op("v", lambda q, c=c: q.tensor_tensor_scan(T.binc[:, c::8], T.ONE[:, c:192:8], T.bT[:, c::8], 0.0, A.mult, A.add),
-               ["ONE", "bT"], (), ["binc"])
-        mm(T.ps3[:, 0:192], T.ONE[:, 0:128], T.binc[:], False, True, ["ONE", "binc"], (), ["ps3"])
-        mm(T.ps4[:, 0:1], T.binc[:, 0:128], T.ONE[:, 0:1], True, True, ["binc", "ONE"], ["ps4"])
-        mm(T.ps4[0:64, 1:2], T.binc[:, 128:192], T.ONE[:, 0:1], True, True, ["binc", "ONE"], (), ["ps4"])
-        ts(T.posI[:], T.ps3[:, 0:192], 4095.0, A.add, ["ps3"], ["posI"])
-        ts(T.indA[:], T.krow[:], T.ps4[:, 0:1], A.is_ge, ["krow", "ps4"], ["indA"])
-        ts(T.loI[:], T.posI[:], 15, A.bitwise_and, ["posI"], ["loI"])
-        ts(T.hiI[:], T.posI[:], 4, A.arith_shift_right, ["posI"], ["hiI"])
-        ts(T.indB[0:64, :], T.krow[0:64, :], T.ps4[0:64, 1:2], A.is_ge, ["krow", "ps4"], ["indB"])
-        cp(T.lob[:], T.loI[:], ["loI"], ["lob"])
-        cp(T.hib[:], T.hiI[:], ["hiI"], ["hib"])
-        for i in range(16):
-            mm(T.ps6[:, 0:16], T.SA[:, sl(i)], T.indA[:, i::16], i == 0, False, ["SA", "indA"], (), ["ps6"])
-        for i in range(16):
-            mm(T.ps6[:, 0:16], T.SA[0:64, sl(i)], T.indB[0:64, i::16], False, i == 15, ["SA", "indB"], (), ["ps6"])
-        for i in range(NS):
-            act(T.sq[:], T.lob[:], ["lob"], ["sq"], f=F.Square, bias=-float(i))
-            act(T.OHL[:, i::16], T.sq[:], ["sq"], (), ["OHL"], f=F.Relu, scale=-1.0, bias=1.0)
-        for i in range(NS, 16):
-            ts(T.OHL[:, i::16], T.lob[:], float(i), A.is_equal, ["lob"], (), ["OHL"])
-        for i in range(16):
-            ts(T.OHH[:, i::16], T.hib[:], float(i), A.is_equal, ["hib", "c0"], (), ["OHH"], s2=col(0), op1=A.mult)
-        for c in range(24):
-            mm(T.ps5[:, 0:128], T.OHL[:, sl(c)], T.OHH[:, sl(c)], c == 0, c == 23, ["OHL", "OHH"], (), ["ps5"])
+        mm(R("ps3", 0, 192), R("M1g"), R("fl"), True, False)
+        scan(R("binc"), R("ONE"), R("fl"))
+        mm(R("ps2", 0, 16), R("BD"), R("binc", 11, 192, 12), True, True)
+        ext(E1, "binc", 0, 192, "ps2", 16, True, True, 0, 12, 12)
+        mm(R("ps3", 0, 192), R("BD"), R("binc"), False, True)
         if t < RO - 1:
             ghosts_a()
-        if t == 0:
-            consts5()
-        o = lambda a, b: T.ov[:, a:b]
-        tt(o(0, 128), T.ps5[:, 0:128], T.BD[:], A.mult, ["ps5", "BD"], ["ovm"])
-        tt(o(128, 192), o(0, 64), o(64, 128), A.add, ["ovm"], ["ov1"])
-        tt(o(192, 224), o(128, 160), o(160, 192), A.add, ["ov1"], ["ov2"])
-        tt(o(224, 240), o(192, 208), o(208, 224), A.add, ["ov2"], ["ov3"])
-        tt(T.vf[:], T.ps6[:, 0:16], o(224, 240), A.add, ["ps6", "ov3"], ["vf"])
-        cp(vU, T.vf[:], ["vf"], ["vU"])
+        cp(R("LW", 0, 32), R("ps2", 0, 32))
+        count16(R("LW", 0, 16), 256, u_(2))
+        mm(R("ps0", 0, 16), R("I12"), R("o2", 15, 256, 16), True, False)
+        tt(R("o3"), IND(R("LW", 16, 40), u_(2)), R("KL2"), A.is_le)
+        ext(E1, "o3", 0, 256, "ps0", 0, False, True)
+        ts(R("PF", 0, 192), R("ps3", 0, 192), 4095.0, A.add)
+        if t < RO - 1:
+            ghosts_a2()
+        cp(u_(3), R("ps0", 0, 16))
+        act(b_(0), R("ps0", 0, 16))
+        tt(R("OH"), IND(R("PF"), u_(3)), R("krow", 0, 256), A.is_equal)
+        mm(R("ps1", 0, 16), R("I16"), b_(0), True, False)
+        ext(EI, "OH", 0, 256, "ps1", 0, False, True)
+        tt(R("Ds"), IND(R("DL"), u_(3)), R("OH"), A.mult)
+        ext(E1, "Ds", 0, 256, "ps2", 0, True, True)
+        cp(vU, R("ps1", 0, 16))
+        act(R("xB", 0, 256), IND(R("XW"), vU))
+        cp(R("vf"), R("ps1", 0, 16))
+        act(R("xB", 256, 512), R("xB", 0, 256))
+        tt(f_(14), R("vf"), tr(1), A.subtract)
+        ts(f_(15), R("vf"), 3071.5, A.is_lt)
+        cp(DlU, R("ps2", 0, 16))
 
-    def own_data():
-        act(T.G2g[:], T.G2[:].indirect(vU), ["G20", "G21", "G22", "G2p", "vU", "c15"], ["G2g"], f=F.Identity, bias=col(15))
-        cp(T.xB[:], T.XW[:].indirect(vU), ["XWx", "XWp", "vU"], ["xB"])
-        tt(T.Dg[:], T.SW2[:, 0:BWW].indirect(vU), T.G2g[:], A.add, S2T + ["G2g", "vU"], ["Dg"])
+    def turn(D, nj, TBn):
+        cp(R("CG", 0, 16 * nj), IND(R("CT"), D))
+        for b in range(nj // 2):
+            op("v", lambda q, b=b: q.transpose(T[TBn][:, :, b], T.CG[:, 32 * b:32 * b + 32]), (None, [(TBn, b, 1 << 20, 64, ALL)]),
+               [R("CG", 32 * b, 32 * b + 32)])
 
-    def spread(x, xt, XX, n, ks, e):
-        for k in ks:
-            if e == "v":
-                cp(T[XX][:, k:16 * n:16], x, [xt], (), [XX])
-            else:
-                act(T[XX][:, k:16 * n:16], x, [xt], (), [XX])
+    def days(nj, TBn, bank, k0, k1, st, sp):
+        n = (k1 - k0) * nj
+        lo, hi = R3(TBn, T[TBn][:, k0:k1, :]), R3(TBn, T[TBn][:, 16 + k0:16 + k1, :])
+        mm(R(bank, 0, n, 2), R("IeP", 16, 144), lo, st, False)
+        mm(R(bank, 0, n, 2), R("IeP", 0, 128), hi, False, st)
+        mm(R(bank, 1, n, 2), R("IoP", 32, 160), lo, st, False)
+        mm(R(bank, 1, n, 2), R("IoP", 16, 144), hi, False, st or sp)
 
-    LB = {16: "ps6", 6: "ps4"}
-
-    def choose_a(Dg, dt_, nj):
-        for i in range(16):
-            mm(T[LB[nj]][:, 0:nj], T.XS[:, sl(i)], Dg[:, i::16], i == 0, i == 15, ["XS", dt_], (), [LB[nj]])
-        mm(T.ps7[:, 0:16 * nj], T.CB[:], Dg, True, False, ["CB", dt_], ["ps7"])
-
-    def choose_b(nj):
+    def cmp_v(x, nj, k):
         n = 16 * nj
-        ts(n_(4, nj), T[LB[nj]][:, 0:nj], 8064.0, A.add, [LB[nj]], ["di"])
-        ts(n_(5, nj), n_(4, nj), 2047, A.bitwise_and, ["di"], ["dm"])
-        cp(DUm(nj), n_(5, nj), ["dm"], ["DUm"])
-        cp(T.wkg[:, 0:n], T.WK[:].indirect(DUm(nj)), ["WK", "DUm"], ["wkg"])
-        mm(T.ps7[:, 0:n], T.I7[:], T.wkg[:, 0:n], False, True, ["I7", "wkg"], (), ["ps7"])
+        tt(R("bits", n * k, n * k + 2 * n), IND(R("SWIN", 0, W), R("cu", nj * k, nj * k + 2 * nj)), x, A.is_lt)
 
-    def choose_c(nj):
-        n = 16 * nj
-        ts(T.ci[:, 0:n], T.ps7[:, 0:n], 8064.0, A.add, ["ps7"], ["ci"])
-        ts(T.cm[:, 0:n], T.ci[:, 0:n], 2047, A.bitwise_and, ["ci"], ["cm"])
-        cp(T.cu[:, 0:n], T.cm[:, 0:n], ["cm"], ["cu"])
+    def choose(t):
+        turn(DlU, 16, "TB")
+        days(16, "TB", "ps3", 0, 16, True, True)
+        cp(R("Dw", 0, 16), R("ps2", 0, 16))
+        cp(R("cu"), R("ps3", 0, 256))
+        for h in range(2):
+            mm(R("ps%d" % h, 0, 128), R("ID"), R("KC", 128 * h, 128 * h + 128), True, False)
+            days(16, "TB", "ps%d" % h, 8 * h, 8 * h + 8, False, False)
+        x = R("xB", 0, 512)
 
-    def choose_d(XX, nj, parts):
-        n = 16 * nj
-        mm(T.ps2[:, 0:n], T.ID[:], T.KC[:, 0:n], True, False, ["ID", "KC"], ["ps2"])
-        for j0, j1 in parts:
-            for j in range(j0, j1):
-                tt(T.B2[:, j, :], T.SWIN[:, 0:W].indirect(T.cu[:, 16 * j:16 * j + 16]), T[XX][:, 256 * j:256 * j + 256], A.is_lt,
-                   ["S", "cu", XX], ["B2%d" % j])
-            for i in range(16):
-                mm(T.ps2[:, 16 * j0:16 * j1], T.XE[:, sl(i)], T.B2[:, j0:j1, 16 * i:16 * i + 16], False, False,
-                   ["XE"] + ["B2%d" % j for j in range(j0, j1)], (), ["ps2"])
-        cp(T.ctc[:, 0:nj, 0:16], T.cm[:, 0:n], ["cm"], (), ["ctc"])
-        cp(T.ctc[:, 0:nj, 16:32], T.cm[:, 0:n], ["cm"], (), ["ctc"])
-        op("v", lambda q: q.transpose(T.ctt[:, 0:nj, :], T.ctc[:, 0:nj, :]), ["ctc"], ["ctt"])
-        mm(T.ps2[:, 0:n], T.Ie[:], T.ctt[:, 0:nj, 0:16], False, False, ["Ie", "ctt"], (), ["ps2"])
-        mm(T.ps2[:, 0:n], T.Io[:], T.ctt[:, 0:nj, 16:32], False, True, ["Io", "ctt"], (), ["ps2"])
+        def sg(a):
+            act(R("SG", 512 * a, 512 * a + 512), IND(R("SWIN", 0, W), R("cu", 160 + 32 * a, 192 + 32 * a)))
 
-    def choose_e(nj):
-        n = 16 * nj
-        K = T.key
-        cp(K[:, 0:n], T.ps2[:, 0:n], ["ps2"], ["key0"])
-        tt(K[:, 256:256 + n // 2], K[:, 0:n:2], K[:, 1:n:2], A.max, ["key0"], ["key1"])
-        tt(K[:, 384:384 + n // 4], K[:, 256:256 + n // 2:2], K[:, 257:256 + n // 2:2], A.max, ["key1"], ["key2"])
-        tt(K[:, 448:448 + n // 8], K[:, 384:384 + n // 4:2], K[:, 385:384 + n // 4:2], A.max, ["key2"], ["key3"])
-        tt(K[:, 480:480 + nj], K[:, 448:448 + n // 8:2], K[:, 449:448 + n // 8:2], A.max, ["key3"], ["kmax"])
+        def sd(a):
+            p = R("ps%d" % (4 + a))
+            mm(p, R("ID"), x, True, False)
+            mm(p, R("NI"), R("SG", 512 * a, 512 * a + 512), False, True)
+            act(R("bits", 2560 + 512 * a, 3072 + 512 * a), p, F.Sign, bias=-TINY)
 
-    def moved(t, nj):
-        km = T.key[:, 480:480 + nj]
-        ts(f_(0, nj), km, T.thr[:, t:t + 1], A.is_ge, ["kmax", "thr%d" % t], ["mv"])
-        ts(n_(0, nj), km, 2047, A.bitwise_and, ["kmax"], ["c1i"])
+        sg(0); cmp_v(x, 16, 8); sg(1); sd(0); cmp_v(x, 16, 0)
+        ext(EC, "bits", 2048, 2560, "ps1", 0, False, False)
+        sg(2); sd(1); cmp_v(x, 16, 2); cmp_v(x, 16, 4)
+        ext(EC, "bits", 0, 1024, "ps0", 0, False, False)
+        sd(2)
+        ext(EH, "bits", 2560, 3584, "ps1", 32, False, False)
+        cmp_v(x, 16, 6)
+        ext(EH, "bits", 3584, 4096, "ps1", 96, False, True)
+        ext(EC, "bits", 1024, 2048, "ps0", 64, False, True)
+        act(R("key", 0, 128), R("ps1", 0, 128))
+        tt(R("key", 128, 256), R("ps0", 0, 128), R("key", 0, 128), A.max)
+        tt(R("key", 0, 64), R("key", 128, 192), R("key", 192, 256), A.max)
+        tt(R("key", 64, 96), R("key", 0, 32), R("key", 32, 64), A.max)
+        tt(n_(5), R("key", 64, 80), R("key", 80, 96), A.max)
 
-    def early():
-        tt(f_(14, 16), T.vf[:], tr(1, 16), A.subtract, ["vf", "trP"], ["vt"])
-        ts(f_(15, 16), T.vf[:], 3071.5, A.is_lt, ["vf"], ["val"])
+    def moved(t, nj, k, m, c):
+        ts(m, k, R("thr", t, t + 1), A.is_ge)
+        ts(c, k, 2047, A.bitwise_and)
+
+    mv, mg = b_(1), b_(2, 6)
 
     def move_list():
-        km = T.key[:, 480:496]
-        ts(n_(3, 16), km, 31, A.bitwise_and, ["kmax"], ["c4i"])
-        ts(n_(2, 16), km, 5, A.arith_shift_right, ["kmax"], ["c3i"], s2=63, op1=A.bitwise_and)
-        cp(b_(1, 16), n_(3, 16), ["c4i"], ["lb"])
-        cp(b_(0, 16), n_(2, 16), ["c3i"], ["hb"])
+        ts(n_(2), n_(5), 5, A.arith_shift_right, 63, A.bitwise_and)
+        ts(n_(3), n_(5), 31, A.bitwise_and)
+        cp(R("smb", 48, 80), R("smi", 32, 64))
         for i in range(16):
-            mm(T.ps3[:, i:256:16], T.XLh[:, sl(i)], b_(0, 16), True, False, ["XLh", "hb"], (), ["ps3"])
-            mm(T.ps3[:, i:256:16], T.XLl[:, sl(i)], b_(1, 16), False, True, ["XLl", "lb"], (), ["ps3"])
-        act(T.RD[:], T.ps3[:, 0:256], ["ps3", "c5"], ["RD"], f=F.Identity, bias=col(5))
-        tt(f_(2, 16), f_(0, 16), f_(14, 16), A.mult, ["mv", "vt"], ["m1"])
-        tt(u_(0, 16), f_(2, 16), tr(1, 16), A.add, ["m1", "trP"], ["voff"])
+            mm(R("ps2", i, 256, 16), R("XLh", 128 * i, 128 * i + 128), b_(3), True, False)
+            mm(R("ps2", i, 256, 16), R("XLl", 128 * i, 128 * i + 128), b_(4), False, True)
+        act(R("RD"), R("ps2", 0, 256), F.Identity, bias=col(5))
 
-    def move_put(last):
-        cp(T.BW[:, 0:4240].indirect(u_(0, 16)), T.RD[:], ["RD", "voff"], BWT)
-        if not last:
-            keep()
+    def move_off():
+        tt(f_(2), mv, f_(14), A.mult)
+        tt(u_(4), f_(2), tr(1), A.add)
+
+    def move_put():
+        cp(IND(R("BW"), u_(4)), R("RD"))
 
     def refuse_a():
-        tt(b_(2, 16), f_(15, 16), f_(0, 16), A.subtract, ["val", "mv"], ["rf"])
-        op("v", lambda q: q.tensor_tensor_scan(b_(3, 16), T.ONE[:, 0:16], b_(2, 16), 0.0, A.mult, A.add), ["ONE", "rf"], ["finc"])
-        mm(T.ps4[:, 0:16], T.M1g[:], b_(2, 16), True, False, ["M1g", "rf"], ["ps4"])
-        mm(T.ps4[:, 0:16], T.BD[:], b_(3, 16), False, True, ["BD", "finc"], (), ["ps4"])
+        tt(b_(5), f_(15), mv, A.subtract)
+        scan(b_(6), R("ONE", 0, 16), b_(5))
+        mm(R("ps4", 0, 16), R("BD"), b_(6), True, True)
+        mm(R("ps4", 16, 32), R("M1g"), b_(5), True, False)
+        mm(R("ps4", 16, 32), R("BD"), b_(6), False, True)
 
     def refuse_b():
-        ts(f_(3, 16), T.ps4[:, 0:16], 4095.0, A.add, ["ps4"], ["rq"])
-        ts(f_(4, 16), f_(3, 16), 95.5, A.is_lt, ["rq"], ["rs"])
-        tt(f_(5, 16), f_(3, 16), tr(3, 16), A.subtract, ["rq", "trR"], ["rt"])
-        tt(f_(6, 16), f_(4, 16), f_(5, 16), A.mult, ["rs", "rt"], ["rr"])
-        tt(u_(1, 16), f_(6, 16), tr(3, 16), A.add, ["rr", "trR"], ["roff"])
+        tt(R("GN", 0, 32), R("ps4", 0, 32), R("C32"), A.add)
+        count16(R("GN", 0, 16), Q, u_(5, 6))
+        mm(R("ps4", 0, 6), R("I16"), R("o2", 15, Q, 16), True, False)
+        tt(R("OH", 0, Q), IND(R("GN", 16, 40), u_(5, 6)), R("krow", 0, Q), A.is_equal)
+        tt(R("Ds", 0, Q), IND(R("Dw"), u_(5, 6)), R("OH", 0, Q), A.mult)
+        ext(EI, "OH", 0, Q, "ps4", 0, False, True)
+        ext(E1, "Ds", 0, Q, "ps5", 0, True, True)
 
     def refuse_c(t):
-        G = T["GS%d" % t]
-        ga, gb = "GSa%d" % t, "GSb%d" % t
-        cp(G[:, 0:448].indirect(u_(1, 16)), T.xB[:], ["xB", "roff"], [ga, gb])
-        cp(G[:, 96:544].indirect(u_(1, 16)), T.Dg[:], ["Dg", "roff", ga], [gb])
         dst, src = cores[(r + 1 + t % (N - 1)) % N], cores[(r - 1 - t % (N - 1)) % N]
-        send(T["GX%d" % t][:], G[:, 0:192], dst, "gu%d" % t, [ga, gb])
+        cp(u_(6, 6), R("ps4", 0, 6))
+        cp(R("GE%d" % t, 0, 6), R("ps5", 0, 6))
+        send(R("GD%d" % t), R("GE%d" % t), dst, "gd%d" % t)
+        arrive("gd%d" % t, len(engs(src, core)), "GD%d" % t)
+
+    def refuse_d(t):
+        dst, src = cores[(r + 1 + t % (N - 1)) % N], cores[(r - 1 - t % (N - 1)) % N]
+        G = "GS%d" % t
+        act(R(G, 0, Q), IND(R("xB", 256, 528), u_(6, 6)))
+        act(R(G, Q, 2 * Q), R(G, 0, Q))
+        send(R("GX%d" % t), R(G), dst, "gu%d" % t)
         arrive("gu%d" % t, len(engs(src, core)), "GX%d" % t)
 
     def parity_a():
-        op("v", lambda q: q.tensor_reduce(f_(7, 1), f_(0, 16), AxisListType.X, A.add), ["mv"], ["mr"])
-        cp(b_(4, 1), f_(7, 1), ["mr"], ["mrb"])
-        mm(T.ps4[:, 16:17], T.ONE[:, 0:128], b_(4, 1), True, True, ["ONE", "mrb"], (), ["ps4"])
+        mm(R("ps7", 0, 16), R("ONE", 0, 128), mv, True, True)
+        act(f_(6), R("ps7", 0, 16), accum_out=f_(7, 1))
 
     def parity_b(t):
-        cp(n_(1, 1), T.ps4[:, 16:17], ["ps4"], ["pi"])
-        ts(n_(1, 1), n_(1, 1), 1, A.bitwise_and, ["pi"], ["pi"])
-        ts(T.thr[:, t + 1:t + 2], n_(1, 1), SC, A.mult, ["pi"], ["thr%d" % (t + 1)], s2=9 * SC, op1=A.add)
+        cp(n_(1, 1), f_(7, 1))
+        ts(n_(1, 1), n_(1, 1), 1, A.bitwise_and)
+        ts(R("thr", t + 1, t + 2), n_(1, 1), SC, A.mult, 9 * SC, A.add)
 
-    def dedup_a(nj):
-        ts(f_(8, nj), n_(0, nj), 1.0, A.add, ["c1i"], ["cp1"])
-        tt(f_(10, nj), n_(0, nj), tr(2, nj), A.subtract, ["c1i", "trS"], ["ct2"])
-        tt(f_(9, nj), f_(8, nj), f_(0, nj), A.mult, ["cp1", "mv"], ["cmf"])
-        cp(T.cmh[:, 0:nj], f_(9, nj), ["cmf"], ["cmh"])
-        for i in range(16):
-            mm(T.ps5[:, i:16 * nj:16], T.XA[:, sl(i)], T.cmh[:, 0:nj], True, True, ["XA", "cmh"], (), ["ps5"])
-
-    def dedup_b(nj):
+    def dedup_a(nj, m, c, MK):
         n = 16 * nj
-        cp(T.cR[:, 0:n], T.ps5[:, 0:n], ["ps5"], ["cR"])
-        mm(T.ps5[:, 0:n], T.BD[:], T.ZER[:, 0:n], True, False, ["BD", "ZER"], ["ps5"])
-        for j in range(nj):
-            ts(T.DE[:, j, 0:n - 16 * j], T.cR[:, 16 * j:n], T.sml[:, 144 + j:145 + j], A.is_equal, ["cR", "cmf"], ["DE%d" % j])
-            if j < nj - 1:
-                mm(T.ps5[:, 16 * (j + 1):n], T.BD[:], T.DE[:, j, 16:n - 16 * j], False, False, ["BD", "DE%d" % j], (), ["ps5"])
-        tt(T.DMb[:, 0:nj, :], T.DE[:, 0:nj, 0:16], T.MK[:, 0:nj, :], A.mult, ["DE%d" % j for j in range(nj)] + ["MK"], ["DMb"])
-        mm(T.ps5[:, 0:n], T.BD[:], T.DMb[:, 0:nj, :], False, True, ["BD", "DMb"], (), ["ps5"])
-
-    def dedup_c(nj):
-        n = 16 * nj
-        cp(T.dupR[:, 0:n], T.ps5[:, 0:n], ["ps5"], ["dupR"])
+        ts(f_(8, nj), c, 1.0, A.add)
+        tt(f_(10, nj), c, tr(2, nj), A.subtract)
+        tt(R("cmh", 0, nj), f_(8, nj), m, A.mult)
+        tt(R("cmw", 0, nj), f_(8, nj), m, A.mult)
+        mm(R("ps6", 0, 2 * n), R("ID"), R(MK), True, False)
         for i in range(16):
-            mm(T.ps6[:, 16:16 + nj], T.XE[:, sl(i)], T.dupR[:, i:n:16], i == 0, i == 15, ["XE", "dupR"], (), ["ps6"])
+            for h in range(2):
+                mm(R("ps6", n * h + i, n * h + n, 16), R("XA", 128 * i, 128 * i + 128), R("cmh", 0, nj), False, i == 15 and h == 1)
 
-    def dedup_d(nj, x, xt):
-        ts(f_(11, nj), T.ps6[:, 16:16 + nj], 0.5, A.is_lt, ["ps6"], ["nd"])
-        tt(f_(12, nj), f_(11, nj), f_(0, nj), A.mult, ["nd", "mv"], ["fm"])
-        tt(f_(13, nj), f_(12, nj), f_(10, nj), A.mult, ["fm", "ct2"], ["fq"])
-        tt(u_(2, nj), f_(13, nj), tr(2, nj), A.add, ["fq", "trS"], ["soff"])
-        cp(T.SWIN[:, 0:2304].indirect(u_(2, nj)), x, [xt, "soff"], ["S"])
+    def dedup_s(nj):
+        act(R("rowS", 0, 32 * nj), R("ps6", 0, 32 * nj))
+
+    def dedup_b(nj, m, RJ):
+        n = 16 * nj
+        tt(R("dd", 0, 2 * n), IND(R("cmw", 0, nj), R(RJ)), R("rowS", 0, 2 * n), A.is_equal)
+        scan(R("de", 0, 2 * n), R("RS32", 0, 2 * n), R("dd", 0, 2 * n))
+        a = m[1][0][1]
+        for h in range(2):
+            tt(R("sml", 192 + h, 192 + nj, 2), R("de", n * h + 31, n * h + n, 32), R("smb", a + h, a + nj, 2), A.is_lt)
+        tt(f_(13, nj), f_(12, nj), f_(10, nj), A.mult)
+        tt(u_(7, nj), f_(13, nj), tr(2, nj), A.add)
+
+    def dedup_c(x, bs):
+        for b in bs:
+            cp(IND(R("SWIN"), R("smu", 112 + 2 * b, 114 + 2 * b)), R(x, 32 * b, 32 * b + 32))
+
+    def guest_a(t):
+        turn(R("GD%d" % t, 0, 6), 6, "TBg")
+        days(6, "TBg", "ps7", 0, 16, True, True)
+
+    def guest_b():
+        cp(R("cu", 0, Q), R("ps7", 0, Q))
+        mm(R("ps7", 0, Q), R("ID"), R("KCg"), True, False)
+        days(6, "TBg", "ps7", 0, 16, False, False)
+
+    def guest_c(t, ks):
+        for k in ks:
+            cmp_v(R("GX%d" % t), 6, k)
+            if k % 8 == 6:
+                ext(EC, "bits", Q * (k - 6), Q * (k + 2), "ps7", 6 * (k - 6), False, k == 14)
+
+    def guest_d(t):
+        cp(R("key", 0, 48), R("ps7", 48, 96))
+        tt(R("key", 48, 96), R("ps7", 0, 48), R("key", 0, 48), A.max)
+        tt(R("key", 0, 24), R("key", 48, 72), R("key", 72, 96), A.max)
+        tt(R("key", 24, 36), R("key", 0, 12), R("key", 12, 24), A.max)
+        tt(n_(4, 6), R("key", 24, 30), R("key", 30, 36), A.max)
+        moved(t, 6, n_(4, 6), mg, n_(0, 6))
+        dedup_a(6, mg, n_(0, 6), "MKg")
 
     for t in range(RO):
         last = t == RO - 1
-        if t:
-            gx, gt = T["GX%d" % (t - 1)], "GX%d" % (t - 1)
-            ghosts_in(t - 1)
-            ext("XP", "BW", "ps0", 0, 192, True, True, ["BW"])
-            dedup_b(16)
-            anchors("PL")
-        dbl(1, 0)
-        if t:
-            dedup_c(16)
-        dbl(1, 1); dbl(1, 2)
-        if t:
-            dedup_d(16, T.xB[:], "xB")
-        anchors("PL1")
-        if t:
-            spread(gx[:, 0:96], gt, "XXg", Q, range(16), "s")
-            choose_a(gx[:, 96:192], gt, 6)
-        dbl(2, 0)
+        a1, a2 = CUT[min(t, 1)]
+        b1, b2 = CUT3[min(t, 1)]
+        m1, m2 = (a1 + V) // 32 * 16, (a2 + V) // 32 * 16
         if t == 0:
-            fill("SA", "BA", [], 1.0)
+            addends(1, m1)
+            for b in ("W2", "W3"):
+                dma(R(b, V, ROOT), R("BW", V, ROOT))
+            dbl_v(1, a1, m1, False)
+            dbl_s(1, 0, a1, "ps0")
+            anch("W2", a1, m1, "ps0")
+            consts2()
+            dbl_v(1, m1, V)
+            anch("W2", 0, a1, "ps0")
+            candidates(1)
         else:
-            choose_b(6)
-        dbl(2, 1); dbl(2, 2)
+            addends(1, a1)
+            ghosts_in(t - 1, ["W2", "W3"])
+            dbl_s(1, 0, a1 // 32 * 16, "ps0")
+            refuse_d(t - 1)
+            dedup_s(16)
+            dbl_s(1, a1 // 32 * 16, a1, "ps0")
+            parity_b(t - 1)
+            dedup_b(16, mv, "RJ")
+            dbl_v(1, a1, m1)
+            anch("W2", a1, m1, "ps0")
+            dedup_c("xB", (7, 6, 5, 4))
+            anch("W2", 0, a1, "ps0")
+            dbl_v(1, m1, V)
+        anch("W2", m1, V, "ps1")
+        addends(2, a2, m1)
+        addends(2, m1)
+        lst("PL1", 0, m1, "ps0")
+        dbl_s(2, 0, a2, "ps0")
         if t:
-            choose_c(6)
-        anchors("PL2")
-        L3a()
+            guest_a(t - 1)
+        dbl_v(2, a2, m2)
+        lst("PL1", m1, V, "ps1")
+        anch("W3", a2, m2, "ps0")
         if t == 0:
             consts3()
-            fill("XE", "BG", [], SC)
-            L3v()
         else:
-            choose_d("XXg", 6, [(0, 6)])
-            L3v()
-            choose_e(6); moved(t - 1, 6); dedup_a(6)
-        L3e()
-        if t:
-            dedup_b(6)
-        L3b()
-        if t:
-            dedup_c(6)
-        L3c()
-        if t:
-            dedup_d(6, gx[:, 0:96], gt)
+            guest_b()
+            dedup_c("xB", (3, 2, 1, 0))
+        anch("W3", 0, a2, "ps0")
+        dbl_v(2, m2, V)
+        anch("W3", m2, V, "ps1")
+        if t == 0:
+            candidates(2)
+        lst("PL2", 0, m2, "ps0")
+        g3("s", 0, b1)
+        own3(0); own3(1)
+        if t == 0:
+            g3("v", b1, 1536)
+            lst("PL2", m2, V, "ps1")
+            g3("s", 1536, b2)
+            e3(0, 1536, True)
+            g3("v", b2, V)
+            date(0)
+            e3(1536, V, True)
+            consts4()
+            consts5()
+        else:
+            guest_c(t - 1, (0, 2))
+            lst("PL2", m2, V, "ps1")
+            g3("s", 1536, b2)
+            guest_c(t - 1, range(4, 16, 2))
+            g3("v", b1, 1536)
+            guest_d(t - 1)
+            e3(0, 1536, True)
+            dedup_s(6)
+            g3("v", b2, V)
+            e3(1536, V, True)
+            dedup_b(6, mg, "RJg")
+            date(0)
+            dedup_c("GX%d" % (t - 1), (2, 1, 0))
         beaten()
+        date(1)
+        beaten2()
+        if t == 0:
+            candidates(3)
         compact(t)
-        own_data()
-        spread(T.xB[:], "xB", "XX", 256, range(0, 9), "s")
-        choose_a(T.Dg[:], "Dg", 16)
-        spread(T.xB[:], "xB", "XX", 256, range(9, 16), "v")
-        early()
-        choose_b(16)
         if not last:
             ghosts_b(t)
-        choose_c(16)
-        choose_d("XX", 16, [(0, 4), (4, 8), (8, 12), (12, 16)])
-        choose_e(16)
-        moved(t, 16)
-        refuse_a()
+        choose(t)
         if last:
-            dedup_a(16)
-            refuse_b(); refuse_c(t)
+            moved(t, 16, n_(5), mv, n_(0))
+            refuse_a()
+            dedup_a(16, mv, n_(0), "MK") if False else None
         else:
             move_list()
-            refuse_b()
-            dedup_a(16)
+            if t == 0:
+                consts6()
+            moved(t, 16, n_(5), mv, n_(0))
+            move_off()
+            ghosts_in(t, ["BW"])
+            refuse_a()
+            dedup_a(16, mv, n_(0), "MK")
+            move_put()
+            anch("BW", 0, CUT[1][0] // 32 * 16, "ps0")
+            anch("BW", CUT[1][0] // 32 * 16, V, "ps1")
             parity_a()
+            lst("PL", 0, CUT[1][0] // 32 * 16, "ps0")
+            refuse_b()
+            lst("PL", CUT[1][0] // 32 * 16, V, "ps1")
             refuse_c(t)
-            move_put(False)
-            parity_b(t)
-    gx, gt = T.GX2, "GX2"
-    dedup_b(16); dedup_c(16)
-    choose_a(gx[:, 96:192], gt, 6)
-    spread(gx[:, 0:96], gt, "XXg", Q, range(16), "s")
-    dedup_d(16, T.xB[:], "xB")
-    choose_b(6); choose_c(6)
+    dedup_a(16, mv, n_(0), "MK")
+    refuse_b()
+    dedup_s(16)
+    refuse_c(2); refuse_d(2)
+    dedup_b(16, mv, "RJ")
     move_list()
-    choose_d("XXg", 6, [(0, 6)])
-    move_put(True)
-    choose_e(6); moved(2, 6); dedup_a(6)
+    dedup_c("xB", range(7, -1, -1))
+    guest_a(2)
+    move_off()
+    guest_b()
+    move_put()
+    guest_c(2, range(0, 16, 2))
 
     def outs(b):
-        p = ["ps0", "ps1", "ps3"][b % 3]
-        mm(T[p][0:40, :], T.OC[:], T.BW[:, 512 * b:512 * b + 512], True, True, ["OC", "BW"], [p])
-        act(T.OUT[:, 512 * b:512 * b + 512], T[p][0:40, :], [p], (), ["OUT"])
+        p = R(["ps0", "ps1", "ps3"][b % 3], rows=(0, 40))
+        mm(p, R("OC"), R("BW", 512 * b, 512 * b + 512), True, True)
+        act(R("OUT", 512 * b, 512 * b + 512), p)
 
-    dedup_b(6)
-    for b in range(2):
+    for b in range(4):
         outs(b)
-    dedup_c(6); dedup_d(6, gx[:, 0:96], gt)
-    for b in range(2, 6):
+    guest_d(2)
+    dedup_s(6)
+    for b in range(4, 6):
         outs(b)
-    dma(T.yan[:], T.OUT[0:8, :], ["OUT"])
-    dma(T.yof[:], T.OUT[32:40, :], ["OUT"])
-    dma(T.ys[:], T.SWIN[:, 0:W], ["S"])
+    dedup_b(6, mg, "RJg")
+    dma(hbm("yan"), R("OUT", rows=(0, 8)))
+    dma(hbm("yof"), R("OUT", rows=(32, 40)))
+    dedup_c("GX2", (2, 1, 0))
+    dma(hbm("ys"), R("SWIN", 0, W))
     for s in total:
         g.wait_ge(T.sem[s], total[s])

@@ -5,6 +5,7 @@ ROOT, BWW = 3968, 3984
 NEG = -4194304.0
 BIG = 1048576.0
 SC = 32768.0
+STAY = 8192.0
 TINY = 2.0 ** -120
 bf, f3, i3, u1, fh = "bfloat16", "float32", "int32", "uint16", "float16"
 SCRATCH = {}
@@ -15,24 +16,33 @@ def _sb(dt_, **kw):
         SCRATCH[n] = ("sbuf", [128] + (w if isinstance(w, list) else [w]), dt_)
 
 
-_sb(i3, anL=192, ofL=248, snL=56, tI=496, DI=192, DL=208, dg=384, smi=96, cpi=8, crow=160, crq=128, crg=128, kri=256, j16=16,
+_sb(i3, anL=192, ofL=248, snL=56, tI=496, DI=192, DL=208, dg=384, smi=128, cpi=8, crow=160, crq=128, crg=128, kri=512, j16=16,
     Dw=24)
-_sb(bf, pl=992, XR=3968, XW=3088, SWIN=2304, WK=2048, BW=4240, W2=BWW, W3=BWW, G3=V, GW=V, Z1=V, Z2=V, dgb=384, bits=4096,
-    SG=1536, fl=192, binc=192, o1=256, o2=256, o3=256, OH=256, xB=528, smb=128, RD=256, EE=1008, XA=2048, XLh=2048, XLl=2048,
-    ZR=2048, BD=128, BDt=128, M1g=128, ID=128, NI=128, I7=128, I12=128, I16=128, IK=128, IeP=160, IoP=160, ONE=192, OC=40,
-    krow=512, kst=512, KQ=256, KL2=256, RST=256, RS32=512, KC=256, KCg=96, MK=512, MKg=192, sg=1024, dd=512, de=512,
+_sb(bf, pl=992, XR=3968, XW=3088, SWIN=2304, WK=2048, BW=4240, W2=BWW, W3=BWW, G3=V, Z1=V, Z2=V, dgb=384, bits=5632,
+    SG=2624, fl=192, binc=192, o1=352, o2=352, o3=256, OH=352, xB=528, smb=128, RD=256, EE=864, XA=2048, XLh=2048, XLl=2048,
+    BD=128, BDt=128, M1g=128, ID=128, NI=128, I7=128, I12=128, I16=128, IK=128, IO=128, IeP=160, IoP=160, ONE=192, OC=40,
+    krow=256, KQ=256, KL2=256, RST=256, RS32=512, KC=256, KCg=192, MK=512, MKg=192, sg=1024, dd=704, de=704,
     GL0=NG, GL1=NG, GO0=NG, GO1=NG, GS0=192, GS1=192, GS2=192, GX0=192, GX1=192, GX2=192)
-_sb(f3, vf=16, sml=256, thr=4, ccol=32, BG=8, tr=48, CT=2048, PF=200, LW=40, GN=40, C32=32, key=256, cmw=16, rowS=512)
-_sb(u1, SL=56, PL=192, PL1=192, PL2=192, DU=192, cu=256, smu=128, REP=16, RJ=32, RJg=12, GD0=8, GD1=8, GD2=8, GE0=8, GE1=8, GE2=8)
-_sb(fh, CG=256, TB=[32, 8], TBg=[32, 3], Ds=256, cmh=16)
+_sb(f3, vf=16, sml=256, thr=4, ccol=32, BG=8, tr=48, CT=2048, PF=200, LW=40, GN=40, C32=32, key=352, cmw=32)
+_sb(u1, SL=56, PL=192, PL1=192, PL2=192, DU=192, cu=352, smu=160, REP=16, GD0=8, GD1=8, GD2=8, GE=24)
+_sb(fh, CG=352, TB=[32, 8], TBg=[32, 3], Ds=352, cmh=64, kr5=512)
 SCRATCH["OUT"] = ("sbuf", [40, V], f3)
 for _b in range(8):
     SCRATCH["ps%d" % _b] = ("psum", [128, 512], f3)
 SEMAPHORES = ["sv", "ss", "sp", "sg", "loc", "gh0", "gh1", "gu0", "gu1", "gu2", "gd0", "gd1", "gd2"] + ["d%d" % k for k in range(90)]
 ALL = (1 << 128) - 1
 
-CUT = {0: (1152, 1152), 1: (1792, 1792)}
-CUT3 = {0: (768, 2304), 1: (1152, 2688)}
+CUT = {"first": [[("S", 896, 0), ("V", 1792, 0), ("a", 2560, 1), ("p", V, 1)], [("S", 896, 0), ("a", 1792, 0), ("a", 2560, 1), ("p", V, 1)],
+                 [("s", 768, 2), ("v", 1536, 2), ("v", 2304, 3), ("s", V, 3)]],
+       "later": [[("S", 1280, 0), ("a", 1920, 0), ("a", 2560, 1), ("p", V, 1)], [("S", 1280, 0), ("a", 1920, 0), ("a", 2560, 1), ("p", V, 1)],
+                 [("s", 1024, 2), ("v", 2048, 2), ("s", V, 3)]],
+       "beat": (384, 2560)}
+GUEST = (12, 10)
+CYCLE, GATHER, SCATTER, PE = 0.001, 1.56, 3.8, 0.0005
+FIXED = {"v": 0.05, "s": 0.065, "g": 0.15, "y": 0.05}
+WAKE, DMA, ISSUE, REMOTE = 0.06, 1.4, 0.6, 2.5
+URGE = 2.0
+PASSES, ORDER = 24, {}
 
 
 def rank_program(g, core, T, topo):
@@ -73,6 +83,131 @@ def rank_program(g, core, T, topo):
             return False
         return not (x[3] == y[3] > 1 and (x[1] - y[1]) % x[3])
 
+    calls, urge = [], [0.0]
+
+    def note(e, fn, rd, wr, cost, late=0.0, sem=None, after=()):
+        k = len(calls)
+        dep = {a: False for a in after}
+        for xs, write in ((rd, False), (wr, True)):
+            for x in xs:
+                for y, w, a in hist.get(x[0], ()):
+                    q = calls[a]["e"]
+                    if (w or write or (x[0][:2] == "ps" and q != e)) and meet(x, y):
+                        dep[a] = not q == e == "p"
+        for x in wr:
+            h = hist.setdefault(x[0], [])
+            if x[0][:2] == "ps":
+                h[:] = []
+            elif x[3] == 1:
+                h[:] = [y for y in h if not (x[1] <= y[0][1] and y[0][2] <= x[2] and y[0][4] & ~x[4] == 0)]
+            h.append((x, True, k))
+        for x in rd:
+            hist.setdefault(x[0], []).append((x, False, k))
+        calls.append({"e": e, "fn": fn, "dep": dep, "cost": cost, "urge": urge[0], "late": late, "sem": sem})
+        return k
+
+    def ap(a):
+        return a[0] if isinstance(a, tuple) else a
+
+    def elems(a):
+        n = 1
+        for d in a.shape[1:]:
+            n *= d
+        return n
+
+    def op(e, fn, out, ins, more=(), rate=1.0):
+        ins = [a for a in ins if isinstance(a, tuple)]
+        rd = [x for a in ins for x in a[1] + (a[2] if len(a) > 2 else [])] + (out[2] if len(out) > 2 else [])
+        wide = [a for a in ins + [out] if len(a) == 2 and elems(a[0]) > 1]
+        n = max([elems(a[0]) for a in wide] + [1])
+        if len(out) > 2:
+            rate = SCATTER
+        elif any(len(a) > 2 for a in ins):
+            rate = GATHER
+        elif e == "v" and all(SCRATCH[a[1][0][0]][2] in (bf, fh, u1) for a in wide):
+            rate /= 2
+        note(e, fn, rd, out[1] + list(more), FIXED[e] + CYCLE * rate * n)
+
+    def dma(out, in_, after=()):
+        a = out if out[1] else in_
+        by = elems(a[0]) * a[0].shape[0] * (2 if SCRATCH[a[1][0][0]][2] == bf else 4)
+        note("y", lambda q: q.dma_start(out[0], in_[0]), in_[1] + list(after), out[1], FIXED["y"], DMA + by / 3e5)
+
+    def hbm(n):
+        return (T[n][:], [])
+
+    def engs(src, dst):
+        return topo.engines(src, dst)[:8]
+
+    def arrive(sem, n, t, sends):
+        note("r", None, [], R(t)[1], 0.0, REMOTE, (sem, n), sends)
+
+    def send(out, in_, dst, sem):
+        rid, pid, _ = topo.addr(dst)
+        e = engs(core, dst)
+        m = 0
+        for k in e:
+            m |= 1 << k
+        total["loc"] = total.get("loc", 0) + len(e)
+        return note("g", lambda q: q.remote_dma(out[0], in_[0], T.sem[sem], T.sem.loc, pid, rid, m), in_[1], [], ISSUE, sem="remote")
+
+    def deal(edges, way):
+        n = len(calls)
+        left = [0] * n
+        for es in edges:
+            for j, d in es:
+                left[j] += 1
+        at, free, out = [0.0] * n, {e: 0.0 for e in "vspgyr"}, []
+        ready = {e: [k for k in range(n) if calls[k]["e"] == e and not left[k]] for e in free}
+        while len(out) < n:
+            best = None
+            for e, ks in ready.items():
+                if not ks:
+                    continue
+                t = max(free[e], min(at[k] for k in ks))
+                k = max((k for k in ks if at[k] <= t), key=lambda k: way[k])
+                for j in ks:
+                    soon = t < at[j] < t + calls[k]["cost"] and way[j] > way[k]
+                    if soon and max(at[j] + way[j], at[j] + calls[j]["cost"] + way[k]) < t + calls[k]["cost"] + way[j]:
+                        k, t = j, at[j]
+                if best is None or t < best[0]:
+                    best = (t, k)
+            t, k = best
+            c = calls[k]
+            ready[c["e"]].remove(k)
+            at[k] = free[c["e"]] = t + c["cost"]
+            out.append(k)
+            for j, d in edges[k]:
+                at[j] = max(at[j], at[k] + d)
+                left[j] -= 1
+                if not left[j]:
+                    ready[calls[j]["e"]].append(j)
+        return out, at
+
+    def order():
+        n = len(calls)
+        fwd = [[] for _ in range(n)]
+        for k, c in enumerate(calls):
+            for a, sem in c["dep"].items():
+                fwd[a].append((k, (calls[a]["late"] + WAKE) * sem))
+        way = [0.0] * n
+        for k in range(n - 1, -1, -1):
+            way[k] = calls[k]["cost"] + max([way[j] + d for j, d in fwd[k]] + [calls[k]["late"]])
+        best = None
+        for _ in range(PASSES):
+            out, at = deal(fwd, [w + c["urge"] for w, c in zip(way, calls)])
+            end = max(a + c["late"] for a, c in zip(at, calls))
+            if best is None or end < best[0]:
+                best = (end, out)
+            tail, nx = [0.0] * n, {}
+            for k in reversed(out):
+                c = calls[k]
+                own = max([tail[j] + d for j, d in fwd[k]] + [c["late"]])
+                tail[k] = c["cost"] + max(own, nx.get(c["e"], 0.0))
+                nx[c["e"]] = tail[k]
+                way[k] = (way[k] + c["cost"] + own) / 2
+        return best[1]
+
     def waits(e, deps):
         m = {}
         for sem, val in deps:
@@ -89,81 +224,32 @@ def rank_program(g, core, T, topo):
                 seen[e][s2] = max(seen[e].get(s2, 0), v2)
             seen[e][sem] = max(seen[e].get(sem, 0), val)
 
-    def deps_of(e, rd, wr):
-        d = []
-        for x in rd:
-            for y, w, s, n, q in hist.get(x[0], ()):
-                if not (q == e == "p") and (w or (x[0][:2] == "ps" and q != e)) and meet(x, y):
-                    d.append((s, n))
-        for x in wr:
-            for y, w, s, n, q in hist.get(x[0], ()):
-                if not (q == e == "p") and meet(x, y):
-                    d.append((s, n))
-        return d
-
-    def note(s, n, q, rd, wr):
-        for x in wr:
-            h = hist.setdefault(x[0], [])
-            if x[0][:2] == "ps":
-                h[:] = []
-            elif x[3] == 1:
-                h[:] = [y for y in h if not (x[1] <= y[0][1] and y[0][2] <= x[2] and y[0][4] & ~x[4] == 0)]
-            h.append((x, True, s, n, q))
-        for x in rd:
-            h = hist.setdefault(x[0], [])
-            h[:] = [y for y in h if not (not y[1] and y[4] == q and y[2] == s and y[0] == x)]
-            h.append((x, False, s, n, q))
-
-    def split(out, ins):
-        rd = list(out[2]) if len(out) > 2 else []
-        for a in ins:
-            if isinstance(a, tuple):
-                rd += a[1] + (a[2] if len(a) > 2 else [])
-        return rd, out[1]
-
-    def ap(a):
-        return a[0] if isinstance(a, tuple) else a
-
-    def op(e, fn, out, ins, more=()):
-        rd, wr = split(out, ins)
-        wr = wr + list(more)
-        waits(e, deps_of(e, rd, wr))
-        cnt[e] += 1
-        fn(ENG[e]).then_inc(T.sem[SEM[e]], 1)
-        know[(SEM[e], cnt[e])] = dict(seen[e])
-        total[SEM[e]] = cnt[e]
-        note(SEM[e], cnt[e], e, rd, wr)
-
-    nd = [0]
-
-    def dma(out, in_):
-        rd, wr = split(out, [in_])
-        waits("y", deps_of("dma", rd, wr))
-        s = "d%d" % nd[0]; nd[0] += 1
-        g.sync.dma_start(out[0], in_[0]).then_inc(T.sem[s], 16)
-        know[(s, 16)] = dict(seen["y"])
-        total[s] = 16
-        note(s, 16, s, rd, wr)
-
-    def hbm(n):
-        return (T[n][:], [])
-
-    def engs(src, dst):
-        return topo.engines(src, dst)[:8]
-
-    def arrive(sem, n, t):
-        total[sem] = n
-        note(sem, n, sem, [], R(t)[1])
-
-    def send(out, in_, dst, sem):
-        waits("g", deps_of("rem", in_[1], []))
-        rid, pid, _ = topo.addr(dst)
-        e = engs(core, dst)
-        m = 0
-        for k in e:
-            m |= 1 << k
-        g.remote_dma(out[0], in_[0], T.sem[sem], T.sem.loc, pid, rid, m)
-        total["loc"] = total.get("loc", 0) + len(e)
+    def issue():
+        nd = 0
+        if len(calls) not in ORDER:
+            ORDER[len(calls)] = order()
+        for k in ORDER[len(calls)]:
+            c = calls[k]
+            e = c["e"]
+            if e == "r":
+                total[c["sem"][0]] = c["sem"][1]
+                continue
+            waits(e, [calls[a]["sem"] for a, sem in c["dep"].items() if sem])
+            x = c["fn"](ENG[e])
+            if c["sem"] == "remote":
+                continue
+            if e == "y":
+                c["sem"] = ("d%d" % nd, 16)
+                nd += 1
+                x.then_inc(T.sem[c["sem"][0]], 16)
+            else:
+                cnt[e] += 1
+                c["sem"] = (SEM[e], cnt[e])
+                x.then_inc(T.sem[SEM[e]], 1)
+            know[c["sem"]] = dict(seen[e])
+            total[c["sem"][0]] = c["sem"][1]
+        for s in total:
+            g.wait_ge(T.sem[s], total[s])
 
     def ts(out, in0, s1, op0, s2=None, op1=None):
         if op1 is None:
@@ -172,7 +258,7 @@ def rank_program(g, core, T, topo):
             op("v", lambda q: q.tensor_scalar(out[0], in0[0], ap(s1), ap(s2), op0, op1), out, [in0, s1, s2])
 
     def tt(out, a, b, o):
-        op("v", lambda q: q.tensor_tensor(out[0], a[0], b[0], o), out, [a, b])
+        op("v", lambda q: q.tensor_tensor(out[0], a[0], b[0], o), out, [a, b], (), 1.0 if a[1][0][0][:2] == "ps" else 2.0)
 
     def cp(out, in_):
         op("v", lambda q: q.tensor_copy(out[0], in_[0]), out, [in_])
@@ -180,22 +266,33 @@ def rank_program(g, core, T, topo):
     def ms(out, c):
         op("v", lambda q: q.memset(out[0], c), out, [])
 
-    def scan(out, d0, d1):
-        op("v", lambda q: q.tensor_tensor_scan(out[0], d0[0], d1[0], 0.0, A.mult, A.add), out, [d0, d1])
+    def scan(out, d0, d1, op0=A.mult, op1=A.add):
+        op("v", lambda q: q.tensor_tensor_scan(out[0], d0[0], d1[0], 0.0, op0, op1), out, [d0, d1])
 
     def act(out, in_, f=F.Copy, **kw):
         more = kw["accum_out"][1] if "accum_out" in kw else []
         op("s", lambda q: q.activation(out[0], in_[0], f, **{k: ap(x) for k, x in kw.items()}), out,
            [in_] + [x for k, x in kw.items() if k != "accum_out"], more)
 
+    def mms(ms_):
+        def fn(q):
+            for out, l, rh, st, sp in ms_:
+                x = q.matmul(out[0], l[0], rh[0], st, sp)
+            return x
+        rd = sorted(set(x for m in ms_ for x in m[1][1] + m[2][1]))
+        note("p", fn, rd, ms_[0][0][1], sum(max(64, elems(m[2][0])) for m in ms_) * PE)
+
     def mm(out, l, rh, st, sp):
-        op("p", lambda q: q.matmul(out[0], l[0], rh[0], st, sp), out, [l, rh])
+        mms([(out, l, rh, st, sp)])
 
     def iota(out, pat, base=0, cm=0):
-        if T[out[1][0][0]].dtype == T.cpi.dtype:
-            op("g", lambda q: q.iota(out[0], pat, base, cm), out, [])
+        if SCRATCH[out[1][0][0]][2] == i3:
+            op("g", lambda q: q.iota(out[0], pat, base, cm), out, [], (), 2.0)
         else:
-            op("g", lambda q: q.iota(out[0], pat, base, cm, allow_small_or_imprecise_dtypes=True), out, [])
+            op("g", lambda q: q.iota(out[0], pat, base, cm, allow_small_or_imprecise_dtypes=True), out, [], (), 2.0)
+
+    def pick(n, src, pat, cmp, base=0, cm=0, fill=0.0):
+        op("g", lambda q: q.affine_select(T[n][:], src[0], pat, cmp, fill, base, cm), R(n), [src], (), 2.0)
 
     f_ = lambda k, nj=16: R("sml", 16 * k, 16 * k + nj)
     n_ = lambda k, nj=16: R("smi", 16 * k, 16 * k + nj)
@@ -204,589 +301,396 @@ def rank_program(g, core, T, topo):
     tr = lambda k, nj=16: R("tr", 16 * k, 16 * k + nj)
     col = lambda k: R("ccol", k, k + 1)
     cpi = lambda k: R("cpi", k, k + 1)
+    ps = lambda b, c0=0, c1=None, s=1: R("ps%d" % b, c0, c1, s)
     EP, ES, E1, EI, EC, EH = range(6)
 
     def sel(n, i):
         return R("EE", 144 * n + 15 - i, 144 * n + 143 - i)
 
-    def ext(n, src, c0, c1, bank, o0, st, sp, i0=0, i1=16, step=16):
-        for i in range(i0, i1):
-            mm(R(bank, o0, o0 + (c1 - c0) // step), sel(n, i), R(src, c0 + i, c1, step), st and i == i0, sp and i == i1 - 1)
+    def ext(n, src, c0, c1, bank, o0, st, sp, i1=16):
+        mms([(ps(bank, o0, o0 + (c1 - c0) // i1), sel(n, i), R(src, c0 + i, c1, i1), st and i == 0, sp and i == i1 - 1) for i in range(i1)])
+
+    def spans(cut):
+        return [(e, ([0] + [c[1] for c in cut])[k], c1, bank) for k, (e, c1, bank) in enumerate(cut)]
+
+    def banks(cut):
+        out = {}
+        for e, c0, c1, bank in spans(cut):
+            out[bank] = (out.get(bank, (c0, c1))[0], c1)
+        return out
 
     dma(R("anL"), hbm("an0"))
     dma(R("ofL"), hbm("of0"))
+    dma(R("WK"), hbm("wk"), R("anL")[1])
     iota(cpi(0), [[1, 1]], 0, 1)
     iota(R("crow"), [[1, 160]], -16)
+    iota(R("kri"), [[1, 512]])
+    for l, z in enumerate(("Z1", "Z2")):
+        cs = [c for k in ("first", "later") for e, c0, c1, b in spans(CUT[k][l]) if e == "a" for c in (c0, c1)]
+        iota(R(z, min(cs), max(cs)), [[0, max(cs) - min(cs)]])
     iota(R("j16"), [[16, 16]])
-    iota(R("krow"), [[0, 2], [1, 256]])
-    iota(R("kst"), [[256, 2], [0, 256]])
-    iota(R("kri"), [[1, 256]])
+    iota(R("KQ"), [[16, 16], [0, 16]])
+    iota(R("XA"), [[0, 2048]], 1)
+    pick("RST", R("XA", 0, 256), [[0, 16], [1, 16]], A.is_gt)
+    pick("RS32", R("XA", 0, 512), [[0, 16], [1, 32]], A.is_equal, fill=-2.0)
+    iota(R("KC", 0, 160), [[-2048, 10], [0, 16]], 15 * 2048)
+    iota(R("KC", 160, 256), [[-2048, 6], [0, 16]], 5 * 2048 + 8 * 32768)
+    for n, nb in (("MK", 8), ("MKg", 3)):
+        iota(R(n), [[-16, 2], [0, nb], [1, 32]])
+    for h, kv in enumerate(GUEST):
+        iota(R("KCg", Q * h, Q * h + 6 * kv), [[-2048, kv], [0, 6]], 15 * 2048)
+        if kv < 16:
+            iota(R("KCg", Q * h + 6 * kv, Q * h + Q), [[-2048, 16 - kv], [0, 6]], (15 - kv) * 2048 + 8 * 32768)
+    for n, base, st in (("XLh", -2048, 1024), ("XLl", -10240, 1024), ("XA", 0, 0)):
+        pick(n, R("XA"), [[-1, 16], [-16, 8], [st, 16]], A.is_equal, base, 1)
     ms(R("XR"), 0.0)
-    ms(R("pl", 192, 248), 15.0); ms(R("pl", 440, 496), 128.0)
-    ts(cpi(1), cpi(0), 15, A.bitwise_and)
-    ts(cpi(2), cpi(0), 4, A.arith_shift_right)
-    ts(R("tI", 0, 192), R("anL"), 8, A.arith_shift_right)
-    ts(R("tI", 192, 384), R("anL"), 255, A.bitwise_and)
-    cp(R("pl", 0, 192), R("tI", 0, 192))
-    cp(R("pl", 248, 440), R("tI", 192, 384))
+    ms(R("pl", 192, 248), float(ROOT)); ms(R("pl", 440, 496), 0.0)
+    cp(R("pl", 0, 192), R("anL"))
+    tt(R("pl", 248, 440), R("anL"), R("pl", 0, 192), A.subtract)
     dma(R("XR", rows=(0, 128, 16)), R("pl", 0, 248))
     dma(R("XR", rows=(1, 128, 16)), R("pl", 248, 496))
     ts(R("tI", 0, 248), R("ofL"), 5, A.arith_shift_right)
     ts(R("tI", 248, 496), R("ofL"), 31, A.bitwise_and)
-    cp(R("pl", 496, 992), R("tI"))
+    cp(R("pl", 496, 744), R("tI", 0, 248))
+    cp(R("pl", 744, 992), R("tI", 248, 496))
     dma(R("XR", rows=(2, 128, 16)), R("pl", 496, 744))
     dma(R("XR", rows=(10, 128, 16)), R("pl", 744, 992))
-    dma(R("WK"), hbm("wk"))
-    dma(R("snL"), hbm("snd"))
-    dma(R("SWIN", 0, W), hbm("s0"))
-    dma(R("XW", 0, V), hbm("x"))
-    cp(R("PL"), R("anL"))
-    cp(R("ccol", 0, 3), R("cpi", 0, 3))
-    ts(cpi(3), cpi(2), 1, A.bitwise_and)
+    dma(R("snL"), hbm("snd"), R("XR")[1])
+    dma(R("SWIN", 0, W), hbm("s0"), R("XR")[1])
+    for i in range(16):
+        (cp if i % 3 < 2 else act)(R("BW", i, ROOT, 16), R("XR", i * 248, (i + 1) * 248))
+    for w in ("W2", "W3"):
+        dma(R(w, V, ROOT), R("BW", V, ROOT))
+    dma(R("XW", 0, V), hbm("x"), R("W2", 0, V)[1])
+    ts(cpi(1), cpi(0), 15, A.bitwise_and)
+    ts(cpi(2), cpi(0), 4, A.arith_shift_right)
     ts(cpi(4), cpi(0), 2, A.bitwise_and)
-    ms(R("EE"), 0.0)
-    ts(col(9), col(1), 0.0, A.is_equal)
-    ts(col(10), col(1), 1.0, A.is_equal)
-    ts(col(11), col(1), 7.5, A.is_lt, 31.0, A.mult)
-    cp(col(12), cpi(4))
+    ts(cpi(3), cpi(2), 1, A.bitwise_and)
+    cp(R("ccol", 0, 3), R("cpi", 0, 3))
     cp(col(7), cpi(3))
-    ts(R("BG"), R("crow", 16, 24), col(2), A.is_equal)
-    ts(col(3), col(9), 256.0, A.mult, col(10), A.add)
-    ts(col(13), col(10), 128.0, A.mult)
-    ts(col(11), col(11), 1.0, A.add)
-    ts(col(5), col(9), 15.0, A.mult, col(13), A.add)
-    ts(col(4), col(12), 0.5, A.mult, col(11), A.mult)
+    cp(col(12), cpi(4))
+    ts(col(3), col(1), 1.5, A.is_lt)
+    ts(col(5), col(1), 0.0, A.is_equal, float(ROOT), A.mult)
     ts(col(6), col(7), -1.0, A.mult, 1.0, A.add)
     ts(col(8), col(1), 11.5, A.is_lt)
+    ts(col(11), col(1), 7.5, A.is_lt, 31.0, A.mult)
+    ts(col(13), col(11), 1.0, A.add)
+    ts(col(4), col(12), 0.5, A.mult, col(13), A.mult)
+    ts(col(14), col(4), 0.5, A.is_gt)
+    cp(R("PL"), R("anL"))
+    for b in ("BW", "W2", "W3"):
+        ts(R(b, ROOT, BWW), R("crow", 0, 16), 0.0, A.mult, col(5), A.add)
+    cp(R("kr5"), R("kri"))
+    ts(R("ID"), R("crow", 16, 144), col(0), A.is_equal)
+    for n, w in (("I7", 7.0), ("IK", -1024.0), ("NI", -1.0), ("I12", 12.0), ("I16", 16.0), ("IO", col(14)), ("M1g", -4096.0)):
+        ts(R(n), R("ID"), w, A.mult)
+    ms(R("EE"), 0.0)
+    ts(R("BG"), R("crow", 16, 24), col(2), A.is_equal)
     for n, w in ((EP, col(3)), (ES, col(4)), (E1, 1.0), (EI, col(1)), (EC, SC), (EH, SC / 2)):
         ts(R("EE", 144 * n + 15, 144 * n + 143, 16), R("BG"), w, A.mult)
-    ts(R("ID"), R("crow", 16, 144), col(0), A.is_equal)
-    ms(R("ZR"), 0.0)
-    for b in ("BW", "W2", "W3"):
-        ts(R(b, ROOT, BWW), R("ZR", 0, 16), col(5), A.add)
-    ts(R("I7"), R("ID"), 7.0, A.mult)
-    ts(R("IK"), R("ID"), -1024.0, A.mult)
-    ms(R("Z1", CUT[0][0], V), 0.0)
-    ms(R("Z2", CUT[0][1], V), 0.0)
-    for n, base, st in (("XLh", -2048, 1024), ("XLl", -10240, 1024), ("XA", 0, 0)):
-        op("g", lambda q, n=n, base=base, st=st: q.affine_select(T[n][:], T.ZR[:], [[-1, 16], [-16, 8], [st, 16]], A.not_equal, 1.0, base, 1),
-           R(n), [R("ZR")])
+    ts(R("crq"), R("crow", 16, 144), 15, A.bitwise_and)
+    ts(R("crg"), R("crow", 16, 144), 4, A.arith_shift_right)
+    ts(R("BD"), R("crg"), col(2), A.is_equal)
+    ts(R("BDt"), R("crq"), col(1), A.is_gt, -1.0, A.add)
+    tt(R("BDt"), R("BDt"), R("BD"), A.mult)
+    tt(R("M1g"), R("M1g"), R("BDt"), A.add)
+    cp(R("krow"), R("kr5", 0, 256))
+    ts(R("KL2"), R("kr5", 1, 257), col(8), A.mult)
+    ts(R("REP"), R("crow", 0, 16), 0.0, A.mult, col(1), A.add)
+    ts(R("KQ"), R("KQ"), col(1), A.add)
+    ts(R("IoP"), R("crow"), col(0), A.is_equal, col(7), A.mult)
+    ts(R("IeP"), R("crow"), col(0), A.is_equal, col(6), A.mult)
+    ts(tr(0), R("j16"), col(1), A.add)
+    ts(tr(1), tr(0), float(BWW), A.add)
+    ts(tr(2), tr(0), float(W), A.add)
+    for n in ("MK", "MKg"):
+        ts(R(n), R(n), col(1), A.is_ge, STAY, A.mult)
+    for x, c in ((R("ONE"), 1.0), (R("thr", 0, 1), 9 * SC), (R("XW", V, V + 16), NEG), (R("xB", 512, 528), NEG), (R("DL", 192, 208), 0),
+                 (R("PF", 192, 200), BIG), (R("LW", 32, 40), BIG), (R("GN", 32, 40), BIG), (R("C32", 0, 16), 0.0),
+                 (R("C32", 16, 32), 4095.0), (R("Dw", 16, 24), 0), (R("GE"), 0), (R("OC"), 0.0)):
+        ms(x, c)
+    ts(R("OC", 0, 8), R("BG"), col(3), A.mult)
+    ts(R("OC", 32, 40), R("BG"), col(4), A.mult)
+    a, b = R("tI", 0, 56), R("tI", 64, 120)
+    ts(a, R("snL"), 15, A.bitwise_and)
+    ts(b, R("snL"), 4, A.arith_shift_right)
+    ts(a, a, 192.0, A.mult)
+    tt(R("SL"), a, b, A.add)
 
     def candidates(b):
         c = (512 * b, 512 * b + 512)
-        s = R("sg", 512 * (b % 2), 512 * (b % 2) + 512)
-        for p in ("ps%d" % (4 + b % 2), "ps%d" % (6 + b % 2)):
-            two = p[2] in "67"
-            mm(R(p), R("I7"), R("WK", *c), True, False)
-            mm(R(p), R("ID"), R("krow"), False, False)
-            mm(R(p), R("ID"), R("kst"), False, not two)
-            if two:
-                mm(R(p), R("IK"), s, False, True)
-                act(R("CT", *c), R(p), F.Identity, bias=512.0 * b - 1024.0)
-            else:
-                act(s, R(p), F.Sign, bias=512.0 * b - 2047.5)
+        s, p = R("sg", 512 * (b % 2), 512 * (b % 2) + 512), ps(6 + b % 2)
+        mms([(p, R("I7"), R("WK", *c), True, False), (p, R("ID"), R("kr5"), False, True)])
+        act(s, p, F.Sign, bias=512.0 * b - 2047.5)
+        mms([(p, R("I7"), R("WK", *c), True, False), (p, R("ID"), R("kr5"), False, False), (p, R("IK"), s, False, True)])
+        act(R("CT", *c), p, F.Identity, bias=512.0 * b - 1024.0)
 
-    candidates(0)
-    for i in range(16):
-        (cp if i % 8 < 6 else act)(R("BW", i, ROOT, 16), R("XR", i * 248, (i + 1) * 248))
+    for b in range(4):
+        candidates(b)
 
-    def consts2():
-        ts(R("crq"), R("crow", 16, 144), 15, A.bitwise_and)
-        ts(R("crg"), R("crow", 16, 144), 4, A.arith_shift_right)
-        ts(R("NI"), R("ID"), -1.0, A.mult)
-        ts(R("BD"), R("crg"), col(2), A.is_equal)
-        ts(R("BDt"), R("crq"), col(1), A.is_gt, -1.0, A.add)
-        ts(R("M1g"), R("ID"), -4096.0, A.mult)
-        tt(R("BDt"), R("BDt"), R("BD"), A.mult)
-        ms(R("ONE"), 1.0)
-        tt(R("M1g"), R("M1g"), R("BDt"), A.add)
-        ms(R("thr", 0, 1), 9 * SC)
-        ms(R("XW", V, V + 16), NEG)
-        ms(R("DL", 192, 208), 0)
-        ms(R("PF", 192, 200), BIG)
-        ms(R("LW", 32, 40), BIG)
-        ts(R("I12"), R("ID"), 12.0, A.mult)
-        ts(R("I16"), R("ID"), 16.0, A.mult)
+    LV = (("BW", "PL", "Z1", "W2", "PL1", (2, 128, 8), (6, 128, 8)), ("W2", "PL1", "Z2", "W3", "PL2", (2, 128, 4), (3, 128, 4)))
 
-    def consts3():
-        ts(R("dg", 0, 256), R("kri"), 15, A.bitwise_and)
-        ts(R("KL2"), R("krow", 0, 256), 1.0, A.add, col(8), A.mult)
-        ts(R("REP"), R("ZR", 0, 16), col(1), A.add)
-        ts(R("RST"), R("dg", 0, 256), 0.5, A.is_gt)
-        tt(R("KQ"), R("kri"), R("dg", 0, 256), A.subtract)
-        ts(R("KL2"), R("KL2"), -1.0, A.add)
-        ts(R("KQ"), R("KQ"), col(1), A.add)
-        ts(tr(0), R("j16"), col(1), A.add)
-        ts(R("IeP"), R("crow"), col(0), A.is_equal, col(6), A.mult)
-        ts(R("IoP"), R("crow"), col(0), A.is_equal, col(7), A.mult)
-        ts(tr(1), tr(0), float(BWW), A.add)
-        ts(tr(2), tr(0), float(W), A.add)
-        ms(R("xB", 512, 528), NEG)
+    def lists(w, p, cut):
+        for bank, (c0, c1) in banks(cut).items():
+            ext(EP, w, c0, c1, bank, c0 // 16, True, True)
+            cp(R(p, c0 // 16, c1 // 16), ps(bank, c0 // 16, c1 // 16))
 
-    def consts4():
-        a, b = R("tI", 0, 56), R("tI", 64, 120)
-        ts(a, R("snL"), 15, A.bitwise_and)
-        ts(b, R("snL"), 4, A.arith_shift_right)
-        ts(R("GW"), R("XR", 0, V), 0.0, A.mult, col(5), A.add)
-        ts(a, a, 192.0, A.mult)
-        tt(R("SL"), a, b, A.add)
+    def dates(cut):
+        for (w, p, z, n, pn, src, dst), lv in zip(LV, cut):
+            for e, c0, c1, bank in spans(lv):
+                x = IND(R(w, 0, BWW), R(p, c0 // 16, c1 // 16))
+                if e == "a":
+                    dma(R(z, c0, c1, rows=src), R(w, c0, c1, rows=src))
+                    tt(R(n, c0, c1), x, R(z, c0, c1), A.add)
+                elif e == "p":
+                    y, s = ps(3, 0, c1 - c0), R("SG", 2112, 2112 + c1 - c0)
+                    mm(y, R("IO"), R(w, c0, c1), True, False)
+                    act(s, x)
+                    mm(y, R("ID"), s, False, True)
+                    act(R(n, c0, c1), y)
+                else:
+                    (cp if e in "vV" else act)(R(n, c0, c1), x)
+                if e in "sv":
+                    dma(R(n, c0, c1, rows=dst), R(w, c0, c1, rows=src))
+                if e == "p":
+                    ext(EP, "SG", 2112, 2112 + c1 - c0, bank, c0 // 16, True, True)
+                else:
+                    ext(EP, n, c0, c1, bank, c0 // 16, True, True)
+                if e in "SV":
+                    dma(R(n, c0, c1, rows=dst), R(w, c0, c1, rows=src))
+                if c1 == banks(lv)[bank][1]:
+                    b0 = banks(lv)[bank][0]
+                    cp(R(pn, b0 // 16, c1 // 16), ps(bank, b0 // 16, c1 // 16))
+        for e, c0, c1, bank in spans(cut[2]):
+            (cp if e == "v" else act)(R("G3", c0, c1), IND(R("W3", 0, BWW), R("PL2", c0 // 16, c1 // 16)))
+        for bank, (c0, c1) in banks(cut[2]).items():
+            c = (c0 // 16, c1 // 16)
+            ext(ES, "W3", c0, c1, bank, c[0], True, False)
+            ext(ES, "G3", c0, c1, bank, c[0], False, True)
+            cp(R("DI", *c), ps(bank, *c))
+            ts(R("DL", *c), R("DI", *c), 2047, A.bitwise_and)
+            cp(R("DU", *c), R("DL", *c))
 
-    def consts5():
-        iota(R("KC", 0, 160), [[-2048, 10], [0, 16]], 15 * 2048)
-        iota(R("KC", 160, 256), [[-2048, 6], [0, 16]], 5 * 2048 + 8 * 32768)
-        iota(R("KCg"), [[-2048, 16], [0, 6]], 15 * 2048)
-        iota(R("RS32"), [[0, 16], [1, 32]])
-        iota(R("tI", 0, 32), [[1, 2], [2, 8], [0, 2]])
-        iota(R("tI", 32, 44), [[1, 2], [2, 3], [0, 2]])
-        for n, nb in (("MK", 8), ("MKg", 3)):
-            iota(R(n), [[-16, 2], [0, nb], [1, 32]])
+    def beaten(m):
+        a, z = CUT["beat"]
+        at = lambda c0, c1: IND(R("SWIN", 0, W), R("DU", c0 // 16, c1 // 16))
+        for c0, c1 in ((3 * a, m), (m, z), (z, V)):
+            tt(R("bits", c0, c1), at(c0, c1), R("XW", c0, c1), A.is_le)
+        for k in range(3):
+            c, p = (a * k, a * k + a), ps(4 + k, 0, a)
+            mm(p, R("ID"), R("XW", *c), True, False)
+            act(R("SG", *c), at(*c))
+            mm(p, R("NI"), R("SG", *c), False, True)
+            act(R("bits", *c), p, F.Sign, bias=TINY)
+        for cs, bank, least in (((3 * a, m, z, V), 0, 4.5), ((0, 2 * a, 3 * a), 1, -7.0)):
+            for c0, c1 in zip(cs, cs[1:]):
+                ext(E1, "bits", c0, c1, bank, c0 // 16, True, True)
+            ts(R("fl", cs[0] // 16, cs[-1] // 16), ps(bank, cs[0] // 16, cs[-1] // 16), least, A.is_lt)
 
-    def consts6():
-        ts(R("RS32"), R("RS32"), 0.5, A.is_gt)
-        cp(R("RJ"), R("tI", 0, 32))
-        cp(R("RJg"), R("tI", 32, 44))
-        for n in ("MK", "MKg"):
-            ts(R(n), R(n), col(1), A.is_ge, 8192.0, A.mult)
-        ms(R("C32", 0, 16), 0.0); ms(R("C32", 16, 32), 4095.0)
-        ms(R("GN", 32, 40), BIG)
-        ms(R("Dw", 16, 24), 0)
-        for t in range(RO):
-            ms(R("GE%d" % t), 0)
-        ms(R("OC"), 0.0)
-        ts(R("OC", 0, 8), R("BG"), col(3), A.mult)
-        ts(R("OC", 32, 40), R("BG"), col(4), A.mult)
-
-    LV = {1: ("BW", "PL", "Z1", "W2", "PL1", (2, 128, 8), (6, 128, 8)), 2: ("W2", "PL1", "Z2", "W3", "PL2", (2, 128, 4), (3, 128, 4))}
-
-    def addends(l, c0, c1=V):
-        w, p, z, n, pn, src, dst = LV[l]
-        dma(R(z, c0, c1, rows=src), R(w, c0, c1, rows=src))
-
-    def dbl_s(l, c0, c1, bank):
-        w, p, z, n, pn, src, dst = LV[l]
-        act(R(n, c0, c1), IND(R(w, 0, BWW), R(p, c0 // 16, c1 // 16)))
-        dma(R(n, c0, c1, rows=dst), R(w, c0, c1, rows=src))
-
-    def dbl_v(l, c0, c1, add=True):
-        w, p, z, n, pn, src, dst = LV[l]
-        if add:
-            tt(R(n, c0, c1), IND(R(w, 0, BWW), R(p, c0 // 16, c1 // 16)), R(z, c0, c1), A.add)
-        else:
-            cp(R(n, c0, c1), IND(R(w, 0, BWW), R(p, c0 // 16, c1 // 16)))
-            dma(R(n, c0, c1, rows=dst), R(w, c0, c1, rows=src))
-
-    def anch(w, c0, c1, bank):
-        ext(EP, w, c0, c1, bank, c0 // 16, True, True)
-
-    def lst(p, c0, c1, bank):
-        cp(R(p, c0 // 16, c1 // 16), R(bank, c0 // 16, c1 // 16))
-
-    def own3(h):
-        ext(ES, "W3", 1536 * h, 1536 * h + 1536, "ps%d" % (2 + h), 0, True, False)
-
-    def g3(e, c0, c1):
-        (cp if e == "v" else act)(R("G3", c0, c1), IND(R("W3", 0, BWW), R("PL2", c0 // 16, c1 // 16)))
-
-    def e3(c0, c1, sp):
-        h = c0 // 1536
-        ext(ES, "G3", c0, c1, "ps%d" % (2 + h), c0 // 16 - 96 * h, False, sp)
-
-    def date(h):
-        c = (96 * h, 96 * h + 96)
-        cp(R("DI", *c), R("ps%d" % (2 + h), 0, 96))
-        ts(R("DL", *c), R("DI", *c), 2047, A.bitwise_and)
-        cp(R("DU", *c), R("DL", *c))
-
-    def beat_v(c0, c1):
-        tt(R("bits", c0, c1), IND(R("SWIN", 0, W), R("DU", c0 // 16, c1 // 16)), R("XW", c0, c1), A.is_le)
-
-    def beat_g(c0, c1):
-        act(R("SG", c0, c1), IND(R("SWIN", 0, W), R("DU", c0 // 16, c1 // 16)))
-
-    def beat_d(c0, c1, bank):
-        mm(R(bank, 0, c1 - c0), R("ID"), R("XW", c0, c1), True, False)
-        mm(R(bank, 0, c1 - c0), R("NI"), R("SG", c0, c1), False, True)
-        act(R("bits", c0, c1), R(bank, 0, c1 - c0), F.Sign, bias=TINY)
-
-    def beat_e(c0, c1, bank):
-        ext(E1, "bits", c0, c1, bank, c0 // 16, True, True)
-
-    def beaten():
-        beat_g(0, 384); beat_v(1152, 1536); beat_g(384, 768)
-        beat_d(0, 384, "ps4")
-
-    def beaten2():
-        beat_v(1536, 2432)
-        beat_g(768, 1152)
-        beat_d(384, 768, "ps5")
-        beat_e(1152, 1536, "ps0")
-        beat_d(768, 1152, "ps4")
-        beat_v(2432, V)
-        beat_e(1536, 2432, "ps0")
-        beat_e(0, 1152, "ps1")
-        beat_e(2432, V, "ps0")
-        ts(R("fl", 0, 72), R("ps1", 0, 72), -7.0, A.is_lt)
-        ts(R("fl", 72, 192), R("ps0", 72, 192), 4.5, A.is_lt)
-
-    def ghosts_a():
+    def ghosts(t):
         ts(R("dg", 0, 192), R("DL", 0, 192), 5, A.arith_shift_right)
         ts(R("dg", 192, 384), R("DL", 0, 192), 31, A.bitwise_and)
-
-    def ghosts_a2():
-        cp(R("dgb"), R("dg"))
-        dma(R("GW", rows=(2, 128, 16)), R("dgb", 0, 192))
-        dma(R("GW", rows=(10, 128, 16)), R("dgb", 192, 384))
-
-    def ghosts_b(t):
-        act(R("GO%d" % t), IND(R("GW"), R("SL")))
-        for d in range(1, N):
-            c = (128 * (d - 1), 128 * d)
-            send(R("GL%d" % t, *c), R("GO%d" % t, *c), cores[(r + d) % N], "gh%d" % t)
-        arrive("gh%d" % t, sum(len(engs(cores[(r - d) % N], core)) for d in range(1, N)), "GL%d" % t)
-
-    def ghosts_in(t, bs):
-        for b in bs:
+        for h in range(2):
+            cp(R("dgb", 192 * h, 192 * h + 192), R("dg", 192 * h, 192 * h + 192))
+            dma(R("XR", 0, V, rows=(2 + 8 * h, 128, 16)), R("dgb", 192 * h, 192 * h + 192))
+        act(R("GO%d" % t), IND(R("XR", 0, V), R("SL")))
+        ks = [send(R("GL%d" % t, 128 * (d - 1), 128 * d), R("GO%d" % t, 128 * (d - 1), 128 * d), cores[(r + d) % N], "gh%d" % t)
+              for d in range(1, N)]
+        arrive("gh%d" % t, sum(len(engs(cores[(r - d) % N], core)) for d in range(1, N)), "GL%d" % t, ks)
+        for b in ("BW", "W2", "W3"):
             dma(R(b, V, ROOT, rows=(2, 128, 8)), R("GL%d" % t, rows=(2, 128, 8)))
 
     vU, DlU = u_(0), u_(1)
 
-    def count16(win, n, out):
-        tt(R("o1", 0, n), IND(win, R("REP", 0, n // 16)), R("KQ", 0, n), A.is_le)
-        scan(R("o2", 0, n), R("RST", 0, n), R("o1", 0, n))
-        cp(out, R("o2", 15, n, 16))
+    def count16(win, o, n, out):
+        tt(R("o1", o, o + n), IND(win, R("REP", 0, n // 16)), R("KQ", 0, n), A.is_le)
+        scan(R("o2", o, o + n), R("RST", 0, n), R("o1", o, o + n))
+        cp(out, R("o2", o + 15, o + n, 16))
 
-    def compact(t):
-        mm(R("ps3", 0, 192), R("M1g"), R("fl"), True, False)
+    def compact():
+        mm(ps(4, 0, 192), R("M1g"), R("fl"), True, False)
         scan(R("binc"), R("ONE"), R("fl"))
-        mm(R("ps2", 0, 16), R("BD"), R("binc", 11, 192, 12), True, True)
-        ext(E1, "binc", 0, 192, "ps2", 16, True, True, 0, 12, 12)
-        mm(R("ps3", 0, 192), R("BD"), R("binc"), False, True)
-        if t < RO - 1:
-            ghosts_a()
-        cp(R("LW", 0, 32), R("ps2", 0, 32))
-        count16(R("LW", 0, 16), 256, u_(2))
-        mm(R("ps0", 0, 16), R("I12"), R("o2", 15, 256, 16), True, False)
-        tt(R("o3"), IND(R("LW", 16, 40), u_(2)), R("KL2"), A.is_le)
-        ext(E1, "o3", 0, 256, "ps0", 0, False, True)
-        ts(R("PF", 0, 192), R("ps3", 0, 192), 4095.0, A.add)
-        if t < RO - 1:
-            ghosts_a2()
-        cp(u_(3), R("ps0", 0, 16))
-        act(b_(0), R("ps0", 0, 16))
-        tt(R("OH"), IND(R("PF"), u_(3)), R("krow", 0, 256), A.is_equal)
-        mm(R("ps1", 0, 16), R("I16"), b_(0), True, False)
-        ext(EI, "OH", 0, 256, "ps1", 0, False, True)
-        tt(R("Ds"), IND(R("DL"), u_(3)), R("OH"), A.mult)
-        ext(E1, "Ds", 0, 256, "ps2", 0, True, True)
-        cp(vU, R("ps1", 0, 16))
+        mm(ps(3, 0, 16), R("BD"), R("binc", 11, 192, 12), True, True)
+        ext(E1, "binc", 0, 192, 5, 0, True, True, 12)
+        mm(ps(4, 0, 192), R("BD"), R("binc"), False, True)
+        cp(R("LW", 0, 16), ps(3, 0, 16))
+        act(R("LW", 16, 32), ps(5, 0, 16))
+        act(R("PF", 0, 192), ps(4, 0, 192), F.Identity, bias=4095.0)
+        count16(R("LW", 0, 16), 0, 256, u_(2))
+        mm(ps(0, 0, 16), R("I12"), R("o2", 15, 256, 16), True, False)
+        tt(R("o3"), IND(R("LW", 16, 40), u_(2)), R("KL2"), A.is_lt)
+        ext(E1, "o3", 0, 256, 0, 0, False, True)
+        cp(u_(3), ps(0, 0, 16))
+        cp(b_(0), u_(3))
+        tt(R("OH", 0, 256), IND(R("PF"), u_(3)), R("krow"), A.is_equal)
+        mm(ps(1, 0, 16), R("I16"), b_(0), True, False)
+        ext(EI, "OH", 0, 256, 1, 0, False, True)
+        tt(R("Ds", 0, 256), IND(R("DL"), u_(3)), R("OH", 0, 256), A.mult)
+        ext(E1, "Ds", 0, 256, 2, 0, True, True)
+        cp(vU, ps(1, 0, 16))
         act(R("xB", 0, 256), IND(R("XW"), vU))
-        cp(R("vf"), R("ps1", 0, 16))
         act(R("xB", 256, 512), R("xB", 0, 256))
-        tt(f_(14), R("vf"), tr(1), A.subtract)
+        cp(DlU, ps(2, 0, 16))
+        cp(R("vf"), vU)
+        cp(R("Dw", 0, 16), DlU)
         ts(f_(15), R("vf"), 3071.5, A.is_lt)
-        cp(DlU, R("ps2", 0, 16))
 
-    def turn(D, nj, TBn):
-        cp(R("CG", 0, 16 * nj), IND(R("CT"), D))
+    def turn(D, o, nj, TBn):
+        cp(R("CG", o, o + 16 * nj), IND(R("CT"), D))
         for b in range(nj // 2):
-            op("v", lambda q, b=b: q.transpose(T[TBn][:, :, b], T.CG[:, 32 * b:32 * b + 32]), (None, [(TBn, b, 1 << 20, 64, ALL)]),
-               [R("CG", 32 * b, 32 * b + 32)])
+            x = R("CG", o + 32 * b, o + 32 * b + 32)
+            op("v", lambda q, b=b, x=x: q.transpose(T[TBn][:, :, b], x[0]), (T[TBn][:, :, b], [(TBn, b, 1 << 20, 64, ALL)]), [x])
 
-    def days(nj, TBn, bank, k0, k1, st, sp):
+    def days(nj, TBn, bank, k0, k1, sp):
         n = (k1 - k0) * nj
         lo, hi = R3(TBn, T[TBn][:, k0:k1, :]), R3(TBn, T[TBn][:, 16 + k0:16 + k1, :])
-        mm(R(bank, 0, n, 2), R("IeP", 16, 144), lo, st, False)
-        mm(R(bank, 0, n, 2), R("IeP", 0, 128), hi, False, st)
-        mm(R(bank, 1, n, 2), R("IoP", 32, 160), lo, st, False)
-        mm(R(bank, 1, n, 2), R("IoP", 16, 144), hi, False, st or sp)
+        mms([(ps(bank, 0, n, 2), R("IeP", 16, 144), lo, True, False), (ps(bank, 0, n, 2), R("IeP", 0, 128), hi, False, False),
+             (ps(bank, 1, n, 2), R("IoP", 32, 160), lo, False, False), (ps(bank, 1, n, 2), R("IoP", 16, 144), hi, False, sp)])
 
-    def cmp_v(x, nj, k):
-        n = 16 * nj
-        tt(R("bits", n * k, n * k + 2 * n), IND(R("SWIN", 0, W), R("cu", nj * k, nj * k + 2 * nj)), x, A.is_lt)
-
-    def choose(t):
-        turn(DlU, 16, "TB")
-        days(16, "TB", "ps3", 0, 16, True, True)
-        cp(R("Dw", 0, 16), R("ps2", 0, 16))
-        cp(R("cu"), R("ps3", 0, 256))
-        for h in range(2):
-            mm(R("ps%d" % h, 0, 128), R("ID"), R("KC", 128 * h, 128 * h + 128), True, False)
-            days(16, "TB", "ps%d" % h, 8 * h, 8 * h + 8, False, False)
+    def choose():
+        turn(DlU, 0, 16, "TB")
+        for h in (1, 0):
+            days(16, "TB", 2 + 5 * h, 8 * h, 8 * h + 8, True)
+            cp(R("cu", 128 * h, 128 * h + 128), ps(2 + 5 * h, 0, 128))
+            days(16, "TB", 3 * h, 8 * h, 8 * h + 8, False)
+            mm(ps(3 * h, 0, 128), R("ID"), R("KC", 128 * h, 128 * h + 128), False, False)
         x = R("xB", 0, 512)
-
-        def sg(a):
-            act(R("SG", 512 * a, 512 * a + 512), IND(R("SWIN", 0, W), R("cu", 160 + 32 * a, 192 + 32 * a)))
-
-        def sd(a):
-            p = R("ps%d" % (4 + a))
-            mm(p, R("ID"), x, True, False)
-            mm(p, R("NI"), R("SG", 512 * a, 512 * a + 512), False, True)
-            act(R("bits", 2560 + 512 * a, 3072 + 512 * a), p, F.Sign, bias=-TINY)
-
-        sg(0); cmp_v(x, 16, 8); sg(1); sd(0); cmp_v(x, 16, 0)
-        ext(EC, "bits", 2048, 2560, "ps1", 0, False, False)
-        sg(2); sd(1); cmp_v(x, 16, 2); cmp_v(x, 16, 4)
-        ext(EC, "bits", 0, 1024, "ps0", 0, False, False)
-        sd(2)
-        ext(EH, "bits", 2560, 3584, "ps1", 32, False, False)
-        cmp_v(x, 16, 6)
-        ext(EH, "bits", 3584, 4096, "ps1", 96, False, True)
-        ext(EC, "bits", 1024, 2048, "ps0", 64, False, True)
-        act(R("key", 0, 128), R("ps1", 0, 128))
-        tt(R("key", 128, 256), R("ps0", 0, 128), R("key", 0, 128), A.max)
+        at = lambda k: IND(R("SWIN", 0, W), R("cu", 16 * k, 16 * k + 32))
+        for k in (8, 0, 2, 4, 6):
+            tt(R("bits", 256 * k, 256 * k + 512), at(k), x, A.is_lt)
+        for a in range(3):
+            s = R("SG", 512 * a, 512 * a + 512)
+            mm(ps(4 + a), R("ID"), x, True, False)
+            act(s, at(10 + 2 * a))
+            mm(ps(4 + a), R("NI"), s, False, True)
+            act(R("bits", 2560 + 512 * a, 3072 + 512 * a), ps(4 + a), F.Sign, bias=-TINY)
+        ext(EC, "bits", 2048, 2560, 3, 0, False, False)
+        ext(EH, "bits", 2560, 3584, 3, 32, False, False)
+        ext(EH, "bits", 3584, 4096, 3, 96, False, True)
+        ext(EC, "bits", 0, 1024, 0, 0, False, False)
+        ext(EC, "bits", 1024, 2048, 0, 64, False, True)
+        act(R("key", 0, 128), ps(3, 0, 128))
+        tt(R("key", 128, 256), ps(0, 0, 128), R("key", 0, 128), A.max)
         tt(R("key", 0, 64), R("key", 128, 192), R("key", 192, 256), A.max)
         tt(R("key", 64, 96), R("key", 0, 32), R("key", 32, 64), A.max)
         tt(n_(5), R("key", 64, 80), R("key", 80, 96), A.max)
 
-    def moved(t, nj, k, m, c):
-        ts(m, k, R("thr", t, t + 1), A.is_ge)
-        ts(c, k, 2047, A.bitwise_and)
-
     mv, mg = b_(1), b_(2, 6)
 
-    def move_list():
+    def moves(t):
+        ts(mv, n_(5), R("thr", t, t + 1), A.is_lt, STAY, A.mult)
         ts(n_(2), n_(5), 5, A.arith_shift_right, 63, A.bitwise_and)
         ts(n_(3), n_(5), 31, A.bitwise_and)
         cp(R("smb", 48, 80), R("smi", 32, 64))
-        for i in range(16):
-            mm(R("ps2", i, 256, 16), R("XLh", 128 * i, 128 * i + 128), b_(3), True, False)
-            mm(R("ps2", i, 256, 16), R("XLl", 128 * i, 128 * i + 128), b_(4), False, True)
-        act(R("RD"), R("ps2", 0, 256), F.Identity, bias=col(5))
-
-    def move_off():
-        tt(f_(2), mv, f_(14), A.mult)
-        tt(u_(4), f_(2), tr(1), A.add)
-
-    def move_put():
+        mms([(ps(2, i, 256, 16), R(("XLh", "XLl")[h], 128 * i, 128 * i + 128), b_(3 + h), h == 0, h == 1)
+             for i in range(16) for h in range(2)])
+        act(R("RD"), ps(2, 0, 256), F.Identity, bias=col(5))
+        tt(f_(2), mv, R("vf"), A.add)
+        tt(u_(4), f_(2), tr(1), A.min)
         cp(IND(R("BW"), u_(4)), R("RD"))
 
-    def refuse_a():
-        tt(b_(5), f_(15), mv, A.subtract)
+    def refuse(t):
+        dst, src = cores[(r + 1 + t % (N - 1)) % N], cores[(r - 1 - t % (N - 1)) % N]
+        tt(b_(5), f_(15), mv, A.min)
         scan(b_(6), R("ONE", 0, 16), b_(5))
-        mm(R("ps4", 0, 16), R("BD"), b_(6), True, True)
-        mm(R("ps4", 16, 32), R("M1g"), b_(5), True, False)
-        mm(R("ps4", 16, 32), R("BD"), b_(6), False, True)
-
-    def refuse_b():
-        tt(R("GN", 0, 32), R("ps4", 0, 32), R("C32"), A.add)
-        count16(R("GN", 0, 16), Q, u_(5, 6))
-        mm(R("ps4", 0, 6), R("I16"), R("o2", 15, Q, 16), True, False)
-        tt(R("OH", 0, Q), IND(R("GN", 16, 40), u_(5, 6)), R("krow", 0, Q), A.is_equal)
-        tt(R("Ds", 0, Q), IND(R("Dw"), u_(5, 6)), R("OH", 0, Q), A.mult)
-        ext(EI, "OH", 0, Q, "ps4", 0, False, True)
-        ext(E1, "Ds", 0, Q, "ps5", 0, True, True)
-
-    def refuse_c(t):
-        dst, src = cores[(r + 1 + t % (N - 1)) % N], cores[(r - 1 - t % (N - 1)) % N]
-        cp(u_(6, 6), R("ps4", 0, 6))
-        cp(R("GE%d" % t, 0, 6), R("ps5", 0, 6))
-        send(R("GD%d" % t), R("GE%d" % t), dst, "gd%d" % t)
-        arrive("gd%d" % t, len(engs(src, core)), "GD%d" % t)
-
-    def refuse_d(t):
-        dst, src = cores[(r + 1 + t % (N - 1)) % N], cores[(r - 1 - t % (N - 1)) % N]
+        mms([(ps(4, 0, 16), R("BD"), b_(6), True, True), (ps(4, 16, 32), R("M1g"), b_(5), True, False),
+             (ps(4, 16, 32), R("BD"), b_(6), False, True)])
+        tt(R("GN", 0, 32), ps(4, 0, 32), R("C32"), A.add)
+        count16(R("GN", 0, 16), 256, Q, u_(5, 6))
+        tt(R("OH", 256, 352), IND(R("GN", 16, 40), u_(5, 6)), R("krow", 0, Q), A.is_equal)
+        tt(R("Ds", 256, 352), IND(R("Dw"), u_(5, 6)), R("OH", 256, 352), A.mult)
+        ext(E1, "Ds", 256, 352, 5, 0, True, True)
+        mm(ps(4, 0, 6), R("I16"), R("o2", 271, 352, 16), True, False)
+        ext(EI, "OH", 256, 352, 4, 0, False, True)
+        cp(R("GE", 8 * t, 8 * t + 6), ps(5, 0, 6))
+        k = send(R("GD%d" % t), R("GE", 8 * t, 8 * t + 8), dst, "gd%d" % t)
+        arrive("gd%d" % t, len(engs(src, core)), "GD%d" % t, [k])
+        cp(u_(6, 6), ps(4, 0, 6))
         G = "GS%d" % t
         act(R(G, 0, Q), IND(R("xB", 256, 528), u_(6, 6)))
         act(R(G, Q, 2 * Q), R(G, 0, Q))
-        send(R("GX%d" % t), R(G), dst, "gu%d" % t)
-        arrive("gu%d" % t, len(engs(src, core)), "GX%d" % t)
+        k = send(R("GX%d" % t), R(G), dst, "gu%d" % t)
+        arrive("gu%d" % t, len(engs(src, core)), "GX%d" % t, [k])
 
-    def parity_a():
-        mm(R("ps7", 0, 16), R("ONE", 0, 128), mv, True, True)
-        act(f_(6), R("ps7", 0, 16), accum_out=f_(7, 1))
-
-    def parity_b(t):
+    def parity(t):
+        mm(ps(7, 0, 16), R("ONE", 0, 128), mv, True, True)
+        act(f_(6), ps(7, 0, 16), accum_out=f_(7, 1))
         cp(n_(1, 1), f_(7, 1))
-        ts(n_(1, 1), n_(1, 1), 1, A.bitwise_and)
+        ts(n_(1, 1), n_(1, 1), 13, A.arith_shift_right, 1, A.bitwise_and)
         ts(R("thr", t + 1, t + 2), n_(1, 1), SC, A.mult, 9 * SC, A.add)
 
-    def dedup_a(nj, m, c, MK):
-        n = 16 * nj
-        ts(f_(8, nj), c, 1.0, A.add)
-        tt(f_(10, nj), c, tr(2, nj), A.subtract)
-        tt(R("cmh", 0, nj), f_(8, nj), m, A.mult)
-        tt(R("cmw", 0, nj), f_(8, nj), m, A.mult)
-        mm(R("ps6", 0, 2 * n), R("ID"), R(MK), True, False)
-        for i in range(16):
-            for h in range(2):
-                mm(R("ps6", n * h + i, n * h + n, 16), R("XA", 128 * i, 128 * i + 128), R("cmh", 0, nj), False, i == 15 and h == 1)
+    def settle(nj, key, m, MK, x, z):
+        n, o = 16 * nj, 512 * z
+        c, lost, off, cw = n_(6 * z, nj), f_(8 + z, nj), f_(10 + z, nj), R("cmw", 16 * z, 16 * z + nj)
+        ts(c, key, 2047, A.bitwise_and)
+        for y in (R("cmh", 32 * z, 32 * z + nj), R("cmh", 32 * z + nj, 32 * z + 2 * nj), cw):
+            tt(y, c, m, A.add)
+        mm(ps(6, 0, 2 * n), R("ID"), R(MK), True, False)
+        mms([(ps(6, i, 2 * n, 16), R("XA", 128 * i, 128 * i + 128), R("cmh", 32 * z, 32 * z + 2 * nj), False, i == 15) for i in range(16)])
+        for j in range(nj):
+            a = n * (j % 2) + 32 * (j // 2)
+            act(R("dd", o + 32 * j, o + 32 * j + 32), ps(6, a, a + 32), F.Sign, scale=-1.0, bias=R("cmw", 16 * z + j, 16 * z + j + 1))
+        scan(R("de", o, o + 2 * n), R("RS32", 0, 2 * n), R("dd", o, o + 2 * n), A.max, A.mult)
+        ts(lost, R("de", o + 31, o + 2 * n, 32), 0.0, A.is_equal, STAY, A.mult)
+        tt(off, lost, cw, A.add)
+        tt(u_(7 + z, nj), off, tr(2, nj), A.min)
+        for b in range(nj // 2 - 1, -1, -1):
+            cp(IND(R("SWIN"), R("smu", 112 + 16 * z + 2 * b, 114 + 16 * z + 2 * b)), R(x, 32 * b, 32 * b + 32))
 
-    def dedup_s(nj):
-        act(R("rowS", 0, 32 * nj), R("ps6", 0, 32 * nj))
-
-    def dedup_b(nj, m, RJ):
-        n = 16 * nj
-        tt(R("dd", 0, 2 * n), IND(R("cmw", 0, nj), R(RJ)), R("rowS", 0, 2 * n), A.is_equal)
-        scan(R("de", 0, 2 * n), R("RS32", 0, 2 * n), R("dd", 0, 2 * n))
-        a = m[1][0][1]
-        for h in range(2):
-            tt(R("sml", 192 + h, 192 + nj, 2), R("de", n * h + 31, n * h + n, 32), R("smb", a + h, a + nj, 2), A.is_lt)
-        tt(f_(13, nj), f_(12, nj), f_(10, nj), A.mult)
-        tt(u_(7, nj), f_(13, nj), tr(2, nj), A.add)
-
-    def dedup_c(x, bs):
-        for b in bs:
-            cp(IND(R("SWIN"), R("smu", 112 + 2 * b, 114 + 2 * b)), R(x, 32 * b, 32 * b + 32))
-
-    def guest_a(t):
-        turn(R("GD%d" % t, 0, 6), 6, "TBg")
-        days(6, "TBg", "ps7", 0, 16, True, True)
-
-    def guest_b():
-        cp(R("cu", 0, Q), R("ps7", 0, Q))
-        mm(R("ps7", 0, Q), R("ID"), R("KCg"), True, False)
-        days(6, "TBg", "ps7", 0, 16, False, False)
-
-    def guest_c(t, ks):
-        for k in ks:
-            cmp_v(R("GX%d" % t), 6, k)
-            if k % 8 == 6:
-                ext(EC, "bits", Q * (k - 6), Q * (k + 2), "ps7", 6 * (k - 6), False, k == 14)
-
-    def guest_d(t):
-        cp(R("key", 0, 48), R("ps7", 48, 96))
-        tt(R("key", 48, 96), R("ps7", 0, 48), R("key", 0, 48), A.max)
-        tt(R("key", 0, 24), R("key", 48, 72), R("key", 72, 96), A.max)
-        tt(R("key", 24, 36), R("key", 0, 12), R("key", 12, 24), A.max)
-        tt(n_(4, 6), R("key", 24, 30), R("key", 30, 36), A.max)
-        moved(t, 6, n_(4, 6), mg, n_(0, 6))
-        dedup_a(6, mg, n_(0, 6), "MKg")
+    def guests(t):
+        h = int(t == RO - 1)
+        kv = GUEST[h]
+        turn(R("GD%d" % t, 0, 6), 256, 6, "TBg")
+        days(6, "TBg", 7, 0, 16, True)
+        cp(R("cu", 256, 352), ps(7, 0, Q))
+        days(6, "TBg", 7, 0, 16, False)
+        mm(ps(7, 0, Q), R("ID"), R("KCg", Q * h, Q * h + Q), False, False)
+        at = lambda k, n: IND(R("SWIN", 0, W), R("cu", 256 + 6 * k, 256 + 6 * (k + n)))
+        for k in range(0, kv, 2):
+            tt(R("bits", 4096 + Q * k, 4096 + Q * (k + 2)), at(k, 2), R("GX%d" % t), A.is_lt)
+        for k in range(kv, 16, 4):
+            n = min(4, 16 - k)
+            s, bank = R("SG", 1536 + Q * (k - kv), 1536 + Q * (k - kv + n)), 4 + (k - kv) // 4
+            mms([(ps(bank, Q * j, Q * (j + 2)), R("ID"), R("GX%d" % t), j == 0, False) for j in range(0, n, 2)])
+            act(s, at(k, n))
+            mm(ps(bank, 0, Q * n), R("NI"), s, False, True)
+            act(R("bits", 4096 + Q * k, 4096 + Q * (k + n)), ps(bank, 0, Q * n), F.Sign, bias=-TINY)
+        cs = [(EC, 0, 10), (EC, 10, 16)] if kv == 16 else [(EH, kv, 16), (EC, 0, kv)]
+        for j, (w, k0, k1) in enumerate(cs):
+            ext(w, "bits", 4096 + Q * k0, 4096 + Q * k1, 7, 6 * k0, False, j == 1)
+        K = lambda a, b: R("key", 256 + a, 256 + b)
+        act(K(0, 48), ps(7, 48, 96))
+        tt(K(48, 96), ps(7, 0, 48), K(0, 48), A.max)
+        tt(K(0, 24), K(48, 72), K(72, 96), A.max)
+        tt(K(24, 36), K(0, 12), K(12, 24), A.max)
+        tt(n_(4, 6), K(24, 30), K(30, 36), A.max)
+        ts(mg, n_(4, 6), R("thr", t, t + 1), A.is_lt, STAY, A.mult)
+        settle(6, n_(4, 6), mg, "MKg", "GX%d" % t, 1)
 
     for t in range(RO):
-        last = t == RO - 1
-        a1, a2 = CUT[min(t, 1)]
-        b1, b2 = CUT3[min(t, 1)]
-        m1, m2 = (a1 + V) // 32 * 16, (a2 + V) // 32 * 16
-        if t == 0:
-            addends(1, m1)
-            for b in ("W2", "W3"):
-                dma(R(b, V, ROOT), R("BW", V, ROOT))
-            dbl_v(1, a1, m1, False)
-            dbl_s(1, 0, a1, "ps0")
-            anch("W2", a1, m1, "ps0")
-            consts2()
-            dbl_v(1, m1, V)
-            anch("W2", 0, a1, "ps0")
-            candidates(1)
-        else:
-            addends(1, a1)
-            ghosts_in(t - 1, ["W2", "W3"])
-            dbl_s(1, 0, a1 // 32 * 16, "ps0")
-            refuse_d(t - 1)
-            dedup_s(16)
-            dbl_s(1, a1 // 32 * 16, a1, "ps0")
-            parity_b(t - 1)
-            dedup_b(16, mv, "RJ")
-            dbl_v(1, a1, m1)
-            anch("W2", a1, m1, "ps0")
-            dedup_c("xB", (7, 6, 5, 4))
-            anch("W2", 0, a1, "ps0")
-            dbl_v(1, m1, V)
-        anch("W2", m1, V, "ps1")
-        addends(2, a2, m1)
-        addends(2, m1)
-        lst("PL1", 0, m1, "ps0")
-        dbl_s(2, 0, a2, "ps0")
+        cut = CUT["later" if t else "first"]
+        dates(cut)
         if t:
-            guest_a(t - 1)
-        dbl_v(2, a2, m2)
-        lst("PL1", m1, V, "ps1")
-        anch("W3", a2, m2, "ps0")
-        if t == 0:
-            consts3()
-        else:
-            guest_b()
-            dedup_c("xB", (3, 2, 1, 0))
-        anch("W3", 0, a2, "ps0")
-        dbl_v(2, m2, V)
-        anch("W3", m2, V, "ps1")
-        if t == 0:
-            candidates(2)
-        lst("PL2", 0, m2, "ps0")
-        g3("s", 0, b1)
-        own3(0); own3(1)
-        if t == 0:
-            g3("v", b1, 1536)
-            lst("PL2", m2, V, "ps1")
-            g3("s", 1536, b2)
-            e3(0, 1536, True)
-            g3("v", b2, V)
-            date(0)
-            e3(1536, V, True)
-            consts4()
-            consts5()
-        else:
-            guest_c(t - 1, (0, 2))
-            lst("PL2", m2, V, "ps1")
-            g3("s", 1536, b2)
-            guest_c(t - 1, range(4, 16, 2))
-            g3("v", b1, 1536)
-            guest_d(t - 1)
-            e3(0, 1536, True)
-            dedup_s(6)
-            g3("v", b2, V)
-            e3(1536, V, True)
-            dedup_b(6, mg, "RJg")
-            date(0)
-            dedup_c("GX%d" % (t - 1), (2, 1, 0))
-        beaten()
-        date(1)
-        beaten2()
-        if t == 0:
-            candidates(3)
-        compact(t)
-        if not last:
-            ghosts_b(t)
-        choose(t)
-        if last:
-            moved(t, 16, n_(5), mv, n_(0))
-            refuse_a()
-            dedup_a(16, mv, n_(0), "MK") if False else None
-        else:
-            move_list()
-            if t == 0:
-                consts6()
-            moved(t, 16, n_(5), mv, n_(0))
-            move_off()
-            ghosts_in(t, ["BW"])
-            refuse_a()
-            dedup_a(16, mv, n_(0), "MK")
-            move_put()
-            anch("BW", 0, CUT[1][0] // 32 * 16, "ps0")
-            anch("BW", CUT[1][0] // 32 * 16, V, "ps1")
-            parity_a()
-            lst("PL", 0, CUT[1][0] // 32 * 16, "ps0")
-            refuse_b()
-            lst("PL", CUT[1][0] // 32 * 16, V, "ps1")
-            refuse_c(t)
-    dedup_a(16, mv, n_(0), "MK")
-    refuse_b()
-    dedup_s(16)
-    refuse_c(2); refuse_d(2)
-    dedup_b(16, mv, "RJ")
-    move_list()
-    dedup_c("xB", range(7, -1, -1))
-    guest_a(2)
-    move_off()
-    guest_b()
-    move_put()
-    guest_c(2, range(0, 16, 2))
-
-    def outs(b):
-        p = R(["ps0", "ps1", "ps3"][b % 3], rows=(0, 40))
+            guests(t - 1)
+        beaten(banks(cut[2])[2][1])
+        if t < RO - 1:
+            ghosts(t)
+        compact()
+        choose()
+        moves(t)
+        urge[0] = URGE
+        refuse(t)
+        urge[0] = 0.0
+        settle(16, n_(5), mv, "MK", "xB", 0)
+        if t < RO - 1:
+            parity(t)
+            lists("BW", "PL", [("", CUT["later"][0][0][1], 0), ("", V, 1)])
+    for b in range(6):
+        p = R("ps%d" % (b % 3), rows=(0, 40))
         mm(p, R("OC"), R("BW", 512 * b, 512 * b + 512), True, True)
         act(R("OUT", 512 * b, 512 * b + 512), p)
-
-    for b in range(4):
-        outs(b)
-    guest_d(2)
-    dedup_s(6)
-    for b in range(4, 6):
-        outs(b)
-    dedup_b(6, mg, "RJg")
+    guests(RO - 1)
     dma(hbm("yan"), R("OUT", rows=(0, 8)))
     dma(hbm("yof"), R("OUT", rows=(32, 40)))
-    dedup_c("GX2", (2, 1, 0))
     dma(hbm("ys"), R("SWIN", 0, W))
-    for s in total:
-        g.wait_ge(T.sem[s], total[s])
+    issue()

@@ -1,4 +1,4 @@
-from concourse.mybir import AluOpType as A, ActivationFunctionType as F
+from concourse.mybir import AluOpType as A, AxisListType, ActivationFunctionType as F
 
 V, W, NG, Q, RO = 3072, 2048, 896, 96, 3
 ROOT, BWW = 3968, 3984
@@ -16,14 +16,13 @@ def _sb(dt_, **kw):
         SCRATCH[n] = ("sbuf", [128] + (w if isinstance(w, list) else [w]), dt_)
 
 
-_sb(i3, anL=192, ofL=248, snL=56, tI=496, DI=192, DL=208, dg=384, smi=128, cpi=8, crow=160, crq=128, crg=128, kri=512, j16=16,
-    Dw=24)
+_sb(i3, anL=192, ofL=248, snL=56, tI=496, DI=192, DL=208, dg=384, smi=128, cpi=8, crow=16, kri=512, Dw=24)
 _sb(bf, pl=992, XR=3968, XW=3088, SWIN=2304, WK=2048, BW=4240, W2=BWW, W3=BWW, G3=V, Z1=V, Z2=V, dgb=384, bits=5632,
-    SG=2624, fl=192, binc=192, o1=352, o2=352, o3=256, OH=352, xB=528, smb=128, RD=256, EE=864, XA=2048, XLh=2048, XLl=2048,
-    BD=128, BDt=128, M1g=128, ID=128, NI=128, I7=128, I12=128, I16=128, IK=128, IO=128, IeP=160, IoP=160, ONE=192, OC=40,
-    krow=256, KQ=256, KL2=256, RST=256, RS32=512, KC=256, KCg=192, MK=512, MKg=192, sg=1024, dd=704, de=704,
-    GL0=NG, GL1=NG, GO0=NG, GO1=NG, GS0=192, GS1=192, GS2=192, GX0=192, GX1=192, GX2=192)
-_sb(f3, vf=16, sml=256, thr=4, ccol=32, BG=8, tr=48, CT=2048, PF=200, LW=40, GN=40, C32=32, key=352, cmw=32)
+    SG=2624, fl=192, binc=192, o1=352, o2=352, o3=256, OH=352, xB=528, smb=128, RD=256, EE=864, XA=2048, DG=2048,
+    BD=128, IdP=160, dgh=2048, dgl=512, j16=16, M1g=128, ID=128, NI=128, I7=128, I12=128, I16=128, IK=128, IO=128, IeP=160,
+    IoP=160, ONE=192, OC=40, krow=256, KQ=256, KL2=256, RST=256, RS32=512, KC=256, KCg=96, MK=512, MKg=192, sg=1024, dd=704,
+    de=704, GL0=NG, GL1=NG, GO0=NG, GO1=NG, GS0=192, GS1=192, GS2=192, GX0=192, GX1=192, GX2=192)
+_sb(f3, vf=16, sml=256, thr=4, ccol=16, tr=48, CT=2048, PF=200, LW=40, GN=40, C32=32, key=352, cmw=64)
 _sb(u1, SL=56, PL=192, PL1=192, PL2=192, DU=192, cu=352, smu=160, REP=16, GD0=8, GD1=8, GD2=8, GE=24)
 _sb(fh, CG=352, TB=[32, 8], TBg=[32, 3], Ds=352, cmh=64, kr5=512)
 SCRATCH["OUT"] = ("sbuf", [40, V], f3)
@@ -34,15 +33,14 @@ ALL = (1 << 128) - 1
 
 CUT = {"first": [[("S", 896, 0), ("V", 1792, 0), ("a", 2560, 1), ("p", V, 1)], [("S", 896, 0), ("a", 1792, 0), ("a", 2560, 1), ("p", V, 1)],
                  [("s", 768, 2), ("v", 1536, 2), ("v", 2304, 3), ("s", V, 3)]],
-       "later": [[("S", 1280, 0), ("a", 1920, 0), ("a", 2560, 1), ("p", V, 1)], [("S", 1280, 0), ("a", 1920, 0), ("a", 2560, 1), ("p", V, 1)],
-                 [("s", 1024, 2), ("v", 2048, 2), ("s", V, 3)]],
-       "beat": (384, 2560)}
-GUEST = (12, 10)
-CYCLE, GATHER, SCATTER, PE = 0.001, 1.56, 3.8, 0.0005
+       "later": [[("d", 1408, 0), ("a", 1920, 1), ("a", 2560, 1), ("p", V, 1)], [("d", 1408, 0), ("a", 1920, 1), ("a", 2560, 1), ("p", V, 1)],
+                 [("s", 1280, 2), ("v", 2048, 2), ("s", V, 3)]],
+       "beat": (320, 2048)}
+OWN, GUEST = 11, 12
+CYCLE, GATHER, SCATTER, PE = 0.0009, 1.56, 3.8, 0.0005
 FIXED = {"v": 0.05, "s": 0.065, "g": 0.15, "y": 0.05}
-WAKE, DMA, ISSUE, REMOTE = 0.06, 1.4, 0.6, 2.5
-URGE = 2.0
-PASSES, ORDER = 24, {}
+WAKE, DMA, ISSUE, REMOTE = 0.13, 2.0, 0.6, 3.2
+PASSES, AHEAD, HOLD, SWAPS, SLACK, ORDER = 16, 8, 0.1, 12000, 0.3, {}
 
 
 def rank_program(g, core, T, topo):
@@ -83,7 +81,7 @@ def rank_program(g, core, T, topo):
             return False
         return not (x[3] == y[3] > 1 and (x[1] - y[1]) % x[3])
 
-    calls, urge = [], [0.0]
+    calls = []
 
     def note(e, fn, rd, wr, cost, late=0.0, sem=None, after=()):
         k = len(calls)
@@ -103,7 +101,7 @@ def rank_program(g, core, T, topo):
             h.append((x, True, k))
         for x in rd:
             hist.setdefault(x[0], []).append((x, False, k))
-        calls.append({"e": e, "fn": fn, "dep": dep, "cost": cost, "urge": urge[0], "late": late, "sem": sem})
+        calls.append({"e": e, "fn": fn, "dep": dep, "cost": cost, "late": late, "sem": sem})
         return k
 
     def ap(a):
@@ -151,30 +149,39 @@ def rank_program(g, core, T, topo):
         total["loc"] = total.get("loc", 0) + len(e)
         return note("g", lambda q: q.remote_dma(out[0], in_[0], T.sem[sem], T.sem.loc, pid, rid, m), in_[1], [], ISSUE, sem="remote")
 
-    def deal(edges, way):
+    def deal(edges, way, due):
         n = len(calls)
         left = [0] * n
         for es in edges:
             for j, d in es:
                 left[j] += 1
-        at, free, out = [0.0] * n, {e: 0.0 for e in "vspgyr"}, []
+        at, free, out, was = [0.0] * n, {e: 0.0 for e in "vspgyr"}, [], [0.0] * n
         ready = {e: [k for k in range(n) if calls[k]["e"] == e and not left[k]] for e in free}
+        ahead = {e: sorted((k for k in range(n) if calls[k]["e"] == e and left[k]), key=lambda k: due[k]) for e in free}
         while len(out) < n:
             best = None
             for e, ks in ready.items():
                 if not ks:
                     continue
-                t = max(free[e], min(at[k] for k in ks))
-                k = max((k for k in ks if at[k] <= t), key=lambda k: way[k])
-                for j in ks:
-                    soon = t < at[j] < t + calls[k]["cost"] and way[j] > way[k]
-                    if soon and max(at[j] + way[j], at[j] + calls[j]["cost"] + way[k]) < t + calls[k]["cost"] + way[j]:
-                        k, t = j, at[j]
-                if best is None or t < best[0]:
-                    best = (t, k)
+                t0 = max(free[e], min(at[k] for k in ks))
+                take = None
+                for k in sorted((k for k in ks if at[k] <= t0), key=lambda k: -way[k])[:4]:
+                    end, t, first = t0 + calls[k]["cost"], t0, k
+                    for j in ks + ahead[e][:AHEAD]:
+                        x = due[j] if left[j] else at[j]
+                        if t0 < x < end and way[j] > way[k] and max(x + way[j], x + calls[j]["cost"] + way[k]) < end + way[j] - HOLD:
+                            if first == k and t == t0 or x < t:
+                                t, first = x, (k if left[j] else j)
+                    if take is None or t < take[0]:
+                        take = (t, first)
+                    if t == t0:
+                        break
+                if best is None or take[0] < best[0]:
+                    best = take
             t, k = best
             c = calls[k]
             ready[c["e"]].remove(k)
+            was[k] = at[k]
             at[k] = free[c["e"]] = t + c["cost"]
             out.append(k)
             for j, d in edges[k]:
@@ -182,7 +189,8 @@ def rank_program(g, core, T, topo):
                 left[j] -= 1
                 if not left[j]:
                     ready[calls[j]["e"]].append(j)
-        return out, at
+                    ahead[calls[j]["e"]].remove(j)
+        return out, was
 
     def order():
         n = len(calls)
@@ -190,12 +198,17 @@ def rank_program(g, core, T, topo):
         for k, c in enumerate(calls):
             for a, sem in c["dep"].items():
                 fwd[a].append((k, (calls[a]["late"] + WAKE) * sem))
-        way = [0.0] * n
+        way, due = [0.0] * n, [0.0] * n
         for k in range(n - 1, -1, -1):
             way[k] = calls[k]["cost"] + max([way[j] + d for j, d in fwd[k]] + [calls[k]["late"]])
         best = None
         for _ in range(PASSES):
-            out, at = deal(fwd, [w + c["urge"] for w, c in zip(way, calls)])
+            out, due = deal(fwd, way, due)
+            at, free = [0.0] * n, {}
+            for k in out:
+                at[k] = free[calls[k]["e"]] = max(at[k], free.get(calls[k]["e"], 0.0)) + calls[k]["cost"]
+                for j, d in fwd[k]:
+                    at[j] = max(at[j], at[k] + d)
             end = max(a + c["late"] for a, c in zip(at, calls))
             if best is None or end < best[0]:
                 best = (end, out)
@@ -206,7 +219,50 @@ def rank_program(g, core, T, topo):
                 tail[k] = c["cost"] + max(own, nx.get(c["e"], 0.0))
                 nx[c["e"]] = tail[k]
                 way[k] = (way[k] + c["cost"] + own) / 2
+        best = (best[0], better(best[1], fwd))
         return best[1]
+
+    def better(out, fwd):
+        n = len(calls)
+        dep = [[(a, (calls[a]["late"] + WAKE) * sem) for a, sem in c["dep"].items()] for c in calls]
+        cost, late, eng = [c["cost"] for c in calls], [c["late"] for c in calls], [c["e"] for c in calls]
+
+        def play(out):
+            at, why, free = [0.0] * n, [None] * n, {}
+            for k in out:
+                t, w = free.get(eng[k], (0.0, None))
+                q = True
+                for a, d in dep[k]:
+                    if at[a] + d > t:
+                        t, w, q = at[a] + d, a, False
+                at[k] = t + cost[k]
+                why[k] = (w, q)
+                free[eng[k]] = (at[k], k)
+            k = max(range(n), key=lambda k: at[k] + late[k])
+            return at[k] + late[k], k, why
+
+        end, last, why = play(out)
+        best = (end, out)
+        for step in range(SWAPS):
+            held, k = [], last
+            while k is not None:
+                if why[k][1] and why[k][0] is not None and why[k][0] not in calls[k]["dep"]:
+                    held.append((why[k][0], k))
+                k = why[k][0]
+            a, b = held[step * 7919 % 10007 % len(held)]
+            i, j = out.index(a), out.index(b)
+            need = {b}
+            for x in reversed(out[i:j]):
+                if any(y in need for y, d in fwd[x]):
+                    need.add(x)
+            if a not in need:
+                new = out[:i] + [x for x in out[i:j + 1] if x in need] + [x for x in out[i:j + 1] if x not in need] + out[j + 1:]
+                e2, k2, w2 = play(new)
+                if e2 <= end + SLACK * (step * 31 % 16) / 15 * (1 - step / SWAPS):
+                    out, end, last, why = new, e2, k2, w2
+                    if end < best[0]:
+                        best = (end, out)
+        return best[-1]
 
     def waits(e, deps):
         m = {}
@@ -291,8 +347,8 @@ def rank_program(g, core, T, topo):
         else:
             op("g", lambda q: q.iota(out[0], pat, base, cm, allow_small_or_imprecise_dtypes=True), out, [], (), 2.0)
 
-    def pick(n, src, pat, cmp, base=0, cm=0, fill=0.0):
-        op("g", lambda q: q.affine_select(T[n][:], src[0], pat, cmp, fill, base, cm), R(n), [src], (), 2.0)
+    def pick(out, src, pat, cmp, base=0, cm=0, fill=0.0):
+        op("g", lambda q: q.affine_select(out[0], src[0], pat, cmp, fill, base, cm), out, [src], (), 2.0)
 
     f_ = lambda k, nj=16: R("sml", 16 * k, 16 * k + nj)
     n_ = lambda k, nj=16: R("smi", 16 * k, 16 * k + nj)
@@ -323,32 +379,42 @@ def rank_program(g, core, T, topo):
     dma(R("ofL"), hbm("of0"))
     dma(R("WK"), hbm("wk"), R("anL")[1])
     iota(cpi(0), [[1, 1]], 0, 1)
-    iota(R("crow"), [[1, 160]], -16)
+    iota(R("crow"), [[1, 16]])
+    iota(R("ONE"), [[0, 192]], 1)
+    pick(R("ID"), R("ONE", 0, 128), [[-1, 128]], A.is_equal, 0, 1)
+    pick(R("IdP"), R("ONE", 0, 160), [[-1, 160]], A.is_equal, 16, 1)
+    pick(R("BD"), R("ONE", 0, 128), [[-16, 8], [0, 16]], A.is_ge, 0, 1)
+    pick(R("BD"), R("BD"), [[16, 8], [0, 16]], A.is_ge, 15, -1)
     iota(R("kri"), [[1, 512]])
+    cp(R("kr5"), R("kri"))
+    iota(R("krow"), [[1, 256]])
+    iota(R("dgh"), [[1, 64], [0, 32]])
+    iota(R("dgl"), [[0, 16], [1, 32]])
+    ms(R("EE"), 0.0)
     for l, z in enumerate(("Z1", "Z2")):
         cs = [c for k in ("first", "later") for e, c0, c1, b in spans(CUT[k][l]) if e == "a" for c in (c0, c1)]
-        iota(R(z, min(cs), max(cs)), [[0, max(cs) - min(cs)]])
+        if l:
+            iota(R(z, min(cs), max(cs)), [[0, max(cs) - min(cs)]])
+        else:
+            ms(R(z, min(cs), max(cs)), 0.0)
     iota(R("j16"), [[16, 16]])
     iota(R("KQ"), [[16, 16], [0, 16]])
     iota(R("XA"), [[0, 2048]], 1)
-    pick("RST", R("XA", 0, 256), [[0, 16], [1, 16]], A.is_gt)
-    pick("RS32", R("XA", 0, 512), [[0, 16], [1, 32]], A.is_equal, fill=-2.0)
-    iota(R("KC", 0, 160), [[-2048, 10], [0, 16]], 15 * 2048)
-    iota(R("KC", 160, 256), [[-2048, 6], [0, 16]], 5 * 2048 + 8 * 32768)
+    pick(R("RST"), R("XA", 0, 256), [[0, 16], [1, 16]], A.is_gt)
+    iota(R("RS32"), [[0, 16], [-8192, 32]], 8192)
+    iota(R("KC", 0, 16 * OWN), [[-2048, OWN], [0, 16]], 15 * 2048)
+    iota(R("KC", 16 * OWN, 256), [[-2048, 16 - OWN], [0, 16]], (15 - OWN) * 2048 + 8 * 32768)
     for n, nb in (("MK", 8), ("MKg", 3)):
-        iota(R(n), [[-16, 2], [0, nb], [1, 32]])
-    for h, kv in enumerate(GUEST):
-        iota(R("KCg", Q * h, Q * h + 6 * kv), [[-2048, kv], [0, 6]], 15 * 2048)
-        if kv < 16:
-            iota(R("KCg", Q * h + 6 * kv, Q * h + Q), [[-2048, 16 - kv], [0, 6]], (15 - kv) * 2048 + 8 * 32768)
-    for n, base, st in (("XLh", -2048, 1024), ("XLl", -10240, 1024), ("XA", 0, 0)):
-        pick(n, R("XA"), [[-1, 16], [-16, 8], [st, 16]], A.is_equal, base, 1)
+        iota(R(n), [[-16, 2], [0, nb], [1, 32]], 1)
+    iota(R("KCg", 0, 6 * GUEST), [[-2048, GUEST], [0, 6]], 15 * 2048)
+    iota(R("KCg", 6 * GUEST, Q), [[-2048, 16 - GUEST], [0, 6]], (15 - GUEST) * 2048 + 8 * 32768)
+    pick(R("XA"), R("XA"), [[-1, 16], [-16, 8], [0, 16]], A.is_equal, 0, 1)
     ms(R("XR"), 0.0)
     ms(R("pl", 192, 248), float(ROOT)); ms(R("pl", 440, 496), 0.0)
     cp(R("pl", 0, 192), R("anL"))
     tt(R("pl", 248, 440), R("anL"), R("pl", 0, 192), A.subtract)
     dma(R("XR", rows=(0, 128, 16)), R("pl", 0, 248))
-    dma(R("XR", rows=(1, 128, 16)), R("pl", 248, 496))
+    dma(R("XR", rows=(8, 128, 16)), R("pl", 248, 496))
     ts(R("tI", 0, 248), R("ofL"), 5, A.arith_shift_right)
     ts(R("tI", 248, 496), R("ofL"), 31, A.bitwise_and)
     cp(R("pl", 496, 744), R("tI", 0, 248))
@@ -361,72 +427,67 @@ def rank_program(g, core, T, topo):
         (cp if i % 3 < 2 else act)(R("BW", i, ROOT, 16), R("XR", i * 248, (i + 1) * 248))
     for w in ("W2", "W3"):
         dma(R(w, V, ROOT), R("BW", V, ROOT))
-    dma(R("XW", 0, V), hbm("x"), R("W2", 0, V)[1])
     ts(cpi(1), cpi(0), 15, A.bitwise_and)
-    ts(cpi(2), cpi(0), 4, A.arith_shift_right)
-    ts(cpi(4), cpi(0), 2, A.bitwise_and)
-    ts(cpi(3), cpi(2), 1, A.bitwise_and)
-    cp(R("ccol", 0, 3), R("cpi", 0, 3))
-    cp(col(7), cpi(3))
-    cp(col(12), cpi(4))
-    ts(col(3), col(1), 1.5, A.is_lt)
-    ts(col(5), col(1), 0.0, A.is_equal, float(ROOT), A.mult)
-    ts(col(6), col(7), -1.0, A.mult, 1.0, A.add)
-    ts(col(8), col(1), 11.5, A.is_lt)
-    ts(col(11), col(1), 7.5, A.is_lt, 31.0, A.mult)
-    ts(col(13), col(11), 1.0, A.add)
-    ts(col(4), col(12), 0.5, A.mult, col(13), A.mult)
-    ts(col(14), col(4), 0.5, A.is_gt)
+    ts(cpi(2), cpi(0), 2, A.bitwise_and)
+    ts(cpi(3), cpi(0), 16, A.bitwise_and)
+    cp(R("ccol", 0, 3), R("cpi", 1, 4))
+    cp(col(12), col(1))
+    cp(col(1), col(0))
+    ts(col(7), col(2), 1.0 / 16, A.mult)
+    ts(col(6), col(2), -1.0 / 16, A.mult, 1.0, A.add)
+    ts(cpi(4), cpi(0), 7, A.bitwise_and)
+    ts(col(3), cpi(4), 0.5, A.is_lt)
+    ts(col(5), col(0), 0.0, A.is_equal, float(ROOT), A.mult)
+    ts(col(8), col(0), 11.5, A.is_lt)
+    ts(col(11), col(0), 7.5, A.is_lt, 31.0, A.mult)
+    ts(col(14), col(12), 0.5, A.mult)
+    ts(col(4), col(11), 1.0, A.add, col(14), A.mult)
+    ts(col(15), col(0), -STAY, A.mult)
     cp(R("PL"), R("anL"))
     for b in ("BW", "W2", "W3"):
-        ts(R(b, ROOT, BWW), R("crow", 0, 16), 0.0, A.mult, col(5), A.add)
-    cp(R("kr5"), R("kri"))
-    ts(R("ID"), R("crow", 16, 144), col(0), A.is_equal)
-    for n, w in (("I7", 7.0), ("IK", -1024.0), ("NI", -1.0), ("I12", 12.0), ("I16", 16.0), ("IO", col(14)), ("M1g", -4096.0)):
-        ts(R(n), R("ID"), w, A.mult)
-    ms(R("EE"), 0.0)
-    ts(R("BG"), R("crow", 16, 24), col(2), A.is_equal)
+        act(R(b, ROOT, BWW), R("ONE", 0, 16), scale=col(5))
+    for n, w in (("I7", 7.0), ("IK", -1024.0), ("NI", -1.0), ("I12", 12.0), ("I16", 16.0), ("IO", col(14))):
+        act(R(n), R("ID"), scale=w)
     for n, w in ((EP, col(3)), (ES, col(4)), (E1, 1.0), (EI, col(1)), (EC, SC), (EH, SC / 2)):
-        ts(R("EE", 144 * n + 15, 144 * n + 143, 16), R("BG"), w, A.mult)
-    ts(R("crq"), R("crow", 16, 144), 15, A.bitwise_and)
-    ts(R("crg"), R("crow", 16, 144), 4, A.arith_shift_right)
-    ts(R("BD"), R("crg"), col(2), A.is_equal)
-    ts(R("BDt"), R("crq"), col(1), A.is_gt, -1.0, A.add)
-    tt(R("BDt"), R("BDt"), R("BD"), A.mult)
-    tt(R("M1g"), R("M1g"), R("BDt"), A.add)
-    cp(R("krow"), R("kr5", 0, 256))
-    ts(R("KL2"), R("kr5", 1, 257), col(8), A.mult)
-    ts(R("REP"), R("crow", 0, 16), 0.0, A.mult, col(1), A.add)
-    ts(R("KQ"), R("KQ"), col(1), A.add)
-    ts(R("IoP"), R("crow"), col(0), A.is_equal, col(7), A.mult)
-    ts(R("IeP"), R("crow"), col(0), A.is_equal, col(6), A.mult)
-    ts(tr(0), R("j16"), col(1), A.add)
-    ts(tr(1), tr(0), float(BWW), A.add)
-    ts(tr(2), tr(0), float(W), A.add)
+        act(R("EE", 144 * n + 15, 144 * n + 143, 16), R("BD", 0, 128, 16), scale=w)
+    act(R("M1g"), R("BD"), scale=-1.0)
+    pick(R("M1g"), R("M1g"), [[-1, 128]], A.is_ge, 0, 1)
+    pick(R("M1g"), R("M1g"), [[-1, 128]], A.not_equal, 0, 1, -4096.0)
+    act(R("KL2"), R("krow"), F.Identity, scale=col(8), bias=col(8))
+    ts(R("REP"), R("crow"), 0.0, A.mult, col(1), A.add)
+    act(R("KQ"), R("KQ"), F.Identity, bias=col(1))
+    act(R("IoP"), R("IdP"), scale=col(7))
+    act(R("IeP"), R("IdP"), scale=col(6))
+    act(tr(0), R("j16"), F.Identity, bias=col(1))
+    act(tr(1), tr(0), F.Identity, bias=float(BWW))
+    act(tr(2), tr(0), F.Identity, bias=float(W))
     for n in ("MK", "MKg"):
-        ts(R(n), R(n), col(1), A.is_ge, STAY, A.mult)
-    for x, c in ((R("ONE"), 1.0), (R("thr", 0, 1), 9 * SC), (R("XW", V, V + 16), NEG), (R("xB", 512, 528), NEG), (R("DL", 192, 208), 0),
+        act(R(n), R(n), F.Relu, scale=STAY, bias=col(15))
+    for x, c in ((R("thr", 0, 1), 9 * SC), (R("XW", V, V + 16), NEG), (R("xB", 512, 528), NEG), (R("DL", 192, 208), 0),
                  (R("PF", 192, 200), BIG), (R("LW", 32, 40), BIG), (R("GN", 32, 40), BIG), (R("C32", 0, 16), 0.0),
                  (R("C32", 16, 32), 4095.0), (R("Dw", 16, 24), 0), (R("GE"), 0), (R("OC"), 0.0)):
         ms(x, c)
-    ts(R("OC", 0, 8), R("BG"), col(3), A.mult)
-    ts(R("OC", 32, 40), R("BG"), col(4), A.mult)
+    act(R("OC", 0, 8), R("BD", 0, 128, 16), scale=col(3))
+    act(R("OC", 32, 40), R("BD", 0, 128, 16), scale=col(4))
+    iota(R("DG"), [[0, W]])
+    dma(R("DG", rows=(2, 128, 16)), R("dgh", rows=(2, 128, 16)))
+    for b in range(4):
+        dma(R("DG", 512 * b, 512 * b + 512, rows=(10, 128, 16)), R("dgl", rows=(10, 128, 16)))
     a, b = R("tI", 0, 56), R("tI", 64, 120)
     ts(a, R("snL"), 15, A.bitwise_and)
     ts(b, R("snL"), 4, A.arith_shift_right)
     ts(a, a, 192.0, A.mult)
     tt(R("SL"), a, b, A.add)
-
-    def candidates(b):
+    for b in range(4):
         c = (512 * b, 512 * b + 512)
         s, p = R("sg", 512 * (b % 2), 512 * (b % 2) + 512), ps(6 + b % 2)
-        mms([(p, R("I7"), R("WK", *c), True, False), (p, R("ID"), R("kr5"), False, True)])
+        mm(p, R("I7"), R("WK", *c), True, False)
+        mm(p, R("ID"), R("kr5"), False, True)
         act(s, p, F.Sign, bias=512.0 * b - 2047.5)
-        mms([(p, R("I7"), R("WK", *c), True, False), (p, R("ID"), R("kr5"), False, False), (p, R("IK"), s, False, True)])
+        mm(p, R("I7"), R("WK", *c), True, False)
+        mm(p, R("ID"), R("kr5"), False, False)
+        mm(p, R("IK"), s, False, True)
         act(R("CT", *c), p, F.Identity, bias=512.0 * b - 1024.0)
-
-    for b in range(4):
-        candidates(b)
 
     LV = (("BW", "PL", "Z1", "W2", "PL1", (2, 128, 8), (6, 128, 8)), ("W2", "PL1", "Z2", "W3", "PL2", (2, 128, 4), (3, 128, 4)))
 
@@ -436,28 +497,40 @@ def rank_program(g, core, T, topo):
             cp(R(p, c0 // 16, c1 // 16), ps(bank, c0 // 16, c1 // 16))
 
     def dates(cut):
+        done = []
         for (w, p, z, n, pn, src, dst), lv in zip(LV, cut):
             for e, c0, c1, bank in spans(lv):
                 x = IND(R(w, 0, BWW), R(p, c0 // 16, c1 // 16))
+                own = lambda: dma(R(n, c0, c1, rows=dst), R(w, c0, c1, rows=src))
                 if e == "a":
-                    dma(R(z, c0, c1, rows=src), R(w, c0, c1, rows=src))
+                    if (c0, c1) not in done:
+                        dma(R(z, c0, c1, rows=src), R(w, c0, c1, rows=src))
                     tt(R(n, c0, c1), x, R(z, c0, c1), A.add)
+                    if ("a", c1, bank) not in [(y[0], y[1], y[3]) for y in spans(lv)]:
+                        a0 = min(y[1] for y in spans(lv) if (y[0], y[3]) == (e, bank))
+                        ext(EP, n, a0, c1, bank, a0 // 16, True, True)
                 elif e == "p":
-                    y, s = ps(3, 0, c1 - c0), R("SG", 2112, 2112 + c1 - c0)
+                    y, s = ps(5, 0, c1 - c0), R("SG", 2112, 2112 + c1 - c0)
                     mm(y, R("IO"), R(w, c0, c1), True, False)
                     act(s, x)
                     mm(y, R("ID"), s, False, True)
                     act(R(n, c0, c1), y)
-                else:
-                    (cp if e in "vV" else act)(R(n, c0, c1), x)
-                if e in "sv":
-                    dma(R(n, c0, c1, rows=dst), R(w, c0, c1, rows=src))
-                if e == "p":
                     ext(EP, "SG", 2112, 2112 + c1 - c0, bank, c0 // 16, True, True)
+                elif e == "d":
+                    o = 1536 * (w == "W2")
+                    own()
+                    act(R("G3", o + c0, o + c1), x)
+                    for rows in (src, (0, 128, 8)):
+                        dma(R(n, c0, c1, rows=rows), R("G3", o + c0, o + c1, rows=rows))
+                    ext(EP, "G3", o + c0, o + c1, bank, c0 // 16, True, True)
                 else:
+                    (cp if e == "V" else act)(R(n, c0, c1), x)
                     ext(EP, n, c0, c1, bank, c0 // 16, True, True)
-                if e in "SV":
-                    dma(R(n, c0, c1, rows=dst), R(w, c0, c1, rows=src))
+                    if e == "V" and ("a", c0, c1) in [y[:3] for y in spans(cut[1])]:
+                        dma(R("Z2", c0, c1, rows=src), R(n, c0, c1, rows=src))
+                        dma(R("Z2", c0, c1, rows=dst), R(w, c0, c1, rows=src))
+                        done.append((c0, c1))
+                    own()
                 if c1 == banks(lv)[bank][1]:
                     b0 = banks(lv)[bank][0]
                     cp(R(pn, b0 // 16, c1 // 16), ps(bank, b0 // 16, c1 // 16))
@@ -474,7 +547,7 @@ def rank_program(g, core, T, topo):
     def beaten(m):
         a, z = CUT["beat"]
         at = lambda c0, c1: IND(R("SWIN", 0, W), R("DU", c0 // 16, c1 // 16))
-        for c0, c1 in ((3 * a, m), (m, z), (z, V)):
+        for c0, c1 in zip(sorted({3 * a, m, z}), sorted({m, z, V})):
             tt(R("bits", c0, c1), at(c0, c1), R("XW", c0, c1), A.is_le)
         for k in range(3):
             c, p = (a * k, a * k + a), ps(4 + k, 0, a)
@@ -482,7 +555,7 @@ def rank_program(g, core, T, topo):
             act(R("SG", *c), at(*c))
             mm(p, R("NI"), R("SG", *c), False, True)
             act(R("bits", *c), p, F.Sign, bias=TINY)
-        for cs, bank, least in (((3 * a, m, z, V), 0, 4.5), ((0, 2 * a, 3 * a), 1, -7.0)):
+        for cs, bank, least in ((sorted({3 * a, m, z, V}), 0, 4.5), ((0, 3 * a), 1, -7.0)):
             for c0, c1 in zip(cs, cs[1:]):
                 ext(E1, "bits", c0, c1, bank, c0 // 16, True, True)
             ts(R("fl", cs[0] // 16, cs[-1] // 16), ps(bank, cs[0] // 16, cs[-1] // 16), least, A.is_lt)
@@ -523,8 +596,8 @@ def rank_program(g, core, T, topo):
         cp(u_(3), ps(0, 0, 16))
         cp(b_(0), u_(3))
         tt(R("OH", 0, 256), IND(R("PF"), u_(3)), R("krow"), A.is_equal)
-        mm(ps(1, 0, 16), R("I16"), b_(0), True, False)
-        ext(EI, "OH", 0, 256, 1, 0, False, True)
+        ext(EI, "OH", 0, 256, 1, 0, True, False)
+        mm(ps(1, 0, 16), R("I16"), b_(0), False, True)
         tt(R("Ds", 0, 256), IND(R("DL"), u_(3)), R("OH", 0, 256), A.mult)
         ext(E1, "Ds", 0, 256, 2, 0, True, True)
         cp(vU, ps(1, 0, 16))
@@ -554,19 +627,20 @@ def rank_program(g, core, T, topo):
             cp(R("cu", 128 * h, 128 * h + 128), ps(2 + 5 * h, 0, 128))
             days(16, "TB", 3 * h, 8 * h, 8 * h + 8, False)
             mm(ps(3 * h, 0, 128), R("ID"), R("KC", 128 * h, 128 * h + 128), False, False)
-        x = R("xB", 0, 512)
-        at = lambda k: IND(R("SWIN", 0, W), R("cu", 16 * k, 16 * k + 32))
-        for k in (8, 0, 2, 4, 6):
-            tt(R("bits", 256 * k, 256 * k + 512), at(k), x, A.is_lt)
-        for a in range(3):
-            s = R("SG", 512 * a, 512 * a + 512)
-            mm(ps(4 + a), R("ID"), x, True, False)
-            act(s, at(10 + 2 * a))
-            mm(ps(4 + a), R("NI"), s, False, True)
-            act(R("bits", 2560 + 512 * a, 3072 + 512 * a), ps(4 + a), F.Sign, bias=-TINY)
-        ext(EC, "bits", 2048, 2560, 3, 0, False, False)
-        ext(EH, "bits", 2560, 3584, 3, 32, False, False)
-        ext(EH, "bits", 3584, 4096, 3, 96, False, True)
+        at = lambda k0, k1: IND(R("SWIN", 0, W), R("cu", 16 * k0, 16 * k1))
+        for k0 in list(range(8, OWN, 2)) + [0, 2, 4, 6]:
+            k1 = min(k0 + 2, OWN)
+            tt(R("bits", 256 * k0, 256 * k1), at(k0, k1), R("xB", 0, 256 * (k1 - k0)), A.is_lt)
+        for a, k0 in enumerate(range(OWN, 16, 2)):
+            k1 = min(k0 + 2, 16)
+            n = 256 * (k1 - k0)
+            s, p = R("SG", 512 * a, 512 * a + n), ps(4 + a, 0, n)
+            mm(p, R("ID"), R("xB", 0, n), True, False)
+            act(s, at(k0, k1))
+            mm(p, R("NI"), s, False, True)
+            act(R("bits", 256 * k0, 256 * k1), p, F.Sign, bias=-TINY)
+        ext(EC, "bits", 2048, 256 * OWN, 3, 0, False, False)
+        ext(EH, "bits", 256 * OWN, 4096, 3, 16 * (OWN - 8), False, True)
         ext(EC, "bits", 0, 1024, 0, 0, False, False)
         ext(EC, "bits", 1024, 2048, 0, 64, False, True)
         act(R("key", 0, 128), ps(3, 0, 128))
@@ -579,12 +653,9 @@ def rank_program(g, core, T, topo):
 
     def moves(t):
         ts(mv, n_(5), R("thr", t, t + 1), A.is_lt, STAY, A.mult)
-        ts(n_(2), n_(5), 5, A.arith_shift_right, 63, A.bitwise_and)
-        ts(n_(3), n_(5), 31, A.bitwise_and)
-        cp(R("smb", 48, 80), R("smi", 32, 64))
-        mms([(ps(2, i, 256, 16), R(("XLh", "XLl")[h], 128 * i, 128 * i + 128), b_(3 + h), h == 0, h == 1)
-             for i in range(16) for h in range(2)])
-        act(R("RD"), ps(2, 0, 256), F.Identity, bias=col(5))
+        ts(n_(0), n_(5), 2047, A.bitwise_and)
+        cp(u_(9), n_(0))
+        act(R("RD"), IND(R("DG"), u_(9)), F.Identity, bias=col(5))
         tt(f_(2), mv, R("vf"), A.add)
         tt(u_(4), f_(2), tr(1), A.min)
         cp(IND(R("BW"), u_(4)), R("RD"))
@@ -619,69 +690,65 @@ def rank_program(g, core, T, topo):
         ts(n_(1, 1), n_(1, 1), 13, A.arith_shift_right, 1, A.bitwise_and)
         ts(R("thr", t + 1, t + 2), n_(1, 1), SC, A.mult, 9 * SC, A.add)
 
-    def settle(nj, key, m, MK, x, z):
+    def settle(nj, c, m, MK, x, z):
         n, o = 16 * nj, 512 * z
-        c, lost, off, cw = n_(6 * z, nj), f_(8 + z, nj), f_(10 + z, nj), R("cmw", 16 * z, 16 * z + nj)
-        ts(c, key, 2047, A.bitwise_and)
+        lost, off, cw = f_(8 + z, nj), f_(10 + z, nj), R("cmw", 16 * z, 16 * z + nj)
         for y in (R("cmh", 32 * z, 32 * z + nj), R("cmh", 32 * z + nj, 32 * z + 2 * nj), cw):
             tt(y, c, m, A.add)
+        tt(off, cw, tr(2, nj), A.min)
+        ts(R("cmw", 32 + 16 * z, 32 + 16 * z + nj), c, -STAY, A.mult)
         mm(ps(6, 0, 2 * n), R("ID"), R(MK), True, False)
         mms([(ps(6, i, 2 * n, 16), R("XA", 128 * i, 128 * i + 128), R("cmh", 32 * z, 32 * z + 2 * nj), False, i == 15) for i in range(16)])
         for j in range(nj):
             a = n * (j % 2) + 32 * (j // 2)
-            act(R("dd", o + 32 * j, o + 32 * j + 32), ps(6, a, a + 32), F.Sign, scale=-1.0, bias=R("cmw", 16 * z + j, 16 * z + j + 1))
-        scan(R("de", o, o + 2 * n), R("RS32", 0, 2 * n), R("dd", o, o + 2 * n), A.max, A.mult)
-        ts(lost, R("de", o + 31, o + 2 * n, 32), 0.0, A.is_equal, STAY, A.mult)
-        tt(off, lost, cw, A.add)
-        tt(u_(7 + z, nj), off, tr(2, nj), A.min)
+            act(R("dd", o + 32 * j, o + 32 * j + 32), ps(6, a, a + 32), F.Abs, scale=STAY,
+                bias=R("cmw", 32 + 16 * z + j, 32 + 16 * z + j + 1))
+        scan(R("de", o, o + 2 * n), R("RS32", 0, 2 * n), R("dd", o, o + 2 * n), A.max, A.min)
+        tt(lost, tr(2, nj), R("de", o + 31, o + 2 * n, 32), A.subtract)
+        tt(u_(7 + z, nj), lost, off, A.max)
         for b in range(nj // 2 - 1, -1, -1):
             cp(IND(R("SWIN"), R("smu", 112 + 16 * z + 2 * b, 114 + 16 * z + 2 * b)), R(x, 32 * b, 32 * b + 32))
 
     def guests(t):
-        h = int(t == RO - 1)
-        kv = GUEST[h]
+        kv, n = GUEST, 16 - GUEST
         turn(R("GD%d" % t, 0, 6), 256, 6, "TBg")
         days(6, "TBg", 7, 0, 16, True)
         cp(R("cu", 256, 352), ps(7, 0, Q))
         days(6, "TBg", 7, 0, 16, False)
-        mm(ps(7, 0, Q), R("ID"), R("KCg", Q * h, Q * h + Q), False, False)
+        mm(ps(7, 0, Q), R("ID"), R("KCg"), False, False)
         at = lambda k, n: IND(R("SWIN", 0, W), R("cu", 256 + 6 * k, 256 + 6 * (k + n)))
         for k in range(0, kv, 2):
             tt(R("bits", 4096 + Q * k, 4096 + Q * (k + 2)), at(k, 2), R("GX%d" % t), A.is_lt)
-        for k in range(kv, 16, 4):
-            n = min(4, 16 - k)
-            s, bank = R("SG", 1536 + Q * (k - kv), 1536 + Q * (k - kv + n)), 4 + (k - kv) // 4
-            mms([(ps(bank, Q * j, Q * (j + 2)), R("ID"), R("GX%d" % t), j == 0, False) for j in range(0, n, 2)])
-            act(s, at(k, n))
-            mm(ps(bank, 0, Q * n), R("NI"), s, False, True)
-            act(R("bits", 4096 + Q * k, 4096 + Q * (k + n)), ps(bank, 0, Q * n), F.Sign, bias=-TINY)
-        cs = [(EC, 0, 10), (EC, 10, 16)] if kv == 16 else [(EH, kv, 16), (EC, 0, kv)]
-        for j, (w, k0, k1) in enumerate(cs):
-            ext(w, "bits", 4096 + Q * k0, 4096 + Q * k1, 7, 6 * k0, False, j == 1)
-        K = lambda a, b: R("key", 256 + a, 256 + b)
-        act(K(0, 48), ps(7, 48, 96))
-        tt(K(48, 96), ps(7, 0, 48), K(0, 48), A.max)
-        tt(K(0, 24), K(48, 72), K(72, 96), A.max)
-        tt(K(24, 36), K(0, 12), K(12, 24), A.max)
-        tt(n_(4, 6), K(24, 30), K(30, 36), A.max)
-        ts(mg, n_(4, 6), R("thr", t, t + 1), A.is_lt, STAY, A.mult)
-        settle(6, n_(4, 6), mg, "MKg", "GX%d" % t, 1)
+        s = R("SG", 1536, 1536 + Q * n)
+        mms([(ps(4, Q * j, Q * (j + 2)), R("ID"), R("GX%d" % t), j == 0, False) for j in range(0, n, 2)])
+        act(s, at(kv, n))
+        mm(ps(4, 0, Q * n), R("NI"), s, False, True)
+        act(R("bits", 4096 + Q * kv, 4096 + Q * 16), ps(4, 0, Q * n), F.Sign, bias=-TINY)
+        ext(EH, "bits", 4096 + Q * kv, 4096 + Q * 16, 7, 6 * kv, False, False)
+        ext(EC, "bits", 4096, 4096 + Q * kv, 7, 0, False, True)
+        for j in range(6):
+            y, x = R("key", 256 + j, 257 + j), ps(7, j, Q, 6)
+            op("v", lambda q, y=y, x=x: q.tensor_reduce(y[0], x[0], AxisListType.X, A.max), y, [x])
+        cp(n_(4, 6), R("key", 256, 262))
+        ts(mg, R("key", 256, 262), R("thr", t, t + 1), A.is_lt, STAY, A.mult)
+        ts(n_(6, 6), n_(4, 6), 2047, A.bitwise_and)
+        settle(6, n_(6, 6), mg, "MKg", "GX%d" % t, 1)
 
     for t in range(RO):
         cut = CUT["later" if t else "first"]
         dates(cut)
         if t:
             guests(t - 1)
+        else:
+            dma(R("XW", 0, V), hbm("x"), R("W2", 0, V)[1])
         beaten(banks(cut[2])[2][1])
         if t < RO - 1:
             ghosts(t)
         compact()
         choose()
         moves(t)
-        urge[0] = URGE
         refuse(t)
-        urge[0] = 0.0
-        settle(16, n_(5), mv, "MK", "xB", 0)
+        settle(16, n_(0), mv, "MK", "xB", 0)
         if t < RO - 1:
             parity(t)
             lists("BW", "PL", [("", CUT["later"][0][0][1], 0), ("", V, 1)])

from concourse.mybir import AluOpType as A, AxisListType, ActivationFunctionType as F

V, W, NG, Q, RO = 3072, 2048, 896, 96, 3
ROOT, BWW = 3968, 3984
NEG = -4194304.0
BIG = 1048576.0
SC = 32768.0
STAY = 8192.0
TINY = 2.0 ** -120
bf, f3, i3, u1, fh = "bfloat16", "float32", "int32", "uint16", "float16"
SCRATCH = {}


def _sb(dt_, **kw):
    for n, w in kw.items():
        SCRATCH[n] = ("sbuf", [128] + (w if isinstance(w, list) else [w]), dt_)


_sb(i3, anL=192, ofL=248, snL=56, tI=496, DI=192, DL=208, dg=384, smi=128, cpi=8, crow=16, kri=512, Dw=24)
_sb(bf, pl=992, XR=3968, XW=3088, SWIN=2304, WK=2048, BW=4240, W2=BWW, W3=BWW, G3=V, Z1=V, Z2=V, dgb=384, bits=5632,
    SG=2624, fl=192, binc=192, o1=352, o2=352, o3=256, OH=352, xB=528, smb=128, RD=256, EE=864, XA=2048, DG=2048,
    BD=128, IdP=160, dgh=2048, dgl=512, j16=16, M1g=128, ID=128, NI=128, I7=128, I12=128, I16=128, IK=128, IO=128, IeP=160,
    IoP=160, ONE=192, OC=40, krow=256, KQ=256, KL2=256, RST=256, RS32=512, KC=256, KCg=96, MK=512, MKg=192, sg=1024, dd=704,
    de=704, GL0=NG, GL1=NG, GO0=NG, GO1=NG, GS0=192, GS1=192, GS2=192, GX0=192, GX1=192, GX2=192)
_sb(f3, vf=16, sml=256, thr=4, ccol=16, tr=48, CT=2048, PF=200, LW=40, GN=40, C32=32, key=352, cmw=64)
_sb(u1, SL=56, PL=192, PL1=192, PL2=192, DU=192, cu=352, smu=160, REP=16, GD0=8, GD1=8, GD2=8, GE=24)
_sb(fh, CG=352, TB=[32, 8], TBg=[32, 3], Ds=352, cmh=64, kr5=512)
SCRATCH["OUT"] = ("sbuf", [40, V], f3)
for _b in range(8):
    SCRATCH["ps%d" % _b] = ("psum", [128, 512], f3)
SEMAPHORES = ["sv", "ss", "sp", "sg", "loc", "gh0", "gh1", "gu0", "gu1", "gu2", "gd0", "gd1", "gd2"] + ["d%d" % k for k in range(90)]
ALL = (1 << 128) - 1

CUT = {"first": [[("S", 896, 0), ("V", 1792, 0), ("a", 2560, 1), ("p", V, 1)], [("S", 896, 0), ("a", 1792, 0), ("a", 2560, 1), ("p", V, 1)],
                 [("s", 768, 2), ("v", 1536, 2), ("v", 2304, 3), ("s", V, 3)]],
       "later": [[("d", 1408, 0), ("a", 1920, 1), ("a", 2560, 1), ("p", V, 1)], [("d", 1408, 0), ("a", 1920, 1), ("a", 2560, 1), ("p", V, 1)],
                 [("s", 1280, 2), ("v", 2048, 2), ("s", V, 3)]],
       "beat": (320, 2048)}
OWN, GUEST = 11, 12
CYCLE, GATHER, SCATTER, PE = 0.0009, 1.56, 3.8, 0.0005
FIXED = {"v": 0.05, "s": 0.065, "g": 0.15, "y": 0.05}
WAKE, DMA, ISSUE, REMOTE = 0.13, 2.0, 0.6, 3.2
PASSES, AHEAD, HOLD, SWAPS, SLACK, ORDER = 16, 8, 0.1, 12000, 0.3, {}


def rank_program(g, core, T, topo):
    r = T.rank_of(core)
    if r is None:
        return
    cores = T.cores
    N = len(cores)
    ENG = {"v": g.vector, "s": g.scalar, "p": g.tensor, "g": g, "y": g.sync}
    SEM = {"v": "sv", "s": "ss", "p": "sp", "g": "sg"}
    cnt = {"v": 0, "s": 0, "p": 0, "g": 0}
    seen = {e: {} for e in ENG}
    know = {}
    hist = {}
    total = {}

    def R(n, a=0, b=None, s=1, rows=None):
        w = T[n].shape[1]
        b = w if b is None else b
        rs = slice(None) if rows is None else slice(*rows)
        m = ALL
        if rows is not None:
            m = 0
            for p in range(T[n].shape[0])[rs]:
                m |= 1 << p
        return (T[n][rs, a:b:s] if s > 1 else T[n][rs, a:b], [(n, a, a + (b - a - 1) // s * s, s, m)])

    def R3(n, ap):
        return (ap, [(n, 0, 1 << 20, 1, ALL)])

    def IND(w, o):
        return (w[0].indirect(o[0]), w[1], o[1])

    def meet(x, y):
        if x[0][:2] == "ps":
            return True
        if x[2] < y[1] or y[2] < x[1] or not x[4] & y[4]:
            return False
        return not (x[3] == y[3] > 1 and (x[1] - y[1]) % x[3])

    calls = []

    def note(e, fn, rd, wr, cost, late=0.0, sem=None, after=()):
        k = len(calls)
        dep = {a: False for a in after}
        for xs, write in ((rd, False), (wr, True)):
            for x in xs:
                for y, w, a in hist.get(x[0], ()):
                    q = calls[a]["e"]
                    if (w or write or (x[0][:2] == "ps" and q != e)) and meet(x, y):
                        dep[a] = not q == e == "p"
        for x in wr:
            h = hist.setdefault(x[0], [])
            if x[0][:2] == "ps":
                h[:] = []
            elif x[3] == 1:
                h[:] = [y for y in h if not (x[1] <= y[0][1] and y[0][2] <= x[2] and y[0][4] & ~x[4] == 0)]
            h.append((x, True, k))
        for x in rd:
            hist.setdefault(x[0], []).append((x, False, k))
        calls.append({"e": e, "fn": fn, "dep": dep, "cost": cost, "late": late, "sem": sem})
        return k

    def ap(a):
        return a[0] if isinstance(a, tuple) else a

    def elems(a):
        n = 1
        for d in a.shape[1:]:
            n *= d
        return n

    def op(e, fn, out, ins, more=(), rate=1.0):
        ins = [a for a in ins if isinstance(a, tuple)]
        rd = [x for a in ins for x in a[1] + (a[2] if len(a) > 2 else [])] + (out[2] if len(out) > 2 else [])
        wide = [a for a in ins + [out] if len(a) == 2 and elems(a[0]) > 1]
        n = max([elems(a[0]) for a in wide] + [1])
        if len(out) > 2:
            rate = SCATTER
        elif any(len(a) > 2 for a in ins):
            rate = GATHER
        elif e == "v" and all(SCRATCH[a[1][0][0]][2] in (bf, fh, u1) for a in wide):
            rate /= 2
        note(e, fn, rd, out[1] + list(more), FIXED[e] + CYCLE * rate * n)

    def dma(out, in_, after=()):
        a = out if out[1] else in_
        by = elems(a[0]) * a[0].shape[0] * (2 if SCRATCH[a[1][0][0]][2] == bf else 4)
        note("y", lambda q: q.dma_start(out[0], in_[0]), in_[1] + list(after), out[1], FIXED["y"], DMA + by / 3e5)

    def hbm(n):
        return (T[n][:], [])

    def engs(src, dst):
        return topo.engines(src, dst)[:8]

    def arrive(sem, n, t, sends):
        note("r", None, [], R(t)[1], 0.0, REMOTE, (sem, n), sends)

    def send(out, in_, dst, sem):
        rid, pid, _ = topo.addr(dst)
        e = engs(core, dst)
        m = 0
        for k in e:
            m |= 1 << k
        total["loc"] = total.get("loc", 0) + len(e)
        return note("g", lambda q: q.remote_dma(out[0], in_[0], T.sem[sem], T.sem.loc, pid, rid, m), in_[1], [], ISSUE, sem="remote")

    def deal(edges, way, due):
        n = len(calls)
        left = [0] * n
        for es in edges:
            for j, d in es:
                left[j] += 1
        at, free, out, was = [0.0] * n, {e: 0.0 for e in "vspgyr"}, [], [0.0] * n
        ready = {e: [k for k in range(n) if calls[k]["e"] == e and not left[k]] for e in free}
        ahead = {e: sorted((k for k in range(n) if calls[k]["e"] == e and left[k]), key=lambda k: due[k]) for e in free}
        while len(out) < n:
            best = None
            for e, ks in ready.items():
                if not ks:
                    continue
                t0 = max(free[e], min(at[k] for k in ks))
                take = None
                for k in sorted((k for k in ks if at[k] <= t0), key=lambda k: -way[k])[:4]:
                    end, t, first = t0 + calls[k]["cost"], t0, k
                    for j in ks + ahead[e][:AHEAD]:
                        x = due[j] if left[j] else at[j]
                        if t0 < x < end and way[j] > way[k] and max(x + way[j], x + calls[j]["cost"] + way[k]) < end + way[j] - HOLD:
                            if first == k and t == t0 or x < t:
                                t, first = x, (k if left[j] else j)
                    if take is None or t < take[0]:
                        take = (t, first)
                    if t == t0:
                        break
                if best is None or take[0] < best[0]:
                    best = take
            t, k = best
            c = calls[k]
            ready[c["e"]].remove(k)
            was[k] = at[k]
            at[k] = free[c["e"]] = t + c["cost"]
            out.append(k)
            for j, d in edges[k]:
                at[j] = max(at[j], at[k] + d)
                left[j] -= 1
                if not left[j]:
                    ready[calls[j]["e"]].append(j)
                    ahead[calls[j]["e"]].remove(j)
        return out, was

    def order():
        n = len(calls)
        fwd = [[] for _ in range(n)]
        for k, c in enumerate(calls):
            for a, sem in c["dep"].items():
                fwd[a].append((k, (calls[a]["late"] + WAKE) * sem))
        way, due = [0.0] * n, [0.0] * n
        for k in range(n - 1, -1, -1):
            way[k] = calls[k]["cost"] + max([way[j] + d for j, d in fwd[k]] + [calls[k]["late"]])
        best = None
        for _ in range(PASSES):
            out, due = deal(fwd, way, due)
            at, free = [0.0] * n, {}
            for k in out:
                at[k] = free[calls[k]["e"]] = max(at[k], free.get(calls[k]["e"], 0.0)) + calls[k]["cost"]
                for j, d in fwd[k]:
                    at[j] = max(at[j], at[k] + d)
            end = max(a + c["late"] for a, c in zip(at, calls))
            if best is None or end < best[0]:
                best = (end, out)
            tail, nx = [0.0] * n, {}
            for k in reversed(out):
                c = calls[k]
                own = max([tail[j] + d for j, d in fwd[k]] + [c["late"]])
                tail[k] = c["cost"] + max(own, nx.get(c["e"], 0.0))
                nx[c["e"]] = tail[k]
                way[k] = (way[k] + c["cost"] + own) / 2
        best = (best[0], better(best[1], fwd))
        return best[1]

    def better(out, fwd):
        n = len(calls)
        dep = [[(a, (calls[a]["late"] + WAKE) * sem) for a, sem in c["dep"].items()] for c in calls]
        cost, late, eng = [c["cost"] for c in calls], [c["late"] for c in calls], [c["e"] for c in calls]

        def play(out):
            at, why, free = [0.0] * n, [None] * n, {}
            for k in out:
                t, w = free.get(eng[k], (0.0, None))
                q = True
                for a, d in dep[k]:
                    if at[a] + d > t:
                        t, w, q = at[a] + d, a, False
                at[k] = t + cost[k]
                why[k] = (w, q)
                free[eng[k]] = (at[k], k)
            k = max(range(n), key=lambda k: at[k] + late[k])
            return at[k] + late[k], k, why

        end, last, why = play(out)
        best = (end, out)
        for step in range(SWAPS):
            held, k = [], last
            while k is not None:
                if why[k][1] and why[k][0] is not None and why[k][0] not in calls[k]["dep"]:
                    held.append((why[k][0], k))
                k = why[k][0]
            a, b = held[step * 7919 % 10007 % len(held)]
            i, j = out.index(a), out.index(b)
            need = {b}
            for x in reversed(out[i:j]):
                if any(y in need for y, d in fwd[x]):
                    need.add(x)
            if a not in need:
                new = out[:i] + [x for x in out[i:j + 1] if x in need] + [x for x in out[i:j + 1] if x not in need] + out[j + 1:]
                e2, k2, w2 = play(new)
                if e2 <= end + SLACK * (step * 31 % 16) / 15 * (1 - step / SWAPS):
                    out, end, last, why = new, e2, k2, w2
                    if end < best[0]:
                        best = (end, out)
        return best[-1]

    def waits(e, deps):
        m = {}
        for sem, val in deps:
            if seen[e].get(sem, 0) < val:
                m[sem] = max(m.get(sem, 0), val)
        for sem, val in list(m.items()):
            for s2, v2 in m.items():
                if s2 != sem and know.get((s2, v2), {}).get(sem, 0) >= val:
                    m[sem] = 0
        for sem, val in m.items():
            if val:
                ENG[e].wait_ge(T.sem[sem], val)
            for s2, v2 in know.get((sem, val), {}).items():
                seen[e][s2] = max(seen[e].get(s2, 0), v2)
            seen[e][sem] = max(seen[e].get(sem, 0), val)

    def issue():
        nd = 0
        if len(calls) not in ORDER:
            ORDER[len(calls)] = order()
        for k in ORDER[len(calls)]:
            c = calls[k]
            e = c["e"]
            if e == "r":
                total[c["sem"][0]] = c["sem"][1]
                continue
            waits(e, [calls[a]["sem"] for a, sem in c["dep"].items() if sem])
            x = c["fn"](ENG[e])
            if c["sem"] == "remote":
                continue
            if e == "y":
                c["sem"] = ("d%d" % nd, 16)
                nd += 1
                x.then_inc(T.sem[c["sem"][0]], 16)
            else:
                cnt[e] += 1
                c["sem"] = (SEM[e], cnt[e])
                x.then_inc(T.sem[SEM[e]], 1)
            know[c["sem"]] = dict(seen[e])
            total[c["sem"][0]] = c["sem"][1]
        for s in total:
            g.wait_ge(T.sem[s], total[s])

    def ts(out, in0, s1, op0, s2=None, op1=None):
        if op1 is None:
            op("v", lambda q: q.tensor_scalar(out[0], in0[0], ap(s1), None, op0), out, [in0, s1])
        else:
            op("v", lambda q: q.tensor_scalar(out[0], in0[0], ap(s1), ap(s2), op0, op1), out, [in0, s1, s2])

    def tt(out, a, b, o):
        op("v", lambda q: q.tensor_tensor(out[0], a[0], b[0], o), out, [a, b], (), 1.0 if a[1][0][0][:2] == "ps" else 2.0)

    def cp(out, in_):
        op("v", lambda q: q.tensor_copy(out[0], in_[0]), out, [in_])

    def ms(out, c):
        op("v", lambda q: q.memset(out[0], c), out, [])

    def scan(out, d0, d1, op0=A.mult, op1=A.add):
        op("v", lambda q: q.tensor_tensor_scan(out[0], d0[0], d1[0], 0.0, op0, op1), out, [d0, d1])

    def act(out, in_, f=F.Copy, **kw):
        more = kw["accum_out"][1] if "accum_out" in kw else []
        op("s", lambda q: q.activation(out[0], in_[0], f, **{k: ap(x) for k, x in kw.items()}), out,
           [in_] + [x for k, x in kw.items() if k != "accum_out"], more)

    def mms(ms_):
        def fn(q):
            for out, l, rh, st, sp in ms_:
                x = q.matmul(out[0], l[0], rh[0], st, sp)
            return x
        rd = sorted(set(x for m in ms_ for x in m[1][1] + m[2][1]))
        note("p", fn, rd, ms_[0][0][1], sum(max(64, elems(m[2][0])) for m in ms_) * PE)

    def mm(out, l, rh, st, sp):
        mms([(out, l, rh, st, sp)])

    def iota(out, pat, base=0, cm=0):
        if SCRATCH[out[1][0][0]][2] == i3:
            op("g", lambda q: q.iota(out[0], pat, base, cm), out, [], (), 2.0)
        else:
            op("g", lambda q: q.iota(out[0], pat, base, cm, allow_small_or_imprecise_dtypes=True), out, [], (), 2.0)

    def pick(out, src, pat, cmp, base=0, cm=0, fill=0.0):
        op("g", lambda q: q.affine_select(out[0], src[0], pat, cmp, fill, base, cm), out, [src], (), 2.0)

    f_ = lambda k, nj=16: R("sml", 16 * k, 16 * k + nj)
    n_ = lambda k, nj=16: R("smi", 16 * k, 16 * k + nj)
    b_ = lambda k, nj=16: R("smb", 16 * k, 16 * k + nj)
    u_ = lambda k, nj=16: R("smu", 16 * k, 16 * k + nj)
    tr = lambda k, nj=16: R("tr", 16 * k, 16 * k + nj)
    col = lambda k: R("ccol", k, k + 1)
    cpi = lambda k: R("cpi", k, k + 1)
    ps = lambda b, c0=0, c1=None, s=1: R("ps%d" % b, c0, c1, s)
    EP, ES, E1, EI, EC, EH = range(6)

    def sel(n, i):
        return R("EE", 144 * n + 15 - i, 144 * n + 143 - i)

    def ext(n, src, c0, c1, bank, o0, st, sp, i1=16):
        mms([(ps(bank, o0, o0 + (c1 - c0) // i1), sel(n, i), R(src, c0 + i, c1, i1), st and i == 0, sp and i == i1 - 1) for i in range(i1)])

    def spans(cut):
        return [(e, ([0] + [c[1] for c in cut])[k], c1, bank) for k, (e, c1, bank) in enumerate(cut)]

    def banks(cut):
        out = {}
        for e, c0, c1, bank in spans(cut):
            out[bank] = (out.get(bank, (c0, c1))[0], c1)
        return out

    dma(R("anL"), hbm("an0"))
    dma(R("ofL"), hbm("of0"))
    dma(R("WK"), hbm("wk"), R("anL")[1])
    iota(cpi(0), [[1, 1]], 0, 1)
    iota(R("crow"), [[1, 16]])
    iota(R("ONE"), [[0, 192]], 1)
    pick(R("ID"), R("ONE", 0, 128), [[-1, 128]], A.is_equal, 0, 1)
    pick(R("IdP"), R("ONE", 0, 160), [[-1, 160]], A.is_equal, 16, 1)
    pick(R("BD"), R("ONE", 0, 128), [[-16, 8], [0, 16]], A.is_ge, 0, 1)
    pick(R("BD"), R("BD"), [[16, 8], [0, 16]], A.is_ge, 15, -1)
    iota(R("kri"), [[1, 512]])
    cp(R("kr5"), R("kri"))
    iota(R("krow"), [[1, 256]])
    iota(R("dgh"), [[1, 64], [0, 32]])
    iota(R("dgl"), [[0, 16], [1, 32]])
    ms(R("EE"), 0.0)
    for l, z in enumerate(("Z1", "Z2")):
        cs = [c for k in ("first", "later") for e, c0, c1, b in spans(CUT[k][l]) if e == "a" for c in (c0, c1)]
        if l:
            iota(R(z, min(cs), max(cs)), [[0, max(cs) - min(cs)]])
        else:
            ms(R(z, min(cs), max(cs)), 0.0)
    iota(R("j16"), [[16, 16]])
    iota(R("KQ"), [[16, 16], [0, 16]])
    iota(R("XA"), [[0, 2048]], 1)
    pick(R("RST"), R("XA", 0, 256), [[0, 16], [1, 16]], A.is_gt)
    iota(R("RS32"), [[0, 16], [-8192, 32]], 8192)
    iota(R("KC", 0, 16 * OWN), [[-2048, OWN], [0, 16]], 15 * 2048)
    iota(R("KC", 16 * OWN, 256), [[-2048, 16 - OWN], [0, 16]], (15 - OWN) * 2048 + 8 * 32768)
    for n, nb in (("MK", 8), ("MKg", 3)):
        iota(R(n), [[-16, 2], [0, nb], [1, 32]], 1)
    iota(R("KCg", 0, 6 * GUEST), [[-2048, GUEST], [0, 6]], 15 * 2048)
    iota(R("KCg", 6 * GUEST, Q), [[-2048, 16 - GUEST], [0, 6]], (15 - GUEST) * 2048 + 8 * 32768)
    pick(R("XA"), R("XA"), [[-1, 16], [-16, 8], [0, 16]], A.is_equal, 0, 1)
    ms(R("XR"), 0.0)
    ms(R("pl", 192, 248), float(ROOT)); ms(R("pl", 440, 496), 0.0)
    cp(R("pl", 0, 192), R("anL"))
    tt(R("pl", 248, 440), R("anL"), R("pl", 0, 192), A.subtract)
    dma(R("XR", rows=(0, 128, 16)), R("pl", 0, 248))
    dma(R("XR", rows=(8, 128, 16)), R("pl", 248, 496))
    ts(R("tI", 0, 248), R("ofL"), 5, A.arith_shift_right)
    ts(R("tI", 248, 496), R("ofL"), 31, A.bitwise_and)
    cp(R("pl", 496, 744), R("tI", 0, 248))
    cp(R("pl", 744, 992), R("tI", 248, 496))
    dma(R("XR", rows=(2, 128, 16)), R("pl", 496, 744))
    dma(R("XR", rows=(10, 128, 16)), R("pl", 744, 992))
    dma(R("snL"), hbm("snd"), R("XR")[1])
    dma(R("SWIN", 0, W), hbm("s0"), R("XR")[1])
    for i in range(16):
        (cp if i % 3 < 2 else act)(R("BW", i, ROOT, 16), R("XR", i * 248, (i + 1) * 248))
    for w in ("W2", "W3"):
        dma(R(w, V, ROOT), R("BW", V, ROOT))
    ts(cpi(1), cpi(0), 15, A.bitwise_and)
    ts(cpi(2), cpi(0), 2, A.bitwise_and)
    ts(cpi(3), cpi(0), 16, A.bitwise_and)
    cp(R("ccol", 0, 3), R("cpi", 1, 4))
    cp(col(12), col(1))
    cp(col(1), col(0))
    ts(col(7), col(2), 1.0 / 16, A.mult)
    ts(col(6), col(2), -1.0 / 16, A.mult, 1.0, A.add)
    ts(cpi(4), cpi(0), 7, A.bitwise_and)
    ts(col(3), cpi(4), 0.5, A.is_lt)
    ts(col(5), col(0), 0.0, A.is_equal, float(ROOT), A.mult)
    ts(col(8), col(0), 11.5, A.is_lt)
    ts(col(11), col(0), 7.5, A.is_lt, 31.0, A.mult)
    ts(col(14), col(12), 0.5, A.mult)
    ts(col(4), col(11), 1.0, A.add, col(14), A.mult)
    ts(col(15), col(0), -STAY, A.mult)
    cp(R("PL"), R("anL"))
    for b in ("BW", "W2", "W3"):
        act(R(b, ROOT, BWW), R("ONE", 0, 16), scale=col(5))
    for n, w in (("I7", 7.0), ("IK", -1024.0), ("NI", -1.0), ("I12", 12.0), ("I16", 16.0), ("IO", col(14))):
        act(R(n), R("ID"), scale=w)
    for n, w in ((EP, col(3)), (ES, col(4)), (E1, 1.0), (EI, col(1)), (EC, SC), (EH, SC / 2)):
        act(R("EE", 144 * n + 15, 144 * n + 143, 16), R("BD", 0, 128, 16), scale=w)
    act(R("M1g"), R("BD"), scale=-1.0)
    pick(R("M1g"), R("M1g"), [[-1, 128]], A.is_ge, 0, 1)
    pick(R("M1g"), R("M1g"), [[-1, 128]], A.not_equal, 0, 1, -4096.0)
    act(R("KL2"), R("krow"), F.Identity, scale=col(8), bias=col(8))
    ts(R("REP"), R("crow"), 0.0, A.mult, col(1), A.add)
    act(R("KQ"), R("KQ"), F.Identity, bias=col(1))
    act(R("IoP"), R("IdP"), scale=col(7))
    act(R("IeP"), R("IdP"), scale=col(6))
    act(tr(0), R("j16"), F.Identity, bias=col(1))
    act(tr(1), tr(0), F.Identity, bias=float(BWW))
    act(tr(2), tr(0), F.Identity, bias=float(W))
    for n in ("MK", "MKg"):
        act(R(n), R(n), F.Relu, scale=STAY, bias=col(15))
    for x, c in ((R("thr", 0, 1), 9 * SC), (R("XW", V, V + 16), NEG), (R("xB", 512, 528), NEG), (R("DL", 192, 208), 0),
                 (R("PF", 192, 200), BIG), (R("LW", 32, 40), BIG), (R("GN", 32, 40), BIG), (R("C32", 0, 16), 0.0),
                 (R("C32", 16, 32), 4095.0), (R("Dw", 16, 24), 0), (R("GE"), 0), (R("OC"), 0.0)):
        ms(x, c)
    act(R("OC", 0, 8), R("BD", 0, 128, 16), scale=col(3))
    act(R("OC", 32, 40), R("BD", 0, 128, 16), scale=col(4))
    iota(R("DG"), [[0, W]])
    dma(R("DG", rows=(2, 128, 16)), R("dgh", rows=(2, 128, 16)))
    for b in range(4):
        dma(R("DG", 512 * b, 512 * b + 512, rows=(10, 128, 16)), R("dgl", rows=(10, 128, 16)))
    a, b = R("tI", 0, 56), R("tI", 64, 120)
    ts(a, R("snL"), 15, A.bitwise_and)
    ts(b, R("snL"), 4, A.arith_shift_right)
    ts(a, a, 192.0, A.mult)
    tt(R("SL"), a, b, A.add)
    for b in range(4):
        c = (512 * b, 512 * b + 512)
        s, p = R("sg", 512 * (b % 2), 512 * (b % 2) + 512), ps(6 + b % 2)
        mm(p, R("I7"), R("WK", *c), True, False)
        mm(p, R("ID"), R("kr5"), False, True)
        act(s, p, F.Sign, bias=512.0 * b - 2047.5)
        mm(p, R("I7"), R("WK", *c), True, False)
        mm(p, R("ID"), R("kr5"), False, False)
        mm(p, R("IK"), s, False, True)
        act(R("CT", *c), p, F.Identity, bias=512.0 * b - 1024.0)

    LV = (("BW", "PL", "Z1", "W2", "PL1", (2, 128, 8), (6, 128, 8)), ("W2", "PL1", "Z2", "W3", "PL2", (2, 128, 4), (3, 128, 4)))

    def lists(w, p, cut):
        for bank, (c0, c1) in banks(cut).items():
            ext(EP, w, c0, c1, bank, c0 // 16, True, True)
            cp(R(p, c0 // 16, c1 // 16), ps(bank, c0 // 16, c1 // 16))

    def dates(cut):
        done = []
        for (w, p, z, n, pn, src, dst), lv in zip(LV, cut):
            for e, c0, c1, bank in spans(lv):
                x = IND(R(w, 0, BWW), R(p, c0 // 16, c1 // 16))
                own = lambda: dma(R(n, c0, c1, rows=dst), R(w, c0, c1, rows=src))
                if e == "a":
                    if (c0, c1) not in done:
                        dma(R(z, c0, c1, rows=src), R(w, c0, c1, rows=src))
                    tt(R(n, c0, c1), x, R(z, c0, c1), A.add)
                    if ("a", c1, bank) not in [(y[0], y[1], y[3]) for y in spans(lv)]:
                        a0 = min(y[1] for y in spans(lv) if (y[0], y[3]) == (e, bank))
                        ext(EP, n, a0, c1, bank, a0 // 16, True, True)
                elif e == "p":
                    y, s = ps(5, 0, c1 - c0), R("SG", 2112, 2112 + c1 - c0)
                    mm(y, R("IO"), R(w, c0, c1), True, False)
                    act(s, x)
                    mm(y, R("ID"), s, False, True)
                    act(R(n, c0, c1), y)
                    ext(EP, "SG", 2112, 2112 + c1 - c0, bank, c0 // 16, True, True)
                elif e == "d":
                    o = 1536 * (w == "W2")
                    own()
                    act(R("G3", o + c0, o + c1), x)
                    for rows in (src, (0, 128, 8)):
                        dma(R(n, c0, c1, rows=rows), R("G3", o + c0, o + c1, rows=rows))
                    ext(EP, "G3", o + c0, o + c1, bank, c0 // 16, True, True)
                else:
                    (cp if e == "V" else act)(R(n, c0, c1), x)
                    ext(EP, n, c0, c1, bank, c0 // 16, True, True)
                    if e == "V" and ("a", c0, c1) in [y[:3] for y in spans(cut[1])]:
                        dma(R("Z2", c0, c1, rows=src), R(n, c0, c1, rows=src))
                        dma(R("Z2", c0, c1, rows=dst), R(w, c0, c1, rows=src))
                        done.append((c0, c1))
                    own()
                if c1 == banks(lv)[bank][1]:
                    b0 = banks(lv)[bank][0]
                    cp(R(pn, b0 // 16, c1 // 16), ps(bank, b0 // 16, c1 // 16))
        for e, c0, c1, bank in spans(cut[2]):
            (cp if e == "v" else act)(R("G3", c0, c1), IND(R("W3", 0, BWW), R("PL2", c0 // 16, c1 // 16)))
        for bank, (c0, c1) in banks(cut[2]).items():
            c = (c0 // 16, c1 // 16)
            ext(ES, "W3", c0, c1, bank, c[0], True, False)
            ext(ES, "G3", c0, c1, bank, c[0], False, True)
            cp(R("DI", *c), ps(bank, *c))
            ts(R("DL", *c), R("DI", *c), 2047, A.bitwise_and)
            cp(R("DU", *c), R("DL", *c))

    def beaten(m):
        a, z = CUT["beat"]
        at = lambda c0, c1: IND(R("SWIN", 0, W), R("DU", c0 // 16, c1 // 16))
        for c0, c1 in zip(sorted({3 * a, m, z}), sorted({m, z, V})):
            tt(R("bits", c0, c1), at(c0, c1), R("XW", c0, c1), A.is_le)
        for k in range(3):
            c, p = (a * k, a * k + a), ps(4 + k, 0, a)
            mm(p, R("ID"), R("XW", *c), True, False)
            act(R("SG", *c), at(*c))
            mm(p, R("NI"), R("SG", *c), False, True)
            act(R("bits", *c), p, F.Sign, bias=TINY)
        for cs, bank, least in ((sorted({3 * a, m, z, V}), 0, 4.5), ((0, 3 * a), 1, -7.0)):
            for c0, c1 in zip(cs, cs[1:]):
                ext(E1, "bits", c0, c1, bank, c0 // 16, True, True)
            ts(R("fl", cs[0] // 16, cs[-1] // 16), ps(bank, cs[0] // 16, cs[-1] // 16), least, A.is_lt)

    def ghosts(t):
        ts(R("dg", 0, 192), R("DL", 0, 192), 5, A.arith_shift_right)
        ts(R("dg", 192, 384), R("DL", 0, 192), 31, A.bitwise_and)
        for h in range(2):
            cp(R("dgb", 192 * h, 192 * h + 192), R("dg", 192 * h, 192 * h + 192))
            dma(R("XR", 0, V, rows=(2 + 8 * h, 128, 16)), R("dgb", 192 * h, 192 * h + 192))
        act(R("GO%d" % t), IND(R("XR", 0, V), R("SL")))
        ks = [send(R("GL%d" % t, 128 * (d - 1), 128 * d), R("GO%d" % t, 128 * (d - 1), 128 * d), cores[(r + d) % N], "gh%d" % t)
              for d in range(1, N)]
        arrive("gh%d" % t, sum(len(engs(cores[(r - d) % N], core)) for d in range(1, N)), "GL%d" % t, ks)
        for b in ("BW", "W2", "W3"):
            dma(R(b, V, ROOT, rows=(2, 128, 8)), R("GL%d" % t, rows=(2, 128, 8)))

    vU, DlU = u_(0), u_(1)

    def count16(win, o, n, out):
        tt(R("o1", o, o + n), IND(win, R("REP", 0, n // 16)), R("KQ", 0, n), A.is_le)
        scan(R("o2", o, o + n), R("RST", 0, n), R("o1", o, o + n))
        cp(out, R("o2", o + 15, o + n, 16))

    def compact():
        mm(ps(4, 0, 192), R("M1g"), R("fl"), True, False)
        scan(R("binc"), R("ONE"), R("fl"))
        mm(ps(3, 0, 16), R("BD"), R("binc", 11, 192, 12), True, True)
        ext(E1, "binc", 0, 192, 5, 0, True, True, 12)
        mm(ps(4, 0, 192), R("BD"), R("binc"), False, True)
        cp(R("LW", 0, 16), ps(3, 0, 16))
        act(R("LW", 16, 32), ps(5, 0, 16))
        act(R("PF", 0, 192), ps(4, 0, 192), F.Identity, bias=4095.0)
        count16(R("LW", 0, 16), 0, 256, u_(2))
        mm(ps(0, 0, 16), R("I12"), R("o2", 15, 256, 16), True, False)
        tt(R("o3"), IND(R("LW", 16, 40), u_(2)), R("KL2"), A.is_lt)
        ext(E1, "o3", 0, 256, 0, 0, False, True)
        cp(u_(3), ps(0, 0, 16))
        cp(b_(0), u_(3))
        tt(R("OH", 0, 256), IND(R("PF"), u_(3)), R("krow"), A.is_equal)
        ext(EI, "OH", 0, 256, 1, 0, True, False)
        mm(ps(1, 0, 16), R("I16"), b_(0), False, True)
        tt(R("Ds", 0, 256), IND(R("DL"), u_(3)), R("OH", 0, 256), A.mult)
        ext(E1, "Ds", 0, 256, 2, 0, True, True)
        cp(vU, ps(1, 0, 16))
        act(R("xB", 0, 256), IND(R("XW"), vU))
        act(R("xB", 256, 512), R("xB", 0, 256))
        cp(DlU, ps(2, 0, 16))
        cp(R("vf"), vU)
        cp(R("Dw", 0, 16), DlU)
        ts(f_(15), R("vf"), 3071.5, A.is_lt)

    def turn(D, o, nj, TBn):
        cp(R("CG", o, o + 16 * nj), IND(R("CT"), D))
        for b in range(nj // 2):
            x = R("CG", o + 32 * b, o + 32 * b + 32)
            op("v", lambda q, b=b, x=x: q.transpose(T[TBn][:, :, b], x[0]), (T[TBn][:, :, b], [(TBn, b, 1 << 20, 64, ALL)]), [x])

    def days(nj, TBn, bank, k0, k1, sp):
        n = (k1 - k0) * nj
        lo, hi = R3(TBn, T[TBn][:, k0:k1, :]), R3(TBn, T[TBn][:, 16 + k0:16 + k1, :])
        mms([(ps(bank, 0, n, 2), R("IeP", 16, 144), lo, True, False), (ps(bank, 0, n, 2), R("IeP", 0, 128), hi, False, False),
             (ps(bank, 1, n, 2), R("IoP", 32, 160), lo, False, False), (ps(bank, 1, n, 2), R("IoP", 16, 144), hi, False, sp)])

    def choose():
        turn(DlU, 0, 16, "TB")
        for h in (1, 0):
            days(16, "TB", 2 + 5 * h, 8 * h, 8 * h + 8, True)
            cp(R("cu", 128 * h, 128 * h + 128), ps(2 + 5 * h, 0, 128))
            days(16, "TB", 3 * h, 8 * h, 8 * h + 8, False)
            mm(ps(3 * h, 0, 128), R("ID"), R("KC", 128 * h, 128 * h + 128), False, False)
        at = lambda k0, k1: IND(R("SWIN", 0, W), R("cu", 16 * k0, 16 * k1))
        for k0 in list(range(8, OWN, 2)) + [0, 2, 4, 6]:
            k1 = min(k0 + 2, OWN)
            tt(R("bits", 256 * k0, 256 * k1), at(k0, k1), R("xB", 0, 256 * (k1 - k0)), A.is_lt)
        for a, k0 in enumerate(range(OWN, 16, 2)):
            k1 = min(k0 + 2, 16)
            n = 256 * (k1 - k0)
            s, p = R("SG", 512 * a, 512 * a + n), ps(4 + a, 0, n)
            mm(p, R("ID"), R("xB", 0, n), True, False)
            act(s, at(k0, k1))
            mm(p, R("NI"), s, False, True)
            act(R("bits", 256 * k0, 256 * k1), p, F.Sign, bias=-TINY)
        ext(EC, "bits", 2048, 256 * OWN, 3, 0, False, False)
        ext(EH, "bits", 256 * OWN, 4096, 3, 16 * (OWN - 8), False, True)
        ext(EC, "bits", 0, 1024, 0, 0, False, False)
        ext(EC, "bits", 1024, 2048, 0, 64, False, True)
        act(R("key", 0, 128), ps(3, 0, 128))
        tt(R("key", 128, 256), ps(0, 0, 128), R("key", 0, 128), A.max)
        tt(R("key", 0, 64), R("key", 128, 192), R("key", 192, 256), A.max)
        tt(R("key", 64, 96), R("key", 0, 32), R("key", 32, 64), A.max)
        tt(n_(5), R("key", 64, 80), R("key", 80, 96), A.max)

    mv, mg = b_(1), b_(2, 6)

    def moves(t):
        ts(mv, n_(5), R("thr", t, t + 1), A.is_lt, STAY, A.mult)
        ts(n_(0), n_(5), 2047, A.bitwise_and)
        cp(u_(9), n_(0))
        act(R("RD"), IND(R("DG"), u_(9)), F.Identity, bias=col(5))
        tt(f_(2), mv, R("vf"), A.add)
        tt(u_(4), f_(2), tr(1), A.min)
        cp(IND(R("BW"), u_(4)), R("RD"))

    def refuse(t):
        dst, src = cores[(r + 1 + t % (N - 1)) % N], cores[(r - 1 - t % (N - 1)) % N]
        tt(b_(5), f_(15), mv, A.min)
        scan(b_(6), R("ONE", 0, 16), b_(5))
        mms([(ps(4, 0, 16), R("BD"), b_(6), True, True), (ps(4, 16, 32), R("M1g"), b_(5), True, False),
             (ps(4, 16, 32), R("BD"), b_(6), False, True)])
        tt(R("GN", 0, 32), ps(4, 0, 32), R("C32"), A.add)
        count16(R("GN", 0, 16), 256, Q, u_(5, 6))
        tt(R("OH", 256, 352), IND(R("GN", 16, 40), u_(5, 6)), R("krow", 0, Q), A.is_equal)
        tt(R("Ds", 256, 352), IND(R("Dw"), u_(5, 6)), R("OH", 256, 352), A.mult)
        ext(E1, "Ds", 256, 352, 5, 0, True, True)
        mm(ps(4, 0, 6), R("I16"), R("o2", 271, 352, 16), True, False)
        ext(EI, "OH", 256, 352, 4, 0, False, True)
        cp(R("GE", 8 * t, 8 * t + 6), ps(5, 0, 6))
        k = send(R("GD%d" % t), R("GE", 8 * t, 8 * t + 8), dst, "gd%d" % t)
        arrive("gd%d" % t, len(engs(src, core)), "GD%d" % t, [k])
        cp(u_(6, 6), ps(4, 0, 6))
        G = "GS%d" % t
        act(R(G, 0, Q), IND(R("xB", 256, 528), u_(6, 6)))
        act(R(G, Q, 2 * Q), R(G, 0, Q))
        k = send(R("GX%d" % t), R(G), dst, "gu%d" % t)
        arrive("gu%d" % t, len(engs(src, core)), "GX%d" % t, [k])

    def parity(t):
        mm(ps(7, 0, 16), R("ONE", 0, 128), mv, True, True)
        act(f_(6), ps(7, 0, 16), accum_out=f_(7, 1))
        cp(n_(1, 1), f_(7, 1))
        ts(n_(1, 1), n_(1, 1), 13, A.arith_shift_right, 1, A.bitwise_and)
        ts(R("thr", t + 1, t + 2), n_(1, 1), SC, A.mult, 9 * SC, A.add)

    def settle(nj, c, m, MK, x, z):
        n, o = 16 * nj, 512 * z
        lost, off, cw = f_(8 + z, nj), f_(10 + z, nj), R("cmw", 16 * z, 16 * z + nj)
        for y in (R("cmh", 32 * z, 32 * z + nj), R("cmh", 32 * z + nj, 32 * z + 2 * nj), cw):
            tt(y, c, m, A.add)
        tt(off, cw, tr(2, nj), A.min)
        ts(R("cmw", 32 + 16 * z, 32 + 16 * z + nj), c, -STAY, A.mult)
        mm(ps(6, 0, 2 * n), R("ID"), R(MK), True, False)
        mms([(ps(6, i, 2 * n, 16), R("XA", 128 * i, 128 * i + 128), R("cmh", 32 * z, 32 * z + 2 * nj), False, i == 15) for i in range(16)])
        for j in range(nj):
            a = n * (j % 2) + 32 * (j // 2)
            act(R("dd", o + 32 * j, o + 32 * j + 32), ps(6, a, a + 32), F.Abs, scale=STAY,
                bias=R("cmw", 32 + 16 * z + j, 32 + 16 * z + j + 1))
        scan(R("de", o, o + 2 * n), R("RS32", 0, 2 * n), R("dd", o, o + 2 * n), A.max, A.min)
        tt(lost, tr(2, nj), R("de", o + 31, o + 2 * n, 32), A.subtract)
        tt(u_(7 + z, nj), lost, off, A.max)
        for b in range(nj // 2 - 1, -1, -1):
            cp(IND(R("SWIN"), R("smu", 112 + 16 * z + 2 * b, 114 + 16 * z + 2 * b)), R(x, 32 * b, 32 * b + 32))

    def guests(t):
        kv, n = GUEST, 16 - GUEST
        turn(R("GD%d" % t, 0, 6), 256, 6, "TBg")
        days(6, "TBg", 7, 0, 16, True)
        cp(R("cu", 256, 352), ps(7, 0, Q))
        days(6, "TBg", 7, 0, 16, False)
        mm(ps(7, 0, Q), R("ID"), R("KCg"), False, False)
        at = lambda k, n: IND(R("SWIN", 0, W), R("cu", 256 + 6 * k, 256 + 6 * (k + n)))
        for k in range(0, kv, 2):
            tt(R("bits", 4096 + Q * k, 4096 + Q * (k + 2)), at(k, 2), R("GX%d" % t), A.is_lt)
        s = R("SG", 1536, 1536 + Q * n)
        mms([(ps(4, Q * j, Q * (j + 2)), R("ID"), R("GX%d" % t), j == 0, False) for j in range(0, n, 2)])
        act(s, at(kv, n))
        mm(ps(4, 0, Q * n), R("NI"), s, False, True)
        act(R("bits", 4096 + Q * kv, 4096 + Q * 16), ps(4, 0, Q * n), F.Sign, bias=-TINY)
        ext(EH, "bits", 4096 + Q * kv, 4096 + Q * 16, 7, 6 * kv, False, False)
        ext(EC, "bits", 4096, 4096 + Q * kv, 7, 0, False, True)
        for j in range(6):
            y, x = R("key", 256 + j, 257 + j), ps(7, j, Q, 6)
            op("v", lambda q, y=y, x=x: q.tensor_reduce(y[0], x[0], AxisListType.X, A.max), y, [x])
        cp(n_(4, 6), R("key", 256, 262))
        ts(mg, R("key", 256, 262), R("thr", t, t + 1), A.is_lt, STAY, A.mult)
        ts(n_(6, 6), n_(4, 6), 2047, A.bitwise_and)
        settle(6, n_(6, 6), mg, "MKg", "GX%d" % t, 1)

    for t in range(RO):
        cut = CUT["later" if t else "first"]
        dates(cut)
        if t:
            guests(t - 1)
        else:
            dma(R("XW", 0, V), hbm("x"), R("W2", 0, V)[1])
        beaten(banks(cut[2])[2][1])
        if t < RO - 1:
            ghosts(t)
        compact()
        choose()
        moves(t)
        refuse(t)
        settle(16, n_(0), mv, "MK", "xB", 0)
        if t < RO - 1:
            parity(t)
            lists("BW", "PL", [("", CUT["later"][0][0][1], 0), ("", V, 1)])
    for b in range(6):
        p = R("ps%d" % (b % 3), rows=(0, 40))
        mm(p, R("OC"), R("BW", 512 * b, 512 * b + 512), True, True)
        act(R("OUT", 512 * b, 512 * b + 512), p)
    guests(RO - 1)
    dma(hbm("yan"), R("OUT", rows=(0, 8)))
    dma(hbm("yof"), R("OUT", rows=(32, 40)))
    dma(hbm("ys"), R("SWIN", 0, W))
    issue()
